import numpy as np
import ml_dtypes


def mxq(x, axis, fmt="e4m3"):
    dtype, down = {"e4m3": (ml_dtypes.float8_e4m3fn, 7), "e5m2": (ml_dtypes.float8_e5m2, 14)}[fmt]
    v = np.moveaxis(np.asarray(x, np.float32).astype(ml_dtypes.bfloat16).astype(np.float64), axis, -1)
    blocks = v.reshape(v.shape[:-1] + (-1, 32))
    amax = np.abs(blocks).max(-1, keepdims=True)
    byte = np.maximum(np.where(amax > 0, np.frexp(amax)[1] - 1 + 127, 0) - down, 1)
    scale = np.exp2(byte - 127.0)
    codes = (blocks / scale).astype(np.float32).astype(dtype).astype(np.float64)
    return np.moveaxis((codes * scale).reshape(v.shape), -1, axis)


WIDE = False


def mx_kscale(k):
    if not WIDE:
        return np.ones(k)
    levels = np.array([10, -10, 5, -5, 0])
    if k % 512:
        return np.exp2(np.random.permutation(np.resize(levels, k // 32))).repeat(32)
    a = np.empty((k // 512, 16))
    for p in range(k // 512):
        a[p, :8] = np.random.permutation(np.resize(levels, 8))
        for g in range(8):
            far = levels[np.abs(levels - a[p, g]) >= 10]
            a[p, g + 8] = far[np.random.randint(len(far))]
    return np.exp2(a.ravel()).repeat(32)


def f64(x):
    return np.asarray(x).astype(np.float64)


def striped(idx):
    return np.tile(idx.reshape(-1, 16).T, (8, 1)).astype(np.uint16)


def unstriped(offs):
    return offs[:16].T.reshape(-1).astype(np.int64)


E2M1 = np.array([0.0, 0.5, 1.0, 1.5, 2.0, 3.0, 4.0, 6.0, -0.0, -0.5, -1.0, -1.5, -2.0, -3.0, -4.0, -6.0])


def pack_weight(w, fmt):
    k, n = w.shape
    w = f64(np.asarray(w, np.float32).astype(ml_dtypes.bfloat16)).reshape(k // 32, 32, n)
    amax = np.abs(w).max(1)
    if fmt == "e4m3":
        byte = np.frexp(amax)[1] - 1 + 127 - 7
    else:
        mant, ex = np.frexp(amax / 6.0)
        byte = np.where(mant > 0.5, ex, ex - 1) + 127
    byte = np.clip(np.where(amax > 0, byte, 1), 1, 254)
    scaled = (w * np.exp2(127.0 - byte)[:, None, :]).reshape(k, n).astype(np.float32)
    by_word = np.ascontiguousarray(scaled.reshape(k // 512, 128, 4, n).transpose(0, 1, 3, 2))
    if fmt == "e4m3":
        words = by_word.astype(ml_dtypes.float8_e4m3fn).view(np.uint8)
    else:
        c = by_word.astype(ml_dtypes.float4_e2m1fn).view(np.uint8) & 0xF
        words = (c[..., 0::2] | (c[..., 1::2] << 4)).reshape(k // 512, 128, 2 * n)
    return np.ascontiguousarray(words), np.ascontiguousarray(byte.astype(np.uint8).reshape(k // 512, 16, n))


def unpack_weight(words, scales, fmt):
    g, _, n = scales.shape
    words = np.ascontiguousarray(words).reshape(g, 128, n, -1)
    if fmt == "e4m3":
        vals = words.view(ml_dtypes.float8_e4m3fn).astype(np.float64)
    else:
        nib = np.empty((g, 128, n, 4), np.uint8)
        nib[..., 0::2] = words & 0xF
        nib[..., 1::2] = words >> 4
        vals = E2M1[nib]
    vals = vals * np.repeat(np.exp2(scales.astype(np.float64) - 127.0), 8, axis=1)[..., None]
    return vals.transpose(0, 1, 3, 2).reshape(g * 512, n)


def gelu(v):
    return 0.5 * v * (1.0 + np.tanh(np.sqrt(2.0 / np.pi) * (v + 0.044715 * v**3)))


K, T, S, M, N = 1024, 2048, 1024, 512, 512

def setup_inputs():
    n = np.random.standard_normal
    s = mx_kscale(K)[:, None]
    u = mx_kscale(S)
    idx = np.random.permutation(T)[:S]
    tab_words, tab_scales = pack_weight(n((K, T)) * s, "e4m3")
    tab2_words, tab2_scales = pack_weight(n((K, T)) * s, "e4m3")
    xt_words, xt_scales = pack_weight(2.0 * n((K, M)) / np.sqrt(K) / s, "e2m1")
    wdT = n((N, T)) / np.sqrt(S)
    wdT[:, idx] /= u
    return {
        "tab_words": tab_words, "tab_scales": tab_scales,
        "tab2_words": tab2_words, "tab2_scales": tab2_scales,
        "xt_words": xt_words, "xt_scales": xt_scales,
        "x": (n((K, M)) / np.sqrt(K) / s).astype(np.float32),
        "g": (np.exp(0.3 * n(S)) * u).astype(np.float32),
        "wdT": wdT.astype(np.float32),
        "offs": striped(idx),
    }

def reference(tab_words, tab_scales, tab2_words, tab2_scales, xt_words, xt_scales, x, g, wdT, offs):
    v = unpack_weight(tab_words, tab_scales, "e4m3")[:, unstriped(offs)]
    v2 = unpack_weight(tab2_words, tab2_scales, "e4m3")[:, unstriped(offs)]
    wd = f64(wdT)[:, unstriped(offs)]
    xt = unpack_weight(xt_words, xt_scales, "e2m1")
    a = v.T @ xt
    b = v2.T @ mxq(f64(x), 0, "e4m3")
    h = 1.0 / (1.0 + np.exp(-a)) * b * f64(g)[:, None]
    y = mxq(wd, 1, "e4m3") @ mxq(h, 0, "e4m3")
    return np.sqrt(np.abs(y))

@@ -1,0 +1,266 @@
+from contextlib import ExitStack
+
+import concourse.mybir as mybir
+from concourse.masks import make_identity
+
+K, T, S, M, N = 1024, 2048, 1024, 512, 512
+FLOPS = 2 * (2 * K * S * M + S * N * M)
+
+F32 = mybir.dt.float32
+BF16 = mybir.dt.bfloat16
+I32 = mybir.dt.int32
+U32 = mybir.dt.uint32
+U16 = mybir.dt.uint16
+U8 = mybir.dt.uint8
+FP8X4 = mybir.dt.float8_e4m3fn_x4
+FP4X4 = mybir.dt.float4_e2m1fn_x4
+ACT = mybir.ActivationFunctionType
+ALU = mybir.AluOpType
+
+P = 128
+KP = K // 512
+JP = S // 512
+NT = N // P
+
+
+def tile_list_cross_modal_shortlist_kernel(
+    tc, tab_words, tab_scales, tab2_words, tab2_scales, xt_words, xt_scales, x, g, wdT, offs, out
+):
+    nc = tc.nc
+    with ExitStack() as ctx:
+        keep = ctx.enter_context(tc.tile_pool(name="keep", bufs=1))
+        big = ctx.enter_context(tc.tile_pool(name="big", bufs=4))
+        ps_a = ctx.enter_context(tc.psum_pool(name="ps_a", bufs=2))
+        ps_b = ctx.enter_context(tc.psum_pool(name="ps_b", bufs=4))
+        ps_t = ctx.enter_context(tc.psum_pool(name="ps_t", bufs=2))
+
+        def sb(name, shape, dtype):
+            return keep.tile(shape, dtype, name=name, align_bytes=64)
+
+        offsets = keep.tile([P, S // 16], U16, name="offsets")
+        nc.sync.dma_start(offsets[:], offs)
+
+        sw1 = sb("sw1", [P, T // 4], I32)
+        sw2 = sb("sw2", [P, T // 4], I32)
+        xts = sb("xts", [P, KP, M // 4], I32)
+        g_rows = sb("g_rows", [P, JP * P], F32)
+        nc.vector.memset(sw1[:], 0)
+        nc.vector.memset(sw2[:], 0)
+        nc.gpsimd.memset(xts[:], 0)
+        nc.gpsimd.memset(g_rows[:], 0.0)
+        ident = sb("ident", [P, P], F32)
+        make_identity(nc, ident[:])
+        s1 = tab_scales.bitcast(I32)
+        s2 = tab2_scales.bitcast(I32)
+
+        def load_words(src, kp):
+            win = big.tile([P, T], I32, name="big", align_bytes=64)
+            nc.sync.dma_start(win[:], src[kp].rearrange("p t i -> p (t i)").bitcast(I32))
+            return win
+
+        def load_x(kp):
+            raw = big.tile([P, 4, M], F32, name="big", align_bytes=64) if kp == 0 else sb("sig00", [P, 4, M], F32)
+            nc.sync.dma_start(raw[:], x[512 * kp : 512 * (kp + 1), :].rearrange("(p i) m -> p i m", i=4))
+            return raw
+
+        def load_wd(nt):
+            win = big.tile([P, T], F32, name="big", align_bytes=64)
+            nc.sync.dma_start(win[:], wdT[P * nt : P * (nt + 1), :])
+            return win
+
+        w1 = [load_words(tab_words, 0)]
+        for q in range(2):
+            nc.sync.dma_start(sw1[32 * q : 32 * q + 8, :], s1[:, 4 * q : 4 * q + 4, :])
+        for q in range(2, 4):
+            nc.sync.dma_start(sw1[32 * q : 32 * q + 4, :], s1[0, 4 * q : 4 * q + 4, :])
+            nc.sync.dma_start(sw1[32 * q - 4 : 32 * q, :], s1[1, 4 * q : 4 * q + 4, :])
+        w1.append(load_words(tab_words, 1))
+        for q in range(4):
+            nc.sync.dma_start(sw2[32 * q : 32 * q + 8, :], s2[:, 4 * q : 4 * q + 4, :])
+        xtw = sb("xtw", [P, KP, M // 2], I32)
+        nc.sync.dma_start(xtw[:], xt_words.bitcast(I32).rearrange("a p c -> p a c"))
+        xs = xt_scales.bitcast(I32)
+        for q in range(4):
+            nc.sync.dma_start(xts[32 * q : 32 * q + 4, :, :], xs[:, 4 * q : 4 * q + 4, :].rearrange("a r c -> r a c"))
+        nc.sync.dma_start(
+            g_rows[0:4, :].rearrange("i (b s) -> i b s", s=8), g.rearrange("(b i s) -> i b s", i=4, s=8)
+        )
+        xraw = [load_x(kp) for kp in range(KP)]
+        w2 = [load_words(tab2_words, kp) for kp in range(KP)]
+        wd = [load_wd(nt) for nt in range(NT)]
+
+        g_bank = ps_t.tile([P, JP, P], F32, name="bank_t")
+        for a in range(JP):
+            nc.tensor.transpose(g_bank[:, a, :], g_rows[:, P * a : P * (a + 1)], ident[:])
+        gains = sb("gains", [P, JP, 4], F32)
+        nc.scalar.copy(gains[:], g_bank[:, :, 0:4])
+
+        def gather_scales(win, name):
+            picked = sb(name + "g", [P, S], U8)
+            nc.vector.tensor_copy(picked[:], win[:].bitcast(U8).indirect(offsets[:]))
+            return picked
+
+        def order_scales(picked, name):
+            plane = sb(name + "p", [P, S], U8)
+            nc.vector.tensor_copy(
+                plane[:].bitcast(I32).rearrange("p (i b h) -> p i b h", i=4, h=2),
+                picked[:].bitcast(I32).rearrange("p (b i h) -> p i b h", i=4, h=2),
+            )
+            return plane
+
+        def gather_words(win, name):
+            picked = sb(name, [P, S], I32)
+            nc.vector.tensor_copy(
+                picked[:].bitcast(U32).rearrange("p (i b s) -> p b i s", i=4, s=8),
+                win[:].bitcast(U32).indirect(offsets[:]),
+            )
+            return picked
+
+        xc, xsc = [], []
+
+        def weave_x(kp):
+            xb = sb("xb%d" % kp, [P, M, 4], BF16)
+            nc.scalar.copy(xb[:], xraw[kp][:].rearrange("p i m -> p m i"))
+            return xb
+
+        def quantize_x(kp, xb):
+            xc.append(sb("xc%d" % kp, [P, M], U32))
+            xsc.append(sb("xsc%d" % kp, [P, M], U8))
+            nc.vector.quantize_mx(out=xc[kp][:].bitcast(FP8X4), scales=xsc[kp][:], in_=xb[:].rearrange("p m i -> p (m i)"))
+
+        v1 = [gather_words(w1[0], "v1_0")]
+        plane1 = order_scales(gather_scales(sw1, "s1"), "s1")
+        plane1b = sb("s1b", [P, S], U8)
+        nc.scalar.dma_start(plane1b[0:64, :].bitcast(I32), plane1[4:68, :].bitcast(I32))
+        nc.scalar.dma_start(plane1b[64:128, :].bitcast(I32), plane1[60:124, :].bitcast(I32))
+        planes1 = [plane1, plane1b]
+        v1.append(gather_words(w1[1], "v1_1"))
+        pick2 = gather_scales(sw2, "s2")
+        xb0 = weave_x(0)
+        xb1 = weave_x(1)
+        quantize_x(0, xb0)
+        plane2 = order_scales(pick2, "s2")
+        v2 = [gather_words(w2[0], "v2_0")]
+        quantize_x(1, xb1)
+        v2.append(gather_words(w2[1], "v2_1"))
+
+        def cols(a, i):
+            return slice(256 * i + P * a, 256 * i + P * (a + 1))
+
+        sig = {}
+        for a in range(JP):
+            for i in range(4):
+                acc = ps_a.tile([P, M], F32, name="acc_a")
+                for kp in range(KP):
+                    nc.tensor.matmul_mx(
+                        out=acc[:],
+                        lhsT=v1[kp][:, cols(a, i)].bitcast(FP8X4),
+                        lhsT_scale=planes1[kp][:, cols(a, i)],
+                        rhs=xtw[:, kp, :].bitcast(U8).bitcast(FP4X4),
+                        rhs_scale=xts[:, kp, :].bitcast(U8),
+                        start=(kp == 0),
+                        stop=(kp == KP - 1),
+                    )
+                sig[a, i] = sb("sig%d%d" % (a, i), [P, M], F32)
+                nc.scalar.activation(sig[a, i][:], acc[:], ACT.Sigmoid)
+
+        def gather_wd(nt, tag):
+            picked = sb(tag, [P, JP, 512], BF16)
+            for a in range(JP):
+                nc.vector.tensor_copy(
+                    picked[:, a, :].rearrange("p (u q s e) -> p q u e s", u=2, s=8, e=2),
+                    wd[nt][:].indirect(offsets[:, 32 * a : 32 * (a + 1)]),
+                )
+            return picked
+
+        def turn_wd(nt, picked, groups):
+            turned = sb("wt%d" % nt, [P, JP, P * 4], BF16)
+            for group in groups:
+                bank = ps_t.tile([P, len(group), 2, P], F32, name="bank_t")
+                for at, a in enumerate(group):
+                    words = picked[:, a, :].bitcast(F32)
+                    for u in range(2):
+                        nc.tensor.transpose(bank[:, at, u, :], words[:, P * u : P * (u + 1)], ident[:])
+                nc.scalar.copy(
+                    turned[:, group[0] : group[-1] + 1, :].bitcast(F32).rearrange("p a (n u) -> p a n u", u=2),
+                    bank[:].rearrange("p a u n -> p a n u"),
+                )
+            return turned
+
+        def quantize_wd(nt, turned, groups):
+            codes = sb("wc%d" % nt, [P, JP * P], U32)
+            scales = sb("ws%d" % nt, [P, JP * P], U8)
+            for group in groups:
+                span = slice(P * group[0], P * (group[-1] + 1))
+                nc.vector.quantize_mx(
+                    out=codes[:, span].bitcast(FP8X4),
+                    scales=scales[:, span],
+                    in_=turned[:, group[0] : group[-1] + 1, :].rearrange("p a c -> p (a c)"),
+                )
+            return codes, scales
+
+        def b_pass(acc, a, i, kp):
+            nc.tensor.matmul_mx(
+                out=acc[:],
+                lhsT=v2[kp][:, cols(a, i)].bitcast(FP8X4),
+                lhsT_scale=plane2[4 * kp : P, cols(a, i)],
+                rhs=xc[kp][:].bitcast(FP8X4),
+                rhs_scale=xsc[kp][:],
+                start=(kp == 0),
+                stop=(kp == KP - 1),
+            )
+
+        def make_h(a, by_pass):
+            flat = sb("hp%d" % a, [P, 4, M], BF16)
+            accs = [ps_b.tile([P, M], F32, name="acc_b") for i in range(4)]
+            if by_pass:
+                for i in range(4):
+                    b_pass(accs[i], a, i, 0)
+            for i in range(4):
+                for kp in range(1 if by_pass else 0, KP):
+                    b_pass(accs[i], a, i, kp)
+                nc.vector.scalar_tensor_tensor(
+                    flat[:, i, :], accs[i][:], gains[:, a, i : i + 1], sig[a, i][:], ALU.mult, ALU.mult
+                )
+            woven = sb("hw%d" % a, [P, M, 4], BF16)
+            nc.scalar.copy(woven[:], flat[:].rearrange("p i m -> p m i"))
+            return woven
+
+        def quantize_h(a, woven):
+            codes = sb("hc%d" % a, [P, M], U32)
+            scales = sb("hs%d" % a, [P, M], U8)
+            nc.vector.quantize_mx(out=codes[:].bitcast(FP8X4), scales=scales[:], in_=woven[:].rearrange("p m i -> p (m i)"))
+            return codes, scales
+
+        def finish(nt, wq, hq):
+            acc = ps_a.tile([P, M], F32, name="acc_a")
+            for a in range(JP):
+                nc.tensor.matmul_mx(
+                    out=acc[:],
+                    lhsT=wq[0][:, P * a : P * (a + 1)].bitcast(FP8X4),
+                    lhsT_scale=wq[1][:, P * a : P * (a + 1)],
+                    rhs=hq[a][0][:].bitcast(FP8X4),
+                    rhs_scale=hq[a][1][:],
+                    start=(a == 0),
+                    stop=(a == JP - 1),
+                )
+            mag = sb("mag%d" % nt, [P, M], F32)
+            nc.scalar.activation(mag[:], acc[:], ACT.Abs)
+            res = sb("res%d" % nt, [P, M], F32)
+            nc.scalar.activation(res[:], mag[:], ACT.Sqrt)
+            nc.sync.dma_start(out[P * nt : P * (nt + 1), :], res[:])
+
+        both, apart = [[0, 1]], [[0], [1]]
+        turned0 = turn_wd(0, gather_wd(0, "wg0"), both)
+        woven0 = make_h(0, True)
+        woven1 = make_h(1, False)
+        wq0 = quantize_wd(0, turned0, both)
+        turned1 = turn_wd(1, gather_wd(1, "sig13"), both)
+        hq = [quantize_h(0, woven0)]
+        turned2 = turn_wd(2, gather_wd(2, "hw0"), both)
+        hq.append(quantize_h(1, woven1))
+        finish(0, wq0, hq)
+        finish(1, quantize_wd(1, turned1, both), hq)
+        turned3 = turn_wd(3, gather_wd(3, "hw1"), apart)
+        finish(2, quantize_wd(2, turned2, both), hq)
+        finish(3, quantize_wd(3, turned3, apart), hq)

@@ -29,9 +29,7 @@ def tile_list_cross_modal_shortlist_kernel(
     nc = tc.nc
     with ExitStack() as ctx:
         keep = ctx.enter_context(tc.tile_pool(name="keep", bufs=1))
-        big = ctx.enter_context(tc.tile_pool(name="big", bufs=4))
-        ps_a = ctx.enter_context(tc.psum_pool(name="ps_a", bufs=2))
-        ps_b = ctx.enter_context(tc.psum_pool(name="ps_b", bufs=4))
+        ps_m = ctx.enter_context(tc.psum_pool(name="ps_m", bufs=1))
         ps_t = ctx.enter_context(tc.psum_pool(name="ps_t", bufs=2))
 
         def sb(name, shape, dtype):
@@ -45,49 +43,51 @@ def tile_list_cross_modal_shortlist_kernel(
         xts = sb("xts", [P, KP, M // 4], I32)
         g_rows = sb("g_rows", [P, JP * P], F32)
         nc.vector.memset(sw1[:], 0)
-        nc.vector.memset(sw2[:], 0)
-        nc.gpsimd.memset(xts[:], 0)
-        nc.gpsimd.memset(g_rows[:], 0.0)
+        nc.gpsimd.memset(sw2[:], 0)
+        nc.vector.memset(xts[:], 0)
+        nc.vector.memset(g_rows[:], 0.0)
         ident = sb("ident", [P, P], F32)
         make_identity(nc, ident[:])
+        warm = sb("warm", [P, 1], F32)
+        nc.scalar.activation(warm[:], ident[:, 0:1], ACT.Sigmoid)
         s1 = tab_scales.bitcast(I32)
         s2 = tab2_scales.bitcast(I32)
 
-        def load_words(src, kp):
-            win = big.tile([P, T], I32, name="big", align_bytes=64)
+        def load_words(src, kp, tag):
+            win = sb(tag, [P, T], I32)
             nc.sync.dma_start(win[:], src[kp].rearrange("p t i -> p (t i)").bitcast(I32))
             return win
 
-        def load_x(kp):
-            raw = big.tile([P, 4, M], F32, name="big", align_bytes=64) if kp == 0 else sb("sig00", [P, 4, M], F32)
-            nc.sync.dma_start(raw[:], x[512 * kp : 512 * (kp + 1), :].rearrange("(p i) m -> p i m", i=4))
+        def load_x(kp, first, width, tag):
+            raw = sb(tag, [P, 4, width], F32)
+            rows = x[512 * kp : 512 * (kp + 1), first : first + width]
+            nc.sync.dma_start(raw[:], rows.rearrange("(p i) m -> p i m", i=4))
             return raw
 
-        def load_wd(nt):
-            win = big.tile([P, T], F32, name="big", align_bytes=64)
+        def load_wd(nt, tag):
+            win = sb(tag, [P, T], F32)
             nc.sync.dma_start(win[:], wdT[P * nt : P * (nt + 1), :])
             return win
 
-        w1 = [load_words(tab_words, 0)]
+        w1 = [load_words(tab_words, 0, "w1_0")]
         for q in range(2):
             nc.sync.dma_start(sw1[32 * q : 32 * q + 8, :], s1[:, 4 * q : 4 * q + 4, :])
         for q in range(2, 4):
             nc.sync.dma_start(sw1[32 * q : 32 * q + 4, :], s1[0, 4 * q : 4 * q + 4, :])
             nc.sync.dma_start(sw1[32 * q - 4 : 32 * q, :], s1[1, 4 * q : 4 * q + 4, :])
-        w1.append(load_words(tab_words, 1))
+        x0 = load_x(0, 0, M, "x0")
+        w1.append(load_words(tab_words, 1, "w1_1"))
         for q in range(4):
             nc.sync.dma_start(sw2[32 * q : 32 * q + 8, :], s2[:, 4 * q : 4 * q + 4, :])
         xtw = sb("xtw", [P, KP, M // 2], I32)
         nc.sync.dma_start(xtw[:], xt_words.bitcast(I32).rearrange("a p c -> p a c"))
-        xs = xt_scales.bitcast(I32)
-        for q in range(4):
-            nc.sync.dma_start(xts[32 * q : 32 * q + 4, :, :], xs[:, 4 * q : 4 * q + 4, :].rearrange("a r c -> r a c"))
         nc.sync.dma_start(
             g_rows[0:4, :].rearrange("i (b s) -> i b s", s=8), g.rearrange("(b i s) -> i b s", i=4, s=8)
         )
-        xraw = [load_x(kp) for kp in range(KP)]
-        w2 = [load_words(tab2_words, kp) for kp in range(KP)]
-        wd = [load_wd(nt) for nt in range(NT)]
+        x1 = load_x(1, 0, M, "x1")
+        xs = xt_scales.bitcast(I32)
+        for q in range(4):
+            nc.sync.dma_start(xts[32 * q : 32 * q + 4, :, :], xs[:, 4 * q : 4 * q + 4, :].rearrange("a r c -> r a c"))
 
         g_bank = ps_t.tile([P, JP, P], F32, name="bank_t")
         for a in range(JP):
@@ -95,18 +95,16 @@ def tile_list_cross_modal_shortlist_kernel(
         gains = sb("gains", [P, JP, 4], F32)
         nc.scalar.copy(gains[:], g_bank[:, :, 0:4])
 
-        def gather_scales(win, name):
-            picked = sb(name + "g", [P, S], U8)
-            nc.vector.tensor_copy(picked[:], win[:].bitcast(U8).indirect(offsets[:]))
+        def gather_scales(win, name, first, last):
+            picked = sb(name, [P, 512 * (last - first)], U8)
+            nc.vector.tensor_copy(picked[:], win[:].bitcast(U8).indirect(offsets[:, 32 * first : 32 * last]))
             return picked
 
-        def order_scales(picked, name):
-            plane = sb(name + "p", [P, S], U8)
+        def order_scales(plane, picked, first, last):
             nc.vector.tensor_copy(
-                plane[:].bitcast(I32).rearrange("p (i b h) -> p i b h", i=4, h=2),
+                plane[:].bitcast(I32).rearrange("p (i b h) -> p i b h", i=4, h=2)[:, :, 16 * first : 16 * last, :],
                 picked[:].bitcast(I32).rearrange("p (b i h) -> p i b h", i=4, h=2),
             )
-            return plane
 
         def gather_words(win, name):
             picked = sb(name, [P, S], I32)
@@ -118,9 +116,12 @@ def tile_list_cross_modal_shortlist_kernel(
 
         xc, xsc = [], []
 
-        def weave_x(kp):
+        def weave_x(kp, raw):
             xb = sb("xb%d" % kp, [P, M, 4], BF16)
-            nc.scalar.copy(xb[:], xraw[kp][:].rearrange("p i m -> p m i"))
+            for c in range(0, M, P):
+                nc.gpsimd.tensor_scalar(
+                    xb[:, c : c + P, :], raw[:, :, c : c + P].rearrange("p i m -> p m i"), 1.0, 0.0, ALU.mult, ALU.add
+                )
             return xb
 
         def quantize_x(kp, xb):
@@ -129,20 +130,38 @@ def tile_list_cross_modal_shortlist_kernel(
             nc.vector.quantize_mx(out=xc[kp][:].bitcast(FP8X4), scales=xsc[kp][:], in_=xb[:].rearrange("p m i -> p (m i)"))
 
         v1 = [gather_words(w1[0], "v1_0")]
-        plane1 = order_scales(gather_scales(sw1, "s1"), "s1")
+        plane1 = sb("s1a", [P, S], U8)
+        pick1 = [gather_scales(sw1, "s1g%d" % a, a, a + 1) for a in range(JP)]
+        for a in range(JP):
+            order_scales(plane1, pick1[a], a, a + 1)
         plane1b = sb("s1b", [P, S], U8)
-        nc.scalar.dma_start(plane1b[0:64, :].bitcast(I32), plane1[4:68, :].bitcast(I32))
-        nc.scalar.dma_start(plane1b[64:128, :].bitcast(I32), plane1[60:124, :].bitcast(I32))
+        nc.sync.dma_start(plane1b[0:64, :].bitcast(I32), plane1[4:68, :].bitcast(I32))
+        nc.sync.dma_start(plane1b[64:128, :].bitcast(I32), plane1[60:124, :].bitcast(I32))
         planes1 = [plane1, plane1b]
+        w2 = [load_words(tab2_words, 0, "s1g1")]
         v1.append(gather_words(w1[1], "v1_1"))
-        pick2 = gather_scales(sw2, "s2")
-        xb0 = weave_x(0)
-        xb1 = weave_x(1)
+        w2.append(load_words(tab2_words, 1, "w1_1"))
+        pick2 = gather_scales(sw2, "s2g", 0, JP)
+        xb0 = weave_x(0, x0)
+        xb1 = weave_x(1, x1)
         quantize_x(0, xb0)
-        plane2 = order_scales(pick2, "s2")
+        plane2 = sb("s2", [P, S], U8)
+        order_scales(plane2, pick2, 0, JP)
+        pair_raw = sb("s2g", [P, 2, T], F32)
+        pair_rows = wdT[0 : 2 * P, :].rearrange("(p e) t -> p e t", e=2)
+        for c in range(2):
+            nc.sync.dma_start(pair_raw[:, :, T // 2 * c : T // 2 * (c + 1)], pair_rows[:, :, T // 2 * c : T // 2 * (c + 1)])
         v2 = [gather_words(w2[0], "v2_0")]
+        wd = {2: load_wd(2, "s1g1")}
         quantize_x(1, xb1)
         v2.append(gather_words(w2[1], "v2_1"))
+        wd[3] = load_wd(3, "w1_1")
+
+        banks = []
+
+        def next_bank():
+            banks.append(ps_m.tile([P, M], F32, name="acc%d" % (len(banks) % 6)))
+            return banks[-1]
 
         def cols(a, i):
             return slice(256 * i + P * a, 256 * i + P * (a + 1))
@@ -150,7 +169,7 @@ def tile_list_cross_modal_shortlist_kernel(
         sig = {}
         for a in range(JP):
             for i in range(4):
-                acc = ps_a.tile([P, M], F32, name="acc_a")
+                acc = next_bank()
                 for kp in range(KP):
                     nc.tensor.matmul_mx(
                         out=acc[:],
@@ -164,28 +183,65 @@ def tile_list_cross_modal_shortlist_kernel(
                 sig[a, i] = sb("sig%d%d" % (a, i), [P, M], F32)
                 nc.scalar.activation(sig[a, i][:], acc[:], ACT.Sigmoid)
 
-        def gather_wd(nt, tag):
-            picked = sb(tag, [P, JP, 512], BF16)
-            for a in range(JP):
+        def gather_wd(nt, tag, groups):
+            picked = sb(tag, [P, 2, JP * 256], BF16)
+            for group in groups:
+                first, last = group[0], group[-1] + 1
                 nc.vector.tensor_copy(
-                    picked[:, a, :].rearrange("p (u q s e) -> p q u e s", u=2, s=8, e=2),
-                    wd[nt][:].indirect(offsets[:, 32 * a : 32 * (a + 1)]),
+                    picked[:, :, 256 * first : 256 * last].rearrange("p u (b s e) -> p b u e s", s=8, e=2),
+                    wd[nt][:].indirect(offsets[:, 32 * first : 32 * last]),
                 )
             return picked
 
-        def turn_wd(nt, picked, groups):
+        def turn_wd(nt, picked, groups, copy):
             turned = sb("wt%d" % nt, [P, JP, P * 4], BF16)
             for group in groups:
                 bank = ps_t.tile([P, len(group), 2, P], F32, name="bank_t")
                 for at, a in enumerate(group):
-                    words = picked[:, a, :].bitcast(F32)
                     for u in range(2):
-                        nc.tensor.transpose(bank[:, at, u, :], words[:, P * u : P * (u + 1)], ident[:])
-                nc.scalar.copy(
+                        words = picked[:, u, 256 * a : 256 * (a + 1)].bitcast(F32)
+                        nc.tensor.transpose(bank[:, at, u, :], words, ident[:])
+                copy(
                     turned[:, group[0] : group[-1] + 1, :].bitcast(F32).rearrange("p a (n u) -> p a n u", u=2),
                     bank[:].rearrange("p a u n -> p a n u"),
                 )
             return turned
+
+        def cast_pair():
+            pairs = sb("pairs", [P, T, 2], BF16)
+            for c in range(2):
+                span = slice(T // 2 * c, T // 2 * (c + 1))
+                nc.scalar.copy(pairs[:, span, :], pair_raw[:, :, span].rearrange("p e t -> p t e"))
+            return pairs
+
+        def gather_pair(pairs, tag):
+            picked = sb(tag, [P, S], F32)
+            nc.vector.tensor_copy(
+                picked[:].bitcast(U32).rearrange("p (i b s) -> p b i s", i=4, s=8),
+                pairs[:].rearrange("p t e -> p (t e)").bitcast(U32).indirect(offsets[:]),
+            )
+            return picked
+
+        def turn_pair(picked):
+            turned = []
+            for a in range(JP):
+                bank = ps_t.tile([P, 4, P], F32, name="bank_t")
+                for i in range(4):
+                    nc.tensor.transpose(bank[:, i, :], picked[:, cols(a, i)], ident[:])
+                turned.append(sb("pt%d" % a, [P, 2 * P, 4], BF16))
+                nc.scalar.copy(turned[a][:], bank[:].bitcast(BF16).rearrange("p i n -> p n i"))
+            return turned
+
+        def quantize_pair(turned):
+            codes = sb("pc", [P, JP, 2 * P], U32)
+            scales = sb("psc", [P, JP, 2 * P], U8)
+            for a in range(JP):
+                nc.vector.quantize_mx(
+                    out=codes[:, a, :].bitcast(FP8X4), scales=scales[:, a, :], in_=turned[a][:].rearrange("p n i -> p (n i)")
+                )
+            return [
+                [(codes[:, a, P * e : P * (e + 1)], scales[:, a, P * e : P * (e + 1)]) for a in range(JP)] for e in range(2)
+            ]
 
         def quantize_wd(nt, turned, groups):
             codes = sb("wc%d" % nt, [P, JP * P], U32)
@@ -197,7 +253,7 @@ def tile_list_cross_modal_shortlist_kernel(
                     scales=scales[:, span],
                     in_=turned[:, group[0] : group[-1] + 1, :].rearrange("p a c -> p (a c)"),
                 )
-            return codes, scales
+            return [(codes[:, P * a : P * (a + 1)], scales[:, P * a : P * (a + 1)]) for a in range(JP)]
 
         def b_pass(acc, a, i, kp):
             nc.tensor.matmul_mx(
@@ -212,7 +268,7 @@ def tile_list_cross_modal_shortlist_kernel(
 
         def make_h(a, by_pass):
             flat = sb("hp%d" % a, [P, 4, M], BF16)
-            accs = [ps_b.tile([P, M], F32, name="acc_b") for i in range(4)]
+            accs = [next_bank() for i in range(4)]
             if by_pass:
                 for i in range(4):
                     b_pass(accs[i], a, i, 0)
@@ -233,12 +289,12 @@ def tile_list_cross_modal_shortlist_kernel(
             return codes, scales
 
         def finish(nt, wq, hq):
-            acc = ps_a.tile([P, M], F32, name="acc_a")
+            acc = next_bank()
             for a in range(JP):
                 nc.tensor.matmul_mx(
                     out=acc[:],
-                    lhsT=wq[0][:, P * a : P * (a + 1)].bitcast(FP8X4),
-                    lhsT_scale=wq[1][:, P * a : P * (a + 1)],
+                    lhsT=wq[a][0].bitcast(FP8X4),
+                    lhsT_scale=wq[a][1],
                     rhs=hq[a][0][:].bitcast(FP8X4),
                     rhs_scale=hq[a][1][:],
                     start=(a == 0),
@@ -251,16 +307,18 @@ def tile_list_cross_modal_shortlist_kernel(
             nc.sync.dma_start(out[P * nt : P * (nt + 1), :], res[:])
 
         both, apart = [[0, 1]], [[0], [1]]
-        turned0 = turn_wd(0, gather_wd(0, "wg0"), both)
+        pairs = cast_pair()
         woven0 = make_h(0, True)
         woven1 = make_h(1, False)
-        wq0 = quantize_wd(0, turned0, both)
-        turned1 = turn_wd(1, gather_wd(1, "sig13"), both)
+        turned01 = turn_pair(gather_pair(pairs, "sig13"))
+        root_warm = sb("root_warm", [P, 1], F32)
+        nc.scalar.activation(root_warm[:], turned01[1][:, 0, 0:1], ACT.Sqrt, scale=0.0)
         hq = [quantize_h(0, woven0)]
-        turned2 = turn_wd(2, gather_wd(2, "hw0"), both)
+        turned2 = turn_wd(2, gather_wd(2, "hw0", both), both, nc.scalar.copy)
         hq.append(quantize_h(1, woven1))
-        finish(0, wq0, hq)
-        finish(1, quantize_wd(1, turned1, both), hq)
-        turned3 = turn_wd(3, gather_wd(3, "hw1"), apart)
+        wq01 = quantize_pair(turned01)
+        finish(0, wq01[0], hq)
+        finish(1, wq01[1], hq)
+        picked3 = gather_wd(3, "hw1", apart)
         finish(2, quantize_wd(2, turned2, both), hq)
-        finish(3, quantize_wd(3, turned3, apart), hq)
+        finish(3, quantize_wd(3, turn_wd(3, picked3, apart, nc.vector.tensor_copy), apart), hq)

@@ -84,7 +84,7 @@ def tile_list_cross_modal_shortlist_kernel(
         nc.sync.dma_start(
             g_rows[0:4, :].rearrange("i (b s) -> i b s", s=8), g.rearrange("(b i s) -> i b s", i=4, s=8)
         )
-        x1 = load_x(1, 0, M, "x1")
+        x1 = load_x(1, 0, M, "sig00")
         xs = xt_scales.bitcast(I32)
         for q in range(4):
             nc.sync.dma_start(xts[32 * q : 32 * q + 4, :, :], xs[:, 4 * q : 4 * q + 4, :].rearrange("a r c -> r a c"))
@@ -116,12 +116,14 @@ def tile_list_cross_modal_shortlist_kernel(
 
         xc, xsc = [], []
 
+        def weave(woven, planes):
+            nc.scalar.copy(
+                woven[:].rearrange("p (c r) i -> p c i r", r=4), planes[:].rearrange("p i (c r) -> p c i r", r=4)
+            )
+
         def weave_x(kp, raw):
             xb = sb("xb%d" % kp, [P, M, 4], BF16)
-            for c in range(0, M, P):
-                nc.gpsimd.tensor_scalar(
-                    xb[:, c : c + P, :], raw[:, :, c : c + P].rearrange("p i m -> p m i"), 1.0, 0.0, ALU.mult, ALU.add
-                )
+            weave(xb, raw)
             return xb
 
         def quantize_x(kp, xb):
@@ -266,7 +268,7 @@ def tile_list_cross_modal_shortlist_kernel(
                 stop=(kp == KP - 1),
             )
 
-        def make_h(a, by_pass):
+        def make_h(a, by_pass, tag):
             flat = sb("hp%d" % a, [P, 4, M], BF16)
             accs = [next_bank() for i in range(4)]
             if by_pass:
@@ -278,47 +280,52 @@ def tile_list_cross_modal_shortlist_kernel(
                 nc.vector.scalar_tensor_tensor(
                     flat[:, i, :], accs[i][:], gains[:, a, i : i + 1], sig[a, i][:], ALU.mult, ALU.mult
                 )
-            woven = sb("hw%d" % a, [P, M, 4], BF16)
-            nc.scalar.copy(woven[:], flat[:].rearrange("p i m -> p m i"))
+            woven = sb(tag, [P, M, 4], BF16)
+            weave(woven, flat)
             return woven
 
-        def quantize_h(a, woven):
-            codes = sb("hc%d" % a, [P, M], U32)
+        def quantize_h(a, woven, tag):
+            codes = sb(tag, [P, M], U32)
             scales = sb("hs%d" % a, [P, M], U8)
             nc.vector.quantize_mx(out=codes[:].bitcast(FP8X4), scales=scales[:], in_=woven[:].rearrange("p m i -> p (m i)"))
             return codes, scales
 
-        def finish(nt, wq, hq):
-            acc = next_bank()
-            for a in range(JP):
-                nc.tensor.matmul_mx(
-                    out=acc[:],
-                    lhsT=wq[a][0].bitcast(FP8X4),
-                    lhsT_scale=wq[a][1],
-                    rhs=hq[a][0][:].bitcast(FP8X4),
-                    rhs_scale=hq[a][1][:],
-                    start=(a == 0),
-                    stop=(a == JP - 1),
-                )
-            mag = sb("mag%d" % nt, [P, M], F32)
-            nc.scalar.activation(mag[:], acc[:], ACT.Abs)
+        def finish(nt, wq, hq, parts, tag):
+            mag = sb(tag, [P, M], F32)
             res = sb("res%d" % nt, [P, M], F32)
-            nc.scalar.activation(res[:], mag[:], ACT.Sqrt)
-            nc.sync.dma_start(out[P * nt : P * (nt + 1), :], res[:])
+            width = M // parts
+            spans = [slice(width * c, width * (c + 1)) for c in range(parts)]
+            accs = [next_bank() for span in spans]
+            for a in range(JP):
+                for acc, span in zip(accs, spans):
+                    nc.tensor.matmul_mx(
+                        out=acc[:, 0:width],
+                        lhsT=wq[a][0].bitcast(FP8X4),
+                        lhsT_scale=wq[a][1],
+                        rhs=hq[a][0][:, span].bitcast(FP8X4),
+                        rhs_scale=hq[a][1][:, span],
+                        start=(a == 0),
+                        stop=(a == JP - 1),
+                    )
+            for acc, span in zip(accs, spans):
+                nc.scalar.activation(mag[:, span], acc[:, 0:width], ACT.Abs)
+                nc.scalar.activation(res[:, span], mag[:, span], ACT.Sqrt)
+                nc.sync.dma_start(out[P * nt : P * (nt + 1), span], res[:, span])
 
         both, apart = [[0, 1]], [[0], [1]]
         pairs = cast_pair()
-        woven0 = make_h(0, True)
-        woven1 = make_h(1, False)
-        turned01 = turn_pair(gather_pair(pairs, "sig13"))
+        woven0 = make_h(0, True, "s2g")
+        woven1 = make_h(1, False, "hw1")
         root_warm = sb("root_warm", [P, 1], F32)
-        nc.scalar.activation(root_warm[:], turned01[1][:, 0, 0:1], ACT.Sqrt, scale=0.0)
-        hq = [quantize_h(0, woven0)]
-        turned2 = turn_wd(2, gather_wd(2, "hw0", both), both, nc.scalar.copy)
-        hq.append(quantize_h(1, woven1))
+        nc.scalar.activation(root_warm[:], woven1[:, 0, 0:1], ACT.Sqrt, scale=0.0)
+        turned01 = turn_pair(gather_pair(pairs, "sig13"))
+        hq = [quantize_h(0, woven0, "pairs")]
+        turned2 = turn_wd(2, gather_wd(2, "s2g", both), both, nc.scalar.copy)
+        hq.append(quantize_h(1, woven1, "hc1"))
         wq01 = quantize_pair(turned01)
-        finish(0, wq01[0], hq)
-        finish(1, wq01[1], hq)
-        picked3 = gather_wd(3, "hw1", apart)
-        finish(2, quantize_wd(2, turned2, both), hq)
-        finish(3, quantize_wd(3, turn_wd(3, picked3, apart, nc.vector.tensor_copy), apart), hq)
+        wq2 = quantize_wd(2, turned2, both)
+        finish(0, wq01[0], hq, 1, "s2g")
+        finish(1, wq01[1], hq, 1, "mag1")
+        finish(2, wq2, hq, 1, "mag2")
+        turned3 = turn_wd(3, gather_wd(3, "wt2", apart), apart, nc.vector.tensor_copy)
+        finish(3, quantize_wd(3, turned3, apart), hq, 2, "mag3")

@@ -41,15 +41,17 @@ def tile_list_cross_modal_shortlist_kernel(
         sw1 = sb("sw1", [P, T // 4], I32)
         sw2 = sb("sw2", [P, T // 4], I32)
         xts = sb("xts", [P, KP, M // 4], I32)
-        g_rows = sb("g_rows", [P, JP * P], F32)
+        g_rows = sb("g_rows", [P, 512], F32)
+        warm = sb("warm", [P, 2], F32)
         nc.vector.memset(sw1[:], 0)
-        nc.gpsimd.memset(sw2[:], 0)
+        nc.vector.memset(warm[:], 0.0)
+        nc.vector.memset(sw2[:], 0)
         nc.vector.memset(xts[:], 0)
-        nc.vector.memset(g_rows[:], 0.0)
+        nc.gpsimd.memset(g_rows[:], 0.0)
+        nc.gpsimd.dma_start(g_rows[0:JP, :], g.rearrange("(a c) -> a c", a=JP))
         ident = sb("ident", [P, P], F32)
         make_identity(nc, ident[:])
-        warm = sb("warm", [P, 1], F32)
-        nc.scalar.activation(warm[:], ident[:, 0:1], ACT.Sigmoid)
+        nc.scalar.activation(warm[:, 1:2], warm[:, 0:1], ACT.Sigmoid)
         s1 = tab_scales.bitcast(I32)
         s2 = tab2_scales.bitcast(I32)
 
@@ -77,23 +79,24 @@ def tile_list_cross_modal_shortlist_kernel(
             nc.sync.dma_start(sw1[32 * q - 4 : 32 * q, :], s1[1, 4 * q : 4 * q + 4, :])
         x0 = load_x(0, 0, M, "x0")
         w1.append(load_words(tab_words, 1, "w1_1"))
-        for q in range(4):
-            nc.sync.dma_start(sw2[32 * q : 32 * q + 8, :], s2[:, 4 * q : 4 * q + 4, :])
         xtw = sb("xtw", [P, KP, M // 2], I32)
         nc.sync.dma_start(xtw[:], xt_words.bitcast(I32).rearrange("a p c -> p a c"))
-        nc.sync.dma_start(
-            g_rows[0:4, :].rearrange("i (b s) -> i b s", s=8), g.rearrange("(b i s) -> i b s", i=4, s=8)
-        )
         x1 = load_x(1, 0, M, "sig00")
+        for q in range(4):
+            nc.gpsimd.dma_start(sw2[32 * q : 32 * q + 8, :], s2[:, 4 * q : 4 * q + 4, :])
         xs = xt_scales.bitcast(I32)
         for q in range(4):
-            nc.sync.dma_start(xts[32 * q : 32 * q + 4, :, :], xs[:, 4 * q : 4 * q + 4, :].rearrange("a r c -> r a c"))
+            nc.gpsimd.dma_start(xts[32 * q : 32 * q + 4, :, :], xs[:, 4 * q : 4 * q + 4, :].rearrange("a r c -> r a c"))
 
-        g_bank = ps_t.tile([P, JP, P], F32, name="bank_t")
-        for a in range(JP):
-            nc.tensor.transpose(g_bank[:, a, :], g_rows[:, P * a : P * (a + 1)], ident[:])
-        gains = sb("gains", [P, JP, 4], F32)
-        nc.scalar.copy(gains[:], g_bank[:, :, 0:4])
+        g_slots = sb("g_slots", [P, 4, P], F32)
+        nc.scalar.copy(
+            g_slots[:].rearrange("p i (q s) -> p i q s", s=8), g_rows[:].rearrange("p (q i s) -> p i q s", i=4, s=8)
+        )
+        g_bank = ps_t.tile([P, 4, P], F32, name="bank_t")
+        for i in range(4):
+            nc.tensor.transpose(g_bank[:, i, :], g_slots[:, i, :], ident[:])
+        gains = sb("gains", [P, 4, JP], F32)
+        nc.scalar.copy(gains[:], g_bank[:, :, 0:JP])
 
         def gather_scales(win, name, first, last):
             picked = sb(name, [P, 512 * (last - first)], U8)
@@ -136,28 +139,28 @@ def tile_list_cross_modal_shortlist_kernel(
         pick1 = [gather_scales(sw1, "s1g%d" % a, a, a + 1) for a in range(JP)]
         for a in range(JP):
             order_scales(plane1, pick1[a], a, a + 1)
+        w2 = [load_words(tab2_words, 0, "s1g0")]
         plane1b = sb("s1b", [P, S], U8)
         nc.sync.dma_start(plane1b[0:64, :].bitcast(I32), plane1[4:68, :].bitcast(I32))
         nc.sync.dma_start(plane1b[64:128, :].bitcast(I32), plane1[60:124, :].bitcast(I32))
         planes1 = [plane1, plane1b]
-        w2 = [load_words(tab2_words, 0, "s1g1")]
+        w2.append(load_words(tab2_words, 1, "s1g1"))
         v1.append(gather_words(w1[1], "v1_1"))
-        w2.append(load_words(tab2_words, 1, "w1_1"))
-        pick2 = gather_scales(sw2, "s2g", 0, JP)
+        pick2 = gather_scales(sw2, "w1_1", 0, JP)
         xb0 = weave_x(0, x0)
         xb1 = weave_x(1, x1)
         quantize_x(0, xb0)
         plane2 = sb("s2", [P, S], U8)
         order_scales(plane2, pick2, 0, JP)
-        pair_raw = sb("s2g", [P, 2, T], F32)
+        pair_raw = sb("sw2", [P, 2, T], F32)
         pair_rows = wdT[0 : 2 * P, :].rearrange("(p e) t -> p e t", e=2)
         for c in range(2):
             nc.sync.dma_start(pair_raw[:, :, T // 2 * c : T // 2 * (c + 1)], pair_rows[:, :, T // 2 * c : T // 2 * (c + 1)])
         v2 = [gather_words(w2[0], "v2_0")]
-        wd = {2: load_wd(2, "s1g1")}
+        wd = {2: load_wd(2, "s1g0")}
         quantize_x(1, xb1)
         v2.append(gather_words(w2[1], "v2_1"))
-        wd[3] = load_wd(3, "w1_1")
+        wd[3] = load_wd(3, "s1g1")
 
         banks = []
 
@@ -278,7 +281,7 @@ def tile_list_cross_modal_shortlist_kernel(
                 for kp in range(1 if by_pass else 0, KP):
                     b_pass(accs[i], a, i, kp)
                 nc.vector.scalar_tensor_tensor(
-                    flat[:, i, :], accs[i][:], gains[:, a, i : i + 1], sig[a, i][:], ALU.mult, ALU.mult
+                    flat[:, i, :], accs[i][:], gains[:, i, a : a + 1], sig[a, i][:], ALU.mult, ALU.mult
                 )
             woven = sb(tag, [P, M, 4], BF16)
             weave(woven, flat)
@@ -314,18 +317,18 @@ def tile_list_cross_modal_shortlist_kernel(
 
         both, apart = [[0, 1]], [[0], [1]]
         pairs = cast_pair()
-        woven0 = make_h(0, True, "s2g")
+        woven0 = make_h(0, True, "sw2")
         woven1 = make_h(1, False, "hw1")
         root_warm = sb("root_warm", [P, 1], F32)
         nc.scalar.activation(root_warm[:], woven1[:, 0, 0:1], ACT.Sqrt, scale=0.0)
         turned01 = turn_pair(gather_pair(pairs, "sig13"))
         hq = [quantize_h(0, woven0, "pairs")]
-        turned2 = turn_wd(2, gather_wd(2, "s2g", both), both, nc.scalar.copy)
+        turned2 = turn_wd(2, gather_wd(2, "sw2", both), both, nc.scalar.copy)
         hq.append(quantize_h(1, woven1, "hc1"))
         wq01 = quantize_pair(turned01)
         wq2 = quantize_wd(2, turned2, both)
-        finish(0, wq01[0], hq, 1, "s2g")
+        finish(0, wq01[0], hq, 1, "sw2")
         finish(1, wq01[1], hq, 1, "mag1")
         finish(2, wq2, hq, 1, "mag2")
-        turned3 = turn_wd(3, gather_wd(3, "wt2", apart), apart, nc.vector.tensor_copy)
+        turned3 = turn_wd(3, gather_wd(3, "pt1", apart), apart, nc.vector.tensor_copy)
         finish(3, quantize_wd(3, turned3, apart), hq, 2, "mag3")

@@ -20,7 +20,9 @@ ALU = mybir.AluOpType
 P = 128
 KP = K // 512
 JP = S // 512
-NT = N // P
+HALF = M // 2
+PIECES = 4
+KIB = 1024
 
 
 def tile_list_cross_modal_shortlist_kernel(
@@ -29,306 +31,246 @@ def tile_list_cross_modal_shortlist_kernel(
     nc = tc.nc
     with ExitStack() as ctx:
         keep = ctx.enter_context(tc.tile_pool(name="keep", bufs=1))
-        ps_m = ctx.enter_context(tc.psum_pool(name="ps_m", bufs=1))
-        ps_t = ctx.enter_context(tc.psum_pool(name="ps_t", bufs=2))
+        stream = ctx.enter_context(tc.tile_pool(name="stream", bufs=1))
+        psum = ctx.enter_context(tc.psum_pool(name="psum", bufs=1))
 
         def sb(name, shape, dtype):
             return keep.tile(shape, dtype, name=name, align_bytes=64)
 
+        def placed(name, shape, dtype, at):
+            return stream.tile(shape, dtype, name=name, align_bytes=64, offset=at)
+
+        banks = []
+
+        def next_bank(shape):
+            banks.append(psum.tile(shape, F32, name="bank%d" % (len(banks) % 8)))
+            return banks[-1]
+
         offsets = keep.tile([P, S // 16], U16, name="offsets")
         nc.sync.dma_start(offsets[:], offs)
 
-        sw1 = sb("sw1", [P, T // 4], I32)
-        sw2 = sb("sw2", [P, T // 4], I32)
-        xts = sb("xts", [P, KP, M // 4], I32)
-        g_rows = sb("g_rows", [P, 512], F32)
-        warm = sb("warm", [P, 2], F32)
-        nc.vector.memset(sw1[:], 0)
-        nc.vector.memset(warm[:], 0.0)
-        nc.vector.memset(sw2[:], 0)
-        nc.vector.memset(xts[:], 0)
-        nc.gpsimd.memset(g_rows[:], 0.0)
-        nc.gpsimd.dma_start(g_rows[0:JP, :], g.rearrange("(a c) -> a c", a=JP))
-        ident = sb("ident", [P, P], F32)
-        make_identity(nc, ident[:])
-        nc.scalar.activation(warm[:, 1:2], warm[:, 0:1], ACT.Sigmoid)
         s1 = tab_scales.bitcast(I32)
         s2 = tab2_scales.bitcast(I32)
+        xs = xt_scales.bitcast(I32)
 
-        def load_words(src, kp, tag):
-            win = sb(tag, [P, T], I32)
+        sw1 = sb("sw1", [P, T // 4], I32)
+        for q in range(4):
+            queue = nc.sync if q < 3 else nc.gpsimd
+            queue.dma_start(sw1[32 * q + 24 : 32 * q + 32, :], s1[:, 4 * q : 4 * q + 4, :])
+        sw2 = placed("sw2", [P, T // 4], I32, 37 * KIB)
+        xts = sb("xts", [P, KP, M // 4], I32)
+        planes1 = sb("planes1", [P, KP, S // 4], I32)
+        g_slots = sb("g_slots", [P, 4, P], F32)
+        warm = placed("warm", [P, 32], F32, 14 * KIB - 64)
+        nc.vector.memset(warm[:], 0.0)
+        nc.vector.memset(xts[:], 0)
+        nc.vector.memset(sw2[:], 0)
+        for q in range(4):
+            nc.vector.memset(sw1[32 * q : 32 * q + 24, :], 0)
+        nc.vector.memset(planes1[:], 0)
+        nc.vector.memset(g_slots[:], 0.0)
+        nc.scalar.activation(warm[:, 1:2], warm[:, 0:1], ACT.Sigmoid)
+
+        def load_words(src, kp, name, at):
+            win = placed(name, [P, T], I32, at)
             nc.sync.dma_start(win[:], src[kp].rearrange("p t i -> p (t i)").bitcast(I32))
             return win
 
-        def load_x(kp, first, width, tag):
-            raw = sb(tag, [P, 4, width], F32)
-            rows = x[512 * kp : 512 * (kp + 1), first : first + width]
+        def load_x(half, kp, at):
+            raw = placed("x%d%d" % (half, kp), [P, 4, HALF], F32, at)
+            rows = x[512 * kp : 512 * (kp + 1), HALF * half : HALF * (half + 1)]
             nc.sync.dma_start(raw[:], rows.rearrange("(p i) m -> p i m", i=4))
             return raw
 
-        def load_wd(nt, tag):
-            win = sb(tag, [P, T], F32)
-            nc.sync.dma_start(win[:], wdT[P * nt : P * (nt + 1), :])
-            return win
+        def load_wd(pair, piece, at):
+            width = T // PIECES
+            raw = placed("wd%d%d" % (pair, piece), [P, 2, width], F32, at)
+            rows = wdT[2 * P * pair : 2 * P * (pair + 1), width * piece : width * (piece + 1)]
+            nc.sync.dma_start(raw[:], rows.rearrange("(p e) t -> p e t", e=2))
+            return raw
 
-        w1 = [load_words(tab_words, 0, "w1_0")]
-        for q in range(2):
-            nc.sync.dma_start(sw1[32 * q : 32 * q + 8, :], s1[:, 4 * q : 4 * q + 4, :])
-        for q in range(2, 4):
-            nc.sync.dma_start(sw1[32 * q : 32 * q + 4, :], s1[0, 4 * q : 4 * q + 4, :])
-            nc.sync.dma_start(sw1[32 * q - 4 : 32 * q, :], s1[1, 4 * q : 4 * q + 4, :])
-        x0 = load_x(0, 0, M, "x0")
-        w1.append(load_words(tab_words, 1, "w1_1"))
-        xtw = sb("xtw", [P, KP, M // 2], I32)
+        w1 = [load_words(tab_words, 0, "w1_0", 2 * KIB), load_words(tab_words, 1, "w1_1", 14 * KIB)]
+        xtw = placed("xtw", [P, KP, M // 2], I32, 12 * KIB)
         nc.sync.dma_start(xtw[:], xt_words.bitcast(I32).rearrange("a p c -> p a c"))
-        x1 = load_x(1, 0, M, "sig00")
+        g_rows = sb("g_rows", [JP, 512], F32)
+        ident = sb("ident", [P, P], F32)
+        make_identity(nc, ident[:])
+        nc.gpsimd.dma_start(g_rows[:], g.rearrange("(a c) -> a c", a=JP))
+        for q in range(4):
+            nc.scalar.dma_start(xts[32 * q : 32 * q + 4, :, :], xs[:, 4 * q : 4 * q + 4, :].rearrange("a r c -> r a c"))
         for q in range(4):
             nc.gpsimd.dma_start(sw2[32 * q : 32 * q + 8, :], s2[:, 4 * q : 4 * q + 4, :])
-        xs = xt_scales.bitcast(I32)
-        for q in range(4):
-            nc.gpsimd.dma_start(xts[32 * q : 32 * q + 4, :, :], xs[:, 4 * q : 4 * q + 4, :].rearrange("a r c -> r a c"))
 
-        g_slots = sb("g_slots", [P, 4, P], F32)
         nc.scalar.copy(
-            g_slots[:].rearrange("p i (q s) -> p i q s", s=8), g_rows[:].rearrange("p (q i s) -> p i q s", i=4, s=8)
+            g_slots[0:JP].rearrange("p i (q s) -> p i q s", s=8), g_rows[:].rearrange("p (q i s) -> p i q s", i=4, s=8)
         )
-        g_bank = ps_t.tile([P, 4, P], F32, name="bank_t")
+        g_bank = next_bank([P, 4, P])
         for i in range(4):
             nc.tensor.transpose(g_bank[:, i, :], g_slots[:, i, :], ident[:])
         gains = sb("gains", [P, 4, JP], F32)
         nc.scalar.copy(gains[:], g_bank[:, :, 0:JP])
 
-        def gather_scales(win, name, first, last):
-            picked = sb(name, [P, 512 * (last - first)], U8)
-            nc.vector.tensor_copy(picked[:], win[:].bitcast(U8).indirect(offsets[:, 32 * first : 32 * last]))
-            return picked
-
-        def order_scales(plane, picked, first, last):
+        def gather_scales(win, picked, plane):
+            nc.vector.tensor_copy(picked[:], win[:].bitcast(U8).indirect(offsets[:]))
             nc.vector.tensor_copy(
-                plane[:].bitcast(I32).rearrange("p (i b h) -> p i b h", i=4, h=2)[:, :, 16 * first : 16 * last, :],
+                plane[:].rearrange("p (i b h) -> p i b h", i=4, h=2),
                 picked[:].bitcast(I32).rearrange("p (b i h) -> p i b h", i=4, h=2),
             )
 
-        def gather_words(win, name):
-            picked = sb(name, [P, S], I32)
-            nc.vector.tensor_copy(
-                picked[:].bitcast(U32).rearrange("p (i b s) -> p b i s", i=4, s=8),
-                win[:].bitcast(U32).indirect(offsets[:]),
-            )
+        def gather_words(words, name, at=None):
+            picked = sb(name, [P, S], U32) if at is None else placed(name, [P, S], U32, at)
+            nc.vector.tensor_copy(picked[:].rearrange("p (i b s) -> p b i s", i=4, s=8), words.indirect(offsets[:]))
             return picked
 
-        xc, xsc = [], []
+        def cast_x(half, raws):
+            woven = sb("xb%d" % half, [P, KP, HALF, 4], BF16)
+            for kp in range(KP):
+                nc.gpsimd.tensor_scalar(
+                    woven[:, kp].rearrange("p (u r) i -> p u i r", r=2),
+                    raws[kp][:].rearrange("p i (u r) -> p u i r", r=2),
+                    1.0,
+                    0.0,
+                    ALU.mult,
+                    ALU.add,
+                )
+            return woven
 
-        def weave(woven, planes):
-            nc.scalar.copy(
-                woven[:].rearrange("p (c r) i -> p c i r", r=4), planes[:].rearrange("p i (c r) -> p c i r", r=4)
-            )
-
-        def weave_x(kp, raw):
-            xb = sb("xb%d" % kp, [P, M, 4], BF16)
-            weave(xb, raw)
-            return xb
-
-        def quantize_x(kp, xb):
-            xc.append(sb("xc%d" % kp, [P, M], U32))
-            xsc.append(sb("xsc%d" % kp, [P, M], U8))
-            nc.vector.quantize_mx(out=xc[kp][:].bitcast(FP8X4), scales=xsc[kp][:], in_=xb[:].rearrange("p m i -> p (m i)"))
-
-        v1 = [gather_words(w1[0], "v1_0")]
-        plane1 = sb("s1a", [P, S], U8)
-        pick1 = [gather_scales(sw1, "s1g%d" % a, a, a + 1) for a in range(JP)]
-        for a in range(JP):
-            order_scales(plane1, pick1[a], a, a + 1)
-        w2 = [load_words(tab2_words, 0, "s1g0")]
-        plane1b = sb("s1b", [P, S], U8)
-        nc.sync.dma_start(plane1b[0:64, :].bitcast(I32), plane1[4:68, :].bitcast(I32))
-        nc.sync.dma_start(plane1b[64:128, :].bitcast(I32), plane1[60:124, :].bitcast(I32))
-        planes1 = [plane1, plane1b]
-        w2.append(load_words(tab2_words, 1, "s1g1"))
-        v1.append(gather_words(w1[1], "v1_1"))
-        pick2 = gather_scales(sw2, "w1_1", 0, JP)
-        xb0 = weave_x(0, x0)
-        xb1 = weave_x(1, x1)
-        quantize_x(0, xb0)
-        plane2 = sb("s2", [P, S], U8)
-        order_scales(plane2, pick2, 0, JP)
-        pair_raw = sb("sw2", [P, 2, T], F32)
-        pair_rows = wdT[0 : 2 * P, :].rearrange("(p e) t -> p e t", e=2)
-        for c in range(2):
-            nc.sync.dma_start(pair_raw[:, :, T // 2 * c : T // 2 * (c + 1)], pair_rows[:, :, T // 2 * c : T // 2 * (c + 1)])
-        v2 = [gather_words(w2[0], "v2_0")]
-        wd = {2: load_wd(2, "s1g0")}
-        quantize_x(1, xb1)
-        v2.append(gather_words(w2[1], "v2_1"))
-        wd[3] = load_wd(3, "s1g1")
-
-        banks = []
-
-        def next_bank():
-            banks.append(ps_m.tile([P, M], F32, name="acc%d" % (len(banks) % 6)))
-            return banks[-1]
+        def quantize(name, woven, passes, width, at=None):
+            shape = [P, passes * width]
+            codes = sb(name + "c", shape, U32) if at is None else placed(name + "c", shape, U32, at)
+            scales = sb(name + "s", [P, passes * width], U8)
+            nc.vector.quantize_mx(out=codes[:].bitcast(FP8X4), scales=scales[:], in_=woven)
+            return codes, scales
 
         def cols(a, i):
             return slice(256 * i + P * a, 256 * i + P * (a + 1))
 
-        sig = {}
+        ordered1 = sb("ordered1", [P, S // 4], I32)
+        gather_scales(sw1, placed("picked1", [P, S], U8, 29 * KIB + 512), ordered1)
+        for kp in range(KP):
+            nc.scalar.dma_start(planes1[0:100, kp, :], ordered1[24 + 4 * kp : 124 + 4 * kp, :])
+        x_raw = [[load_x(0, kp, (26 + 4 * kp) * KIB) for kp in range(KP)]]
+        v1 = [gather_words(w1[0][:].bitcast(U32), "v1_0")]
+        w2 = [load_words(tab2_words, 0, "w2_0", 2 * KIB)]
+        v1.append(gather_words(w1[1][:].bitcast(U32), "v1_1"))
+        w2.append(load_words(tab2_words, 1, "w2_1", 18 * KIB))
+        wd_raw = [[load_wd(0, 0, 14 * KIB)]]
+        plane2 = sb("plane2", [P, S // 4], I32)
+        gather_scales(sw2, placed("picked2", [P, S], U8, 42 * KIB), plane2)
+        wd_raw[0].extend([load_wd(0, c, (30 + 4 * c) * KIB) for c in range(1, 3)])
+        x_woven = cast_x(0, x_raw[0])
+        xq = [quantize("x0", x_woven[:].rearrange("p a m i -> p (a m i)"), KP, HALF)]
+        v2 = [gather_words(w2[0][:].bitcast(U32), "v2_0", 42 * KIB)]
+        wd_raw[0].append(load_wd(0, 3, 0))
+        wd_raw.append([load_wd(1, c, (4 + 4 * c) * KIB) for c in range(2)])
+        v2.append(gather_words(w2[1][:].bitcast(U32), "v2_1"))
+        wd_raw[1].extend([load_wd(1, c, (10 + 4 * c) * KIB) for c in range(2, 4)])
+
+        gated = [sb("gated%d" % a, [P, 4, M], F32) for a in range(JP)]
         for a in range(JP):
             for i in range(4):
-                acc = next_bank()
+                acc = next_bank([P, M])
                 for kp in range(KP):
                     nc.tensor.matmul_mx(
                         out=acc[:],
                         lhsT=v1[kp][:, cols(a, i)].bitcast(FP8X4),
-                        lhsT_scale=planes1[kp][:, cols(a, i)],
+                        lhsT_scale=planes1[:, kp, :].bitcast(U8)[:, cols(a, i)],
                         rhs=xtw[:, kp, :].bitcast(U8).bitcast(FP4X4),
                         rhs_scale=xts[:, kp, :].bitcast(U8),
                         start=(kp == 0),
                         stop=(kp == KP - 1),
                     )
-                sig[a, i] = sb("sig%d%d" % (a, i), [P, M], F32)
-                nc.scalar.activation(sig[a, i][:], acc[:], ACT.Sigmoid)
+                sig = sb("sig%d%d" % (a, i), [P, M], F32)
+                nc.scalar.activation(sig[:], acc[:], ACT.Sigmoid)
+                nc.gpsimd.tensor_scalar(gated[a][:, i, :], sig[:], gains[:, i, a : a + 1], 0.0, ALU.mult, ALU.add)
 
-        def gather_wd(nt, tag, groups):
-            picked = sb(tag, [P, 2, JP * 256], BF16)
-            for group in groups:
-                first, last = group[0], group[-1] + 1
-                nc.vector.tensor_copy(
-                    picked[:, :, 256 * first : 256 * last].rearrange("p u (b s e) -> p b u e s", s=8, e=2),
-                    wd[nt][:].indirect(offsets[:, 32 * first : 32 * last]),
-                )
-            return picked
-
-        def turn_wd(nt, picked, groups, copy):
-            turned = sb("wt%d" % nt, [P, JP, P * 4], BF16)
-            for group in groups:
-                bank = ps_t.tile([P, len(group), 2, P], F32, name="bank_t")
-                for at, a in enumerate(group):
-                    for u in range(2):
-                        words = picked[:, u, 256 * a : 256 * (a + 1)].bitcast(F32)
-                        nc.tensor.transpose(bank[:, at, u, :], words, ident[:])
-                copy(
-                    turned[:, group[0] : group[-1] + 1, :].bitcast(F32).rearrange("p a (n u) -> p a n u", u=2),
-                    bank[:].rearrange("p a u n -> p a n u"),
-                )
-            return turned
-
-        def cast_pair():
-            pairs = sb("pairs", [P, T, 2], BF16)
-            for c in range(2):
-                span = slice(T // 2 * c, T // 2 * (c + 1))
-                nc.scalar.copy(pairs[:, span, :], pair_raw[:, :, span].rearrange("p e t -> p t e"))
+        def cast_pair(pair):
+            pairs = sb("pairs%d" % pair, [P, T, 2], BF16)
+            width = T // PIECES
+            for c in range(PIECES):
+                nc.scalar.copy(pairs[:, width * c : width * (c + 1), :], wd_raw[pair][c][:].rearrange("p e t -> p t e"))
             return pairs
 
-        def gather_pair(pairs, tag):
-            picked = sb(tag, [P, S], F32)
-            nc.vector.tensor_copy(
-                picked[:].bitcast(U32).rearrange("p (i b s) -> p b i s", i=4, s=8),
-                pairs[:].rearrange("p t e -> p (t e)").bitcast(U32).indirect(offsets[:]),
-            )
-            return picked
-
-        def turn_pair(picked):
-            turned = []
+        def turn_pair(picked, turned):
             for a in range(JP):
-                bank = ps_t.tile([P, 4, P], F32, name="bank_t")
+                bank = next_bank([P, 4, P])
                 for i in range(4):
-                    nc.tensor.transpose(bank[:, i, :], picked[:, cols(a, i)], ident[:])
-                turned.append(sb("pt%d" % a, [P, 2 * P, 4], BF16))
-                nc.scalar.copy(turned[a][:], bank[:].bitcast(BF16).rearrange("p i n -> p n i"))
-            return turned
+                    nc.tensor.transpose(bank[:, i, :], picked[:, cols(a, i)].bitcast(F32), ident[:])
+                nc.scalar.copy(turned[:, a], bank[:].bitcast(BF16).rearrange("p i n -> p n i"))
 
-        def quantize_pair(turned):
-            codes = sb("pc", [P, JP, 2 * P], U32)
-            scales = sb("psc", [P, JP, 2 * P], U8)
-            for a in range(JP):
-                nc.vector.quantize_mx(
-                    out=codes[:, a, :].bitcast(FP8X4), scales=scales[:, a, :], in_=turned[a][:].rearrange("p n i -> p (n i)")
-                )
-            return [
-                [(codes[:, a, P * e : P * (e + 1)], scales[:, a, P * e : P * (e + 1)]) for a in range(JP)] for e in range(2)
-            ]
+        def make_h(first, width, at=None):
+            half = first // HALF
+            codes, scales = xq[half]
+            shape = [P, JP, width, 4]
+            woven = sb("h%d" % first, shape, BF16) if at is None else placed("h%d" % first, shape, BF16, at)
+            for c in range(width // P):
+                col = first + P * c
+                for a in range(JP):
+                    bank = next_bank([P, 4, P])
+                    for i in range(4):
+                        for kp in range(KP):
+                            span = slice(HALF * kp + col % HALF, HALF * kp + col % HALF + P)
+                            nc.tensor.matmul_mx(
+                                out=bank[:, i, :],
+                                lhsT=v2[kp][:, cols(a, i)].bitcast(FP8X4),
+                                lhsT_scale=plane2[4 * kp : P, :].bitcast(U8)[:, cols(a, i)],
+                                rhs=codes[:, span].bitcast(FP8X4),
+                                rhs_scale=scales[:, span],
+                                start=(kp == 0),
+                                stop=(kp == KP - 1),
+                            )
+                    nc.vector.tensor_tensor(
+                        woven[:, a, P * c : P * (c + 1), :].rearrange("p (u r) i -> p u i r", r=2),
+                        bank[:].rearrange("p i (u r) -> p u i r", r=2),
+                        gated[a][:, :, col : col + P].rearrange("p i (u r) -> p u i r", r=2),
+                        ALU.mult,
+                    )
+            return quantize("h%d" % first, woven[:].rearrange("p a m i -> p (a m i)"), JP, width)
 
-        def quantize_wd(nt, turned, groups):
-            codes = sb("wc%d" % nt, [P, JP * P], U32)
-            scales = sb("ws%d" % nt, [P, JP * P], U8)
-            for group in groups:
-                span = slice(P * group[0], P * (group[-1] + 1))
-                nc.vector.quantize_mx(
-                    out=codes[:, span].bitcast(FP8X4),
-                    scales=scales[:, span],
-                    in_=turned[:, group[0] : group[-1] + 1, :].rearrange("p a c -> p (a c)"),
-                )
-            return [(codes[:, P * a : P * (a + 1)], scales[:, P * a : P * (a + 1)]) for a in range(JP)]
+        out_rows = out.rearrange("(t p) m -> p t m", p=P)
 
-        def b_pass(acc, a, i, kp):
-            nc.tensor.matmul_mx(
-                out=acc[:],
-                lhsT=v2[kp][:, cols(a, i)].bitcast(FP8X4),
-                lhsT_scale=plane2[4 * kp : P, cols(a, i)],
-                rhs=xc[kp][:].bitcast(FP8X4),
-                rhs_scale=xsc[kp][:],
-                start=(kp == 0),
-                stop=(kp == KP - 1),
-            )
-
-        def make_h(a, by_pass, tag):
-            flat = sb("hp%d" % a, [P, 4, M], BF16)
-            accs = [next_bank() for i in range(4)]
-            if by_pass:
-                for i in range(4):
-                    b_pass(accs[i], a, i, 0)
-            for i in range(4):
-                for kp in range(1 if by_pass else 0, KP):
-                    b_pass(accs[i], a, i, kp)
-                nc.vector.scalar_tensor_tensor(
-                    flat[:, i, :], accs[i][:], gains[:, i, a : a + 1], sig[a, i][:], ALU.mult, ALU.mult
-                )
-            woven = sb(tag, [P, M, 4], BF16)
-            weave(woven, flat)
-            return woven
-
-        def quantize_h(a, woven, tag):
-            codes = sb(tag, [P, M], U32)
-            scales = sb("hs%d" % a, [P, M], U8)
-            nc.vector.quantize_mx(out=codes[:].bitcast(FP8X4), scales=scales[:], in_=woven[:].rearrange("p m i -> p (m i)"))
-            return codes, scales
-
-        def finish(nt, wq, hq, parts, tag):
-            mag = sb(tag, [P, M], F32)
-            res = sb("res%d" % nt, [P, M], F32)
-            width = M // parts
-            spans = [slice(width * c, width * (c + 1)) for c in range(parts)]
-            accs = [next_bank() for span in spans]
-            for a in range(JP):
-                for acc, span in zip(accs, spans):
+        def finish(tiles, hq, first, width):
+            bank = next_bank([P, len(tiles), width])
+            for at, nt in enumerate(tiles):
+                codes, scales = wq[nt // 2]
+                for a in range(JP):
+                    rows = slice(2 * P * a + P * (nt % 2), 2 * P * a + P * (nt % 2 + 1))
+                    span = slice(width * a, width * (a + 1))
                     nc.tensor.matmul_mx(
-                        out=acc[:, 0:width],
-                        lhsT=wq[a][0].bitcast(FP8X4),
-                        lhsT_scale=wq[a][1],
-                        rhs=hq[a][0][:, span].bitcast(FP8X4),
-                        rhs_scale=hq[a][1][:, span],
+                        out=bank[:, at, :],
+                        lhsT=codes[:, rows].bitcast(FP8X4),
+                        lhsT_scale=scales[:, rows],
+                        rhs=hq[0][:, span].bitcast(FP8X4),
+                        rhs_scale=hq[1][:, span],
                         start=(a == 0),
                         stop=(a == JP - 1),
                     )
-            for acc, span in zip(accs, spans):
-                nc.scalar.activation(mag[:, span], acc[:, 0:width], ACT.Abs)
-                nc.scalar.activation(res[:, span], mag[:, span], ACT.Sqrt)
-                nc.sync.dma_start(out[P * nt : P * (nt + 1), span], res[:, span])
+            name = "%d_%d" % (tiles[0], first)
+            mag = sb("mag" + name, [P, len(tiles), width], F32)
+            res = sb("res" + name, [P, len(tiles), width], F32)
+            nc.scalar.activation(mag[:], bank[:], ACT.Abs)
+            nc.scalar.activation(res[:], mag[:], ACT.Sqrt)
+            nc.sync.dma_start(out_rows[:, tiles[0] : tiles[-1] + 1, first : first + width], res[:])
 
-        both, apart = [[0, 1]], [[0], [1]]
-        pairs = cast_pair()
-        woven0 = make_h(0, True, "sw2")
-        woven1 = make_h(1, False, "hw1")
+        pairs0 = cast_pair(0)
+        x_raw.append([load_x(1, kp, (34 + 4 * kp) * KIB) for kp in range(KP)])
+        h_first = make_h(0, HALF)
+        picked0 = gather_words(pairs0[:].rearrange("p t e -> p (t e)").bitcast(U32), "wp0")
+        pairs1 = cast_pair(1)
+        picked1 = gather_words(pairs1[:].rearrange("p t e -> p (t e)").bitcast(U32), "wp1")
+        turned0 = placed("turned0", [P, JP, 2 * P, 4], BF16, 22 * KIB)
+        turn_pair(picked0, turned0)
         root_warm = sb("root_warm", [P, 1], F32)
-        nc.scalar.activation(root_warm[:], woven1[:, 0, 0:1], ACT.Sqrt, scale=0.0)
-        turned01 = turn_pair(gather_pair(pairs, "sig13"))
-        hq = [quantize_h(0, woven0, "pairs")]
-        turned2 = turn_wd(2, gather_wd(2, "sw2", both), both, nc.scalar.copy)
-        hq.append(quantize_h(1, woven1, "hc1"))
-        wq01 = quantize_pair(turned01)
-        wq2 = quantize_wd(2, turned2, both)
-        finish(0, wq01[0], hq, 1, "sw2")
-        finish(1, wq01[1], hq, 1, "mag1")
-        finish(2, wq2, hq, 1, "mag2")
-        turned3 = turn_wd(3, gather_wd(3, "pt1", apart), apart, nc.vector.tensor_copy)
-        finish(3, quantize_wd(3, turned3, apart), hq, 2, "mag3")
+        nc.scalar.activation(root_warm[:], turned0[:, 1, 0, 0:1], ACT.Sqrt, scale=0.0)
+        wq = [quantize("w0", turned0[:].rearrange("p a n i -> p (a n i)"), JP, 2 * P)]
+        x_woven = cast_x(1, x_raw[1])
+        xq.append(quantize("x1", x_woven[:].rearrange("p a m i -> p (a m i)"), KP, HALF))
+        turned1 = sb("turned1", [P, JP, 2 * P, 4], BF16)
+        turn_pair(picked1, turned1)
+        finish([0, 1], h_first, 0, HALF)
+        h_third = make_h(HALF, P, 46 * KIB)
+        wq.append(quantize("w1", turned1[:].rearrange("p a n i -> p (a n i)"), JP, 2 * P, 46 * KIB))
+        h_fourth = make_h(HALF + P, P)
+        finish([2, 3], h_first, 0, HALF)
+        finish([0, 1, 2, 3], h_third, HALF, P)
+        finish([0, 1, 2, 3], h_fourth, HALF + P, P)

@@ -40,6 +40,9 @@ def tile_list_cross_modal_shortlist_kernel(
         def placed(name, shape, dtype, at):
             return stream.tile(shape, dtype, name=name, align_bytes=64, offset=at)
 
+        def tile(name, shape, dtype, at):
+            return sb(name, shape, dtype) if at is None else placed(name, shape, dtype, at)
+
         banks = []
 
         def next_bank(shape):
@@ -57,7 +60,7 @@ def tile_list_cross_modal_shortlist_kernel(
         for q in range(4):
             queue = nc.sync if q < 3 else nc.gpsimd
             queue.dma_start(sw1[32 * q + 24 : 32 * q + 32, :], s1[:, 4 * q : 4 * q + 4, :])
-        sw2 = placed("sw2", [P, T // 4], I32, 37 * KIB)
+        sw2 = sb("sw2", [P, T // 4], I32)
         xts = sb("xts", [P, KP, M // 4], I32)
         planes1 = sb("planes1", [P, KP, S // 4], I32)
         g_slots = sb("g_slots", [P, 4, P], F32)
@@ -71,25 +74,25 @@ def tile_list_cross_modal_shortlist_kernel(
         nc.vector.memset(g_slots[:], 0.0)
         nc.scalar.activation(warm[:, 1:2], warm[:, 0:1], ACT.Sigmoid)
 
-        def load_words(src, kp, name, at):
-            win = placed(name, [P, T], I32, at)
+        def load_words(src, kp, name, at=None):
+            win = tile(name, [P, T], I32, at)
             nc.sync.dma_start(win[:], src[kp].rearrange("p t i -> p (t i)").bitcast(I32))
             return win
 
-        def load_x(half, kp, at):
-            raw = placed("x%d%d" % (half, kp), [P, 4, HALF], F32, at)
+        def load_x(half, kp, at=None):
+            raw = tile("x%d%d" % (half, kp), [P, 4, HALF], F32, at)
             rows = x[512 * kp : 512 * (kp + 1), HALF * half : HALF * (half + 1)]
             nc.sync.dma_start(raw[:], rows.rearrange("(p i) m -> p i m", i=4))
             return raw
 
-        def load_wd(pair, piece, at):
+        def load_wd(pair, piece, at=None):
             width = T // PIECES
-            raw = placed("wd%d%d" % (pair, piece), [P, 2, width], F32, at)
+            raw = tile("wd%d%d" % (pair, piece), [P, 2, width], F32, at)
             rows = wdT[2 * P * pair : 2 * P * (pair + 1), width * piece : width * (piece + 1)]
             nc.sync.dma_start(raw[:], rows.rearrange("(p e) t -> p e t", e=2))
             return raw
 
-        w1 = [load_words(tab_words, 0, "w1_0", 2 * KIB), load_words(tab_words, 1, "w1_1", 14 * KIB)]
+        w1 = [load_words(tab_words, 0, "w1_0"), load_words(tab_words, 1, "w1_1", 14 * KIB)]
         xtw = placed("xtw", [P, KP, M // 2], I32, 12 * KIB)
         nc.sync.dma_start(xtw[:], xt_words.bitcast(I32).rearrange("a p c -> p a c"))
         g_rows = sb("g_rows", [JP, 512], F32)
@@ -117,23 +120,22 @@ def tile_list_cross_modal_shortlist_kernel(
                 picked[:].bitcast(I32).rearrange("p (b i h) -> p i b h", i=4, h=2),
             )
 
-        def gather_words(words, name, at=None):
-            picked = sb(name, [P, S], U32) if at is None else placed(name, [P, S], U32, at)
-            nc.vector.tensor_copy(picked[:].rearrange("p (i b s) -> p b i s", i=4, s=8), words.indirect(offsets[:]))
+        def gather_words(words, name, parts):
+            picked = sb(name, [P, S], U32)
+            blocks = picked[:].rearrange("p (i b s) -> p b i s", i=4, s=8)
+            for part in range(parts):
+                first, last = 32 * part // parts, 32 * (part + 1) // parts
+                nc.vector.tensor_copy(blocks[:, first:last], words.indirect(offsets[:, 2 * first : 2 * last]))
             return picked
 
-        def cast_x(half, raws):
-            woven = sb("xb%d" % half, [P, KP, HALF, 4], BF16)
+        def cast_x(half, raws, parts):
+            width = HALF // parts
+            woven = sb("xb%d" % half, [P, parts, KP, width, 4], BF16)
             for kp in range(KP):
-                nc.gpsimd.tensor_scalar(
-                    woven[:, kp].rearrange("p (u r) i -> p u i r", r=2),
-                    raws[kp][:].rearrange("p i (u r) -> p u i r", r=2),
-                    1.0,
-                    0.0,
-                    ALU.mult,
-                    ALU.add,
-                )
-            return woven
+                for part in range(parts):
+                    rows = raws[kp][:, :, width * part : width * (part + 1)]
+                    nc.gpsimd.tensor_scalar(woven[:, part, kp], rows.rearrange("p i m -> p m i"), 1.0, 0.0, ALU.mult, ALU.add)
+            return [woven[:, part].rearrange("p a m i -> p (a m i)") for part in range(parts)]
 
         def quantize(name, woven, passes, width, at=None):
             shape = [P, passes * width]
@@ -150,21 +152,19 @@ def tile_list_cross_modal_shortlist_kernel(
         for kp in range(KP):
             nc.scalar.dma_start(planes1[0:100, kp, :], ordered1[24 + 4 * kp : 124 + 4 * kp, :])
         x_raw = [[load_x(0, kp, (26 + 4 * kp) * KIB) for kp in range(KP)]]
-        v1 = [gather_words(w1[0][:].bitcast(U32), "v1_0")]
-        w2 = [load_words(tab2_words, 0, "w2_0", 2 * KIB)]
-        v1.append(gather_words(w1[1][:].bitcast(U32), "v1_1"))
-        w2.append(load_words(tab2_words, 1, "w2_1", 18 * KIB))
-        wd_raw = [[load_wd(0, 0, 14 * KIB)]]
+        v1 = [gather_words(w1[0][:].bitcast(U32), "v1_0", 1)]
+        w2 = [load_words(tab2_words, 0, "w2_0", 34 * KIB)]
+        v1.append(gather_words(w1[1][:].bitcast(U32), "v1_1", JP))
+        w2.append(load_words(tab2_words, 1, "w2_1"))
+        wd_raw = [[load_wd(0, c) for c in range(PIECES)], [load_wd(1, c) for c in range(PIECES - 1)]]
+        wd_raw[1].append(load_wd(1, PIECES - 1, 22 * KIB))
+        x_raw.append([load_x(1, kp) for kp in range(KP)])
         plane2 = sb("plane2", [P, S // 4], I32)
-        gather_scales(sw2, placed("picked2", [P, S], U8, 42 * KIB), plane2)
-        wd_raw[0].extend([load_wd(0, c, (30 + 4 * c) * KIB) for c in range(1, 3)])
-        x_woven = cast_x(0, x_raw[0])
-        xq = [quantize("x0", x_woven[:].rearrange("p a m i -> p (a m i)"), KP, HALF)]
-        v2 = [gather_words(w2[0][:].bitcast(U32), "v2_0", 42 * KIB)]
-        wd_raw[0].append(load_wd(0, 3, 0))
-        wd_raw.append([load_wd(1, c, (4 + 4 * c) * KIB) for c in range(2)])
-        v2.append(gather_words(w2[1][:].bitcast(U32), "v2_1"))
-        wd_raw[1].extend([load_wd(1, c, (10 + 4 * c) * KIB) for c in range(2, 4)])
+        gather_scales(sw2, placed("picked2", [P, S], U8, 14 * KIB), plane2)
+        x_woven = cast_x(0, x_raw[0], 1)
+        v2 = [gather_words(w2[0][:].bitcast(U32), "v2_0", 1)]
+        x_first = quantize("x0", x_woven[0], KP, HALF, 34 * KIB)
+        v2.append(gather_words(w2[1][:].bitcast(U32), "v2_1", JP))
 
         gated = [sb("gated%d" % a, [P, 4, M], F32) for a in range(JP)]
         for a in range(JP):
@@ -184,6 +184,9 @@ def tile_list_cross_modal_shortlist_kernel(
                 nc.scalar.activation(sig[:], acc[:], ACT.Sigmoid)
                 nc.gpsimd.tensor_scalar(gated[a][:, i, :], sig[:], gains[:, i, a : a + 1], 0.0, ALU.mult, ALU.add)
 
+        root_warm = sb("root_warm", [P, 1], F32)
+        nc.scalar.activation(root_warm[:], sig[:, 0:1], ACT.Sqrt)
+
         def cast_pair(pair):
             pairs = sb("pairs%d" % pair, [P, T, 2], BF16)
             width = T // PIECES
@@ -198,18 +201,16 @@ def tile_list_cross_modal_shortlist_kernel(
                     nc.tensor.transpose(bank[:, i, :], picked[:, cols(a, i)].bitcast(F32), ident[:])
                 nc.scalar.copy(turned[:, a], bank[:].bitcast(BF16).rearrange("p i n -> p n i"))
 
-        def make_h(first, width, at=None):
-            half = first // HALF
-            codes, scales = xq[half]
-            shape = [P, JP, width, 4]
-            woven = sb("h%d" % first, shape, BF16) if at is None else placed("h%d" % first, shape, BF16, at)
-            for c in range(width // P):
-                col = first + P * c
-                for a in range(JP):
+        def make_h(xq, first, width):
+            codes, scales = xq
+            woven = sb("h%d" % first, [P, JP, width, 4], BF16)
+            for a in range(JP):
+                for c in range(width // P):
+                    col = first + P * c
                     bank = next_bank([P, 4, P])
                     for i in range(4):
                         for kp in range(KP):
-                            span = slice(HALF * kp + col % HALF, HALF * kp + col % HALF + P)
+                            span = slice(width * kp + P * c, width * kp + P * (c + 1))
                             nc.tensor.matmul_mx(
                                 out=bank[:, i, :],
                                 lhsT=v2[kp][:, cols(a, i)].bitcast(FP8X4),
@@ -253,24 +254,22 @@ def tile_list_cross_modal_shortlist_kernel(
             nc.sync.dma_start(out_rows[:, tiles[0] : tiles[-1] + 1, first : first + width], res[:])
 
         pairs0 = cast_pair(0)
-        x_raw.append([load_x(1, kp, (34 + 4 * kp) * KIB) for kp in range(KP)])
-        h_first = make_h(0, HALF)
-        picked0 = gather_words(pairs0[:].rearrange("p t e -> p (t e)").bitcast(U32), "wp0")
+        h_first = make_h(x_first, 0, HALF)
+        picked0 = gather_words(pairs0[:].rearrange("p t e -> p (t e)").bitcast(U32), "wp0", JP)
         pairs1 = cast_pair(1)
-        picked1 = gather_words(pairs1[:].rearrange("p t e -> p (t e)").bitcast(U32), "wp1")
+        picked1 = gather_words(pairs1[:].rearrange("p t e -> p (t e)").bitcast(U32), "wp1", JP)
         turned0 = placed("turned0", [P, JP, 2 * P, 4], BF16, 22 * KIB)
         turn_pair(picked0, turned0)
-        root_warm = sb("root_warm", [P, 1], F32)
-        nc.scalar.activation(root_warm[:], turned0[:, 1, 0, 0:1], ACT.Sqrt, scale=0.0)
+        x_woven = cast_x(1, x_raw[1], 2)
+        x_third = quantize("x2", x_woven[0], KP, P)
         wq = [quantize("w0", turned0[:].rearrange("p a n i -> p (a n i)"), JP, 2 * P)]
-        x_woven = cast_x(1, x_raw[1])
-        xq.append(quantize("x1", x_woven[:].rearrange("p a m i -> p (a m i)"), KP, HALF))
+        x_fourth = quantize("x3", x_woven[1], KP, P)
         turned1 = sb("turned1", [P, JP, 2 * P, 4], BF16)
         turn_pair(picked1, turned1)
         finish([0, 1], h_first, 0, HALF)
-        h_third = make_h(HALF, P, 46 * KIB)
-        wq.append(quantize("w1", turned1[:].rearrange("p a n i -> p (a n i)"), JP, 2 * P, 46 * KIB))
-        h_fourth = make_h(HALF + P, P)
+        h_third = make_h(x_third, HALF, P)
+        wq.append(quantize("w1", turned1[:].rearrange("p a n i -> p (a n i)"), JP, 2 * P))
+        h_fourth = make_h(x_fourth, HALF + P, P)
         finish([2, 3], h_first, 0, HALF)
         finish([0, 1, 2, 3], h_third, HALF, P)
         finish([0, 1, 2, 3], h_fourth, HALF + P, P)

@@ -57,20 +57,18 @@ def tile_list_cross_modal_shortlist_kernel(
         xs = xt_scales.bitcast(I32)
 
         sw1 = sb("sw1", [P, T // 4], I32)
+        nc.vector.memset(sw1[:], 0)
         for q in range(4):
-            queue = nc.sync if q < 3 else nc.gpsimd
-            queue.dma_start(sw1[32 * q + 24 : 32 * q + 32, :], s1[:, 4 * q : 4 * q + 4, :])
+            nc.sync.dma_start(sw1[32 * q : 32 * q + 8, :], s1[:, 4 * q : 4 * q + 4, :])
         sw2 = sb("sw2", [P, T // 4], I32)
         xts = sb("xts", [P, KP, M // 4], I32)
-        planes1 = sb("planes1", [P, KP, S // 4], I32)
+        shifted1 = sb("shifted1", [P, S // 4], I32)
         g_slots = sb("g_slots", [P, 4, P], F32)
-        warm = placed("warm", [P, 32], F32, 14 * KIB - 64)
-        nc.vector.memset(warm[:], 0.0)
+        warm = sb("warm", [P, 2], F32)
         nc.vector.memset(xts[:], 0)
-        nc.vector.memset(sw2[:], 0)
-        for q in range(4):
-            nc.vector.memset(sw1[32 * q : 32 * q + 24, :], 0)
-        nc.vector.memset(planes1[:], 0)
+        nc.gpsimd.memset(sw2[:], 0)
+        nc.vector.memset(warm[:], 0.0)
+        nc.vector.memset(shifted1[:], 0)
         nc.vector.memset(g_slots[:], 0.0)
         nc.scalar.activation(warm[:, 1:2], warm[:, 0:1], ACT.Sigmoid)
 
@@ -92,17 +90,18 @@ def tile_list_cross_modal_shortlist_kernel(
             nc.sync.dma_start(raw[:], rows.rearrange("(p e) t -> p e t", e=2))
             return raw
 
-        w1 = [load_words(tab_words, 0, "w1_0"), load_words(tab_words, 1, "w1_1", 14 * KIB)]
-        xtw = placed("xtw", [P, KP, M // 2], I32, 12 * KIB)
-        nc.sync.dma_start(xtw[:], xt_words.bitcast(I32).rearrange("a p c -> p a c"))
-        g_rows = sb("g_rows", [JP, 512], F32)
-        ident = sb("ident", [P, P], F32)
-        make_identity(nc, ident[:])
-        nc.gpsimd.dma_start(g_rows[:], g.rearrange("(a c) -> a c", a=JP))
+        w1 = [load_words(tab_words, 0, "w1_0")]
         for q in range(4):
-            nc.scalar.dma_start(xts[32 * q : 32 * q + 4, :, :], xs[:, 4 * q : 4 * q + 4, :].rearrange("a r c -> r a c"))
+            nc.sync.dma_start(xts[32 * q : 32 * q + 4, :, :], xs[:, 4 * q : 4 * q + 4, :].rearrange("a r c -> r a c"))
+        g_rows = sb("g_rows", [JP, 512], F32)
+        nc.sync.dma_start(g_rows[:], g.rearrange("(a c) -> a c", a=JP))
+        w1.append(load_words(tab_words, 1, "w1_1", 0))
+        xtw = sb("xtw", [P, KP, M // 2], I32)
+        nc.sync.dma_start(xtw[:], xt_words.bitcast(I32).rearrange("a p c -> p a c"))
         for q in range(4):
             nc.gpsimd.dma_start(sw2[32 * q : 32 * q + 8, :], s2[:, 4 * q : 4 * q + 4, :])
+        ident = sb("ident", [P, P], F32)
+        make_identity(nc, ident[:])
 
         nc.scalar.copy(
             g_slots[0:JP].rearrange("p i (q s) -> p i q s", s=8), g_rows[:].rearrange("p (q i s) -> p i q s", i=4, s=8)
@@ -148,22 +147,22 @@ def tile_list_cross_modal_shortlist_kernel(
             return slice(256 * i + P * a, 256 * i + P * (a + 1))
 
         ordered1 = sb("ordered1", [P, S // 4], I32)
-        gather_scales(sw1, placed("picked1", [P, S], U8, 29 * KIB + 512), ordered1)
-        for kp in range(KP):
-            nc.scalar.dma_start(planes1[0:100, kp, :], ordered1[24 + 4 * kp : 124 + 4 * kp, :])
-        x_raw = [[load_x(0, kp, (26 + 4 * kp) * KIB) for kp in range(KP)]]
+        gather_scales(sw1, sb("picked1", [P, S], U8), ordered1)
+        nc.sync.dma_start(shifted1[0:100, :], ordered1[4:104, :])
+        planes1 = [ordered1, shifted1]
+        x_raw = [[load_x(0, kp) for kp in range(KP)]]
         v1 = [gather_words(w1[0][:].bitcast(U32), "v1_0", 1)]
-        w2 = [load_words(tab2_words, 0, "w2_0", 34 * KIB)]
+        w2 = [load_words(tab2_words, 0, "w2_0", 12 * KIB)]
         v1.append(gather_words(w1[1][:].bitcast(U32), "v1_1", JP))
         w2.append(load_words(tab2_words, 1, "w2_1"))
         wd_raw = [[load_wd(0, c) for c in range(PIECES)], [load_wd(1, c) for c in range(PIECES - 1)]]
-        wd_raw[1].append(load_wd(1, PIECES - 1, 22 * KIB))
+        wd_raw[1].append(load_wd(1, PIECES - 1, 8 * KIB))
         x_raw.append([load_x(1, kp) for kp in range(KP)])
         plane2 = sb("plane2", [P, S // 4], I32)
-        gather_scales(sw2, placed("picked2", [P, S], U8, 14 * KIB), plane2)
+        gather_scales(sw2, placed("picked2", [P, S], U8, 0), plane2)
         x_woven = cast_x(0, x_raw[0], 1)
         v2 = [gather_words(w2[0][:].bitcast(U32), "v2_0", 1)]
-        x_first = quantize("x0", x_woven[0], KP, HALF, 34 * KIB)
+        x_first = quantize("x0", x_woven[0], KP, HALF, 12 * KIB)
         v2.append(gather_words(w2[1][:].bitcast(U32), "v2_1", JP))
 
         gated = [sb("gated%d" % a, [P, 4, M], F32) for a in range(JP)]
@@ -174,7 +173,7 @@ def tile_list_cross_modal_shortlist_kernel(
                     nc.tensor.matmul_mx(
                         out=acc[:],
                         lhsT=v1[kp][:, cols(a, i)].bitcast(FP8X4),
-                        lhsT_scale=planes1[:, kp, :].bitcast(U8)[:, cols(a, i)],
+                        lhsT_scale=planes1[kp][:].bitcast(U8)[:, cols(a, i)],
                         rhs=xtw[:, kp, :].bitcast(U8).bitcast(FP4X4),
                         rhs_scale=xts[:, kp, :].bitcast(U8),
                         start=(kp == 0),
@@ -258,7 +257,7 @@ def tile_list_cross_modal_shortlist_kernel(
         picked0 = gather_words(pairs0[:].rearrange("p t e -> p (t e)").bitcast(U32), "wp0", JP)
         pairs1 = cast_pair(1)
         picked1 = gather_words(pairs1[:].rearrange("p t e -> p (t e)").bitcast(U32), "wp1", JP)
-        turned0 = placed("turned0", [P, JP, 2 * P, 4], BF16, 22 * KIB)
+        turned0 = placed("turned0", [P, JP, 2 * P, 4], BF16, 8 * KIB)
         turn_pair(picked0, turned0)
         x_woven = cast_x(1, x_raw[1], 2)
         x_third = quantize("x2", x_woven[0], KP, P)

@@ -51,36 +51,37 @@ def tile_list_cross_modal_shortlist_kernel(
 
         offsets = keep.tile([P, S // 16], U16, name="offsets")
         nc.sync.dma_start(offsets[:], offs)
-
-        s1 = tab_scales.bitcast(I32)
-        s2 = tab2_scales.bitcast(I32)
-        xs = xt_scales.bitcast(I32)
+        g_rows = sb("g_rows", [JP, 512], F32)
+        nc.scalar.dma_start(g_rows[:], g.rearrange("(a c) -> a c", a=JP))
 
         sw1 = sb("sw1", [P, T // 4], I32)
-        nc.vector.memset(sw1[:], 0)
-        for q in range(4):
-            nc.sync.dma_start(sw1[32 * q : 32 * q + 8, :], s1[:, 4 * q : 4 * q + 4, :])
         sw2 = sb("sw2", [P, T // 4], I32)
         xts = sb("xts", [P, KP, M // 4], I32)
         shifted1 = sb("shifted1", [P, S // 4], I32)
         g_slots = sb("g_slots", [P, 4, P], F32)
         warm = sb("warm", [P, 2], F32)
-        nc.vector.memset(xts[:], 0)
-        nc.gpsimd.memset(sw2[:], 0)
+        nc.vector.memset(sw1[:], 0)
         nc.vector.memset(warm[:], 0.0)
+        nc.vector.memset(sw2[:], 0)
+        nc.vector.memset(xts[:], 0)
         nc.vector.memset(shifted1[:], 0)
         nc.vector.memset(g_slots[:], 0.0)
+        ident = sb("ident", [P, P], F32)
+        make_identity(nc, ident[:])
         nc.scalar.activation(warm[:, 1:2], warm[:, 0:1], ACT.Sigmoid)
+
+        def load_scales(win, src):
+            for q in range(4):
+                nc.sync.dma_start(win[32 * q : 32 * q + 8, :], src.bitcast(I32)[:, 4 * q : 4 * q + 4, :])
 
         def load_words(src, kp, name, at=None):
             win = tile(name, [P, T], I32, at)
             nc.sync.dma_start(win[:], src[kp].rearrange("p t i -> p (t i)").bitcast(I32))
             return win
 
-        def load_x(half, kp, at=None):
-            raw = tile("x%d%d" % (half, kp), [P, 4, HALF], F32, at)
-            rows = x[512 * kp : 512 * (kp + 1), HALF * half : HALF * (half + 1)]
-            nc.sync.dma_start(raw[:], rows.rearrange("(p i) m -> p i m", i=4))
+        def load_x(kp):
+            raw = sb("x%d" % kp, [P, 4, M], F32)
+            nc.sync.dma_start(raw[:], x[512 * kp : 512 * (kp + 1), :].rearrange("(p i) m -> p i m", i=4))
             return raw
 
         def load_wd(pair, piece, at=None):
@@ -90,18 +91,19 @@ def tile_list_cross_modal_shortlist_kernel(
             nc.sync.dma_start(raw[:], rows.rearrange("(p e) t -> p e t", e=2))
             return raw
 
+        def load_tile(nt, at=None):
+            win = tile("wd%d" % nt, [P, T], F32, at)
+            nc.sync.dma_start(win[:], wdT[P * nt : P * (nt + 1), :])
+            return win
+
+        load_scales(sw1, tab_scales)
+        x_raw = [load_x(0)]
+        load_scales(sw2, tab2_scales)
+        x_raw.append(load_x(1))
         w1 = [load_words(tab_words, 0, "w1_0")]
+        xs = xt_scales.bitcast(I32)
         for q in range(4):
             nc.sync.dma_start(xts[32 * q : 32 * q + 4, :, :], xs[:, 4 * q : 4 * q + 4, :].rearrange("a r c -> r a c"))
-        g_rows = sb("g_rows", [JP, 512], F32)
-        nc.sync.dma_start(g_rows[:], g.rearrange("(a c) -> a c", a=JP))
-        w1.append(load_words(tab_words, 1, "w1_1", 0))
-        xtw = sb("xtw", [P, KP, M // 2], I32)
-        nc.sync.dma_start(xtw[:], xt_words.bitcast(I32).rearrange("a p c -> p a c"))
-        for q in range(4):
-            nc.gpsimd.dma_start(sw2[32 * q : 32 * q + 8, :], s2[:, 4 * q : 4 * q + 4, :])
-        ident = sb("ident", [P, P], F32)
-        make_identity(nc, ident[:])
 
         nc.scalar.copy(
             g_slots[0:JP].rearrange("p i (q s) -> p i q s", s=8), g_rows[:].rearrange("p (q i s) -> p i q s", i=4, s=8)
@@ -119,22 +121,20 @@ def tile_list_cross_modal_shortlist_kernel(
                 picked[:].bitcast(I32).rearrange("p (b i h) -> p i b h", i=4, h=2),
             )
 
-        def gather_words(words, name, parts):
-            picked = sb(name, [P, S], U32)
+        def gather_words(words, name, parts, at=None):
+            picked = tile(name, [P, S], U32, at)
             blocks = picked[:].rearrange("p (i b s) -> p b i s", i=4, s=8)
             for part in range(parts):
                 first, last = 32 * part // parts, 32 * (part + 1) // parts
                 nc.vector.tensor_copy(blocks[:, first:last], words.indirect(offsets[:, 2 * first : 2 * last]))
             return picked
 
-        def cast_x(half, raws, parts):
-            width = HALF // parts
-            woven = sb("xb%d" % half, [P, parts, KP, width, 4], BF16)
-            for kp in range(KP):
-                for part in range(parts):
-                    rows = raws[kp][:, :, width * part : width * (part + 1)]
-                    nc.gpsimd.tensor_scalar(woven[:, part, kp], rows.rearrange("p i m -> p m i"), 1.0, 0.0, ALU.mult, ALU.add)
-            return [woven[:, part].rearrange("p a m i -> p (a m i)") for part in range(parts)]
+        def cast_x(kp):
+            woven = sb("xb%d" % kp, [P, M, 4], BF16)
+            nc.scalar.copy(
+                woven[:].rearrange("p (c r) i -> p c i r", r=4), x_raw[kp][:].rearrange("p i (c r) -> p c i r", r=4)
+            )
+            return woven[:].rearrange("p m i -> p (m i)")
 
         def quantize(name, woven, passes, width, at=None):
             shape = [P, passes * width]
@@ -146,46 +146,6 @@ def tile_list_cross_modal_shortlist_kernel(
         def cols(a, i):
             return slice(256 * i + P * a, 256 * i + P * (a + 1))
 
-        ordered1 = sb("ordered1", [P, S // 4], I32)
-        gather_scales(sw1, sb("picked1", [P, S], U8), ordered1)
-        nc.sync.dma_start(shifted1[0:100, :], ordered1[4:104, :])
-        planes1 = [ordered1, shifted1]
-        x_raw = [[load_x(0, kp) for kp in range(KP)]]
-        v1 = [gather_words(w1[0][:].bitcast(U32), "v1_0", 1)]
-        w2 = [load_words(tab2_words, 0, "w2_0", 12 * KIB)]
-        v1.append(gather_words(w1[1][:].bitcast(U32), "v1_1", JP))
-        w2.append(load_words(tab2_words, 1, "w2_1"))
-        wd_raw = [[load_wd(0, c) for c in range(PIECES)], [load_wd(1, c) for c in range(PIECES - 1)]]
-        wd_raw[1].append(load_wd(1, PIECES - 1, 8 * KIB))
-        x_raw.append([load_x(1, kp) for kp in range(KP)])
-        plane2 = sb("plane2", [P, S // 4], I32)
-        gather_scales(sw2, placed("picked2", [P, S], U8, 0), plane2)
-        x_woven = cast_x(0, x_raw[0], 1)
-        v2 = [gather_words(w2[0][:].bitcast(U32), "v2_0", 1)]
-        x_first = quantize("x0", x_woven[0], KP, HALF, 12 * KIB)
-        v2.append(gather_words(w2[1][:].bitcast(U32), "v2_1", JP))
-
-        gated = [sb("gated%d" % a, [P, 4, M], F32) for a in range(JP)]
-        for a in range(JP):
-            for i in range(4):
-                acc = next_bank([P, M])
-                for kp in range(KP):
-                    nc.tensor.matmul_mx(
-                        out=acc[:],
-                        lhsT=v1[kp][:, cols(a, i)].bitcast(FP8X4),
-                        lhsT_scale=planes1[kp][:].bitcast(U8)[:, cols(a, i)],
-                        rhs=xtw[:, kp, :].bitcast(U8).bitcast(FP4X4),
-                        rhs_scale=xts[:, kp, :].bitcast(U8),
-                        start=(kp == 0),
-                        stop=(kp == KP - 1),
-                    )
-                sig = sb("sig%d%d" % (a, i), [P, M], F32)
-                nc.scalar.activation(sig[:], acc[:], ACT.Sigmoid)
-                nc.gpsimd.tensor_scalar(gated[a][:, i, :], sig[:], gains[:, i, a : a + 1], 0.0, ALU.mult, ALU.add)
-
-        root_warm = sb("root_warm", [P, 1], F32)
-        nc.scalar.activation(root_warm[:], sig[:, 0:1], ACT.Sqrt)
-
         def cast_pair(pair):
             pairs = sb("pairs%d" % pair, [P, T, 2], BF16)
             width = T // PIECES
@@ -193,53 +153,51 @@ def tile_list_cross_modal_shortlist_kernel(
                 nc.scalar.copy(pairs[:, width * c : width * (c + 1), :], wd_raw[pair][c][:].rearrange("p e t -> p t e"))
             return pairs
 
-        def turn_pair(picked, turned):
-            for a in range(JP):
-                bank = next_bank([P, 4, P])
-                for i in range(4):
-                    nc.tensor.transpose(bank[:, i, :], picked[:, cols(a, i)].bitcast(F32), ident[:])
-                nc.scalar.copy(turned[:, a], bank[:].bitcast(BF16).rearrange("p i n -> p n i"))
-
-        def make_h(xq, first, width):
-            codes, scales = xq
-            woven = sb("h%d" % first, [P, JP, width, 4], BF16)
+        def make_h(first, width, at=None):
+            woven = tile("h%d" % first, [P, JP, width, 4], BF16, at)
             for a in range(JP):
                 for c in range(width // P):
-                    col = first + P * c
+                    span = slice(first + P * c, first + P * (c + 1))
                     bank = next_bank([P, 4, P])
                     for i in range(4):
                         for kp in range(KP):
-                            span = slice(width * kp + P * c, width * kp + P * (c + 1))
                             nc.tensor.matmul_mx(
                                 out=bank[:, i, :],
                                 lhsT=v2[kp][:, cols(a, i)].bitcast(FP8X4),
                                 lhsT_scale=plane2[4 * kp : P, :].bitcast(U8)[:, cols(a, i)],
-                                rhs=codes[:, span].bitcast(FP8X4),
-                                rhs_scale=scales[:, span],
+                                rhs=xq[kp][0][:, span].bitcast(FP8X4),
+                                rhs_scale=xq[kp][1][:, span],
                                 start=(kp == 0),
                                 stop=(kp == KP - 1),
                             )
                     nc.vector.tensor_tensor(
                         woven[:, a, P * c : P * (c + 1), :].rearrange("p (u r) i -> p u i r", r=2),
                         bank[:].rearrange("p i (u r) -> p u i r", r=2),
-                        gated[a][:, :, col : col + P].rearrange("p i (u r) -> p u i r", r=2),
+                        gated[a][:, :, span].rearrange("p i (u r) -> p u i r", r=2),
                         ALU.mult,
                     )
-            return quantize("h%d" % first, woven[:].rearrange("p a m i -> p (a m i)"), JP, width)
+            return woven[:].rearrange("p a m i -> p (a m i)")
+
+        def turn(name, picked, rows, dtype, at=None):
+            turned = tile(name, [P, JP, rows, 4], BF16, at)
+            for a in range(JP):
+                bank = next_bank([P, 4, P])
+                for i in range(4):
+                    nc.tensor.transpose(bank[:, i, :], picked[:, cols(a, i)].bitcast(F32), ident[:])
+                nc.scalar.copy(turned[:, a], bank[:].bitcast(dtype).rearrange("p i n -> p n i"))
+            return turned
 
         out_rows = out.rearrange("(t p) m -> p t m", p=P)
 
         def finish(tiles, hq, first, width):
             bank = next_bank([P, len(tiles), width])
             for at, nt in enumerate(tiles):
-                codes, scales = wq[nt // 2]
                 for a in range(JP):
-                    rows = slice(2 * P * a + P * (nt % 2), 2 * P * a + P * (nt % 2 + 1))
                     span = slice(width * a, width * (a + 1))
                     nc.tensor.matmul_mx(
                         out=bank[:, at, :],
-                        lhsT=codes[:, rows].bitcast(FP8X4),
-                        lhsT_scale=scales[:, rows],
+                        lhsT=wq[nt][a][0].bitcast(FP8X4),
+                        lhsT_scale=wq[nt][a][1],
                         rhs=hq[0][:, span].bitcast(FP8X4),
                         rhs_scale=hq[1][:, span],
                         start=(a == 0),
@@ -252,23 +210,80 @@ def tile_list_cross_modal_shortlist_kernel(
             nc.scalar.activation(res[:], mag[:], ACT.Sqrt)
             nc.sync.dma_start(out_rows[:, tiles[0] : tiles[-1] + 1, first : first + width], res[:])
 
+        def quantize_rows(name, turned, tiles):
+            codes, scales = quantize(name, turned[:].rearrange("p a n i -> p (a n i)"), JP, P * tiles)
+            spans = [[slice(P * (tiles * a + t), P * (tiles * a + t + 1)) for a in range(JP)] for t in range(tiles)]
+            return [[(codes[:, span], scales[:, span]) for span in row] for row in spans]
+
+        def open_gates(a):
+            sigs = []
+            for i in range(4):
+                acc = next_bank([P, M])
+                for kp in range(KP):
+                    nc.tensor.matmul_mx(
+                        out=acc[:],
+                        lhsT=v1[kp][:, cols(a, i)].bitcast(FP8X4),
+                        lhsT_scale=planes1[kp][:].bitcast(U8)[:, cols(a, i)],
+                        rhs=xtw[:, kp, :].bitcast(U8).bitcast(FP4X4),
+                        rhs_scale=xts[:, kp, :].bitcast(U8),
+                        start=(kp == 0),
+                        stop=(kp == KP - 1),
+                    )
+                sigs.append(sb("sig%d%d" % (a, i), [P, M], F32))
+                nc.scalar.activation(sigs[i][:], acc[:], ACT.Sigmoid)
+            return sigs
+
+        def gains_on_scalar(a, span):
+            for i in range(4):
+                nc.scalar.activation(gated[a][:, i, span], sigs[a][i][:, span], ACT.Copy, scale=gains[:, i, a : a + 1])
+
+        def gains_on_vector(a, span):
+            for i in range(4):
+                nc.vector.tensor_scalar(gated[a][:, i, span], sigs[a][i][:, span], gains[:, i, a : a + 1], None, ALU.mult)
+
+        ordered1 = sb("ordered1", [P, S // 4], I32)
+        gather_scales(sw1, sb("picked1", [P, S], U8), ordered1)
+        w1.append(load_words(tab_words, 1, "w1_1", 2 * KIB))
+        xtw = sb("xtw", [P, KP, M // 2], I32)
+        nc.sync.dma_start(xtw[:], xt_words.bitcast(I32).rearrange("a p c -> p a c"))
+        nc.sync.dma_start(shifted1[0:100, :], ordered1[4:104, :])
+        planes1 = [ordered1, shifted1]
+        w2 = [load_words(tab2_words, 0, "w2_0"), load_words(tab2_words, 1, "w2_1", 10 * KIB)]
+        wd_raw = [[load_wd(0, c) for c in range(PIECES)]]
+        wd_tiles = [load_tile(2, 18 * KIB), load_tile(3)]
+
+        plane2 = sb("plane2", [P, S // 4], I32)
+        gather_scales(sw2, placed("picked2", [P, S], U8, 0), plane2)
+        x_woven = [cast_x(kp) for kp in range(KP)]
+        xq = [quantize("x0", x_woven[0], 1, M, 0)]
+        v1 = [gather_words(w1[0][:].bitcast(U32), "v1_0", 1)]
+        v1.append(gather_words(w1[1][:].bitcast(U32), "v1_1", JP))
+        xq.append(quantize("x1", x_woven[1], 1, M, 2 * KIB))
+        gated = [sb("gated0", [P, 4, M], F32)]
+        sigs = [open_gates(a) for a in range(JP)]
+        gains_on_scalar(0, slice(0, M))
+        v2 = [gather_words(w2[0][:].bitcast(U32), "v2_0", 1)]
+        v2.append(gather_words(w2[1][:].bitcast(U32), "v2_1", 1))
+        gated.append(placed("gated1", [P, 4, M], F32, 10 * KIB))
+        gains_on_vector(1, slice(0, M))
         pairs0 = cast_pair(0)
-        h_first = make_h(x_first, 0, HALF)
-        picked0 = gather_words(pairs0[:].rearrange("p t e -> p (t e)").bitcast(U32), "wp0", JP)
-        pairs1 = cast_pair(1)
-        picked1 = gather_words(pairs1[:].rearrange("p t e -> p (t e)").bitcast(U32), "wp1", JP)
-        turned0 = placed("turned0", [P, JP, 2 * P, 4], BF16, 8 * KIB)
-        turn_pair(picked0, turned0)
-        x_woven = cast_x(1, x_raw[1], 2)
-        x_third = quantize("x2", x_woven[0], KP, P)
-        wq = [quantize("w0", turned0[:].rearrange("p a n i -> p (a n i)"), JP, 2 * P)]
-        x_fourth = quantize("x3", x_woven[1], KP, P)
-        turned1 = sb("turned1", [P, JP, 2 * P, 4], BF16)
-        turn_pair(picked1, turned1)
+        root_warm = sb("root_warm", [P, 1], F32)
+        nc.scalar.activation(root_warm[:], pairs0[:, T - 1, 0:1], ACT.Sqrt, scale=0.0)
+        h_first = make_h(0, HALF)
+        picked2 = gather_words(wd_tiles[0][:].bitcast(U32), "wp2", 1)
+        h_first = quantize("h0", h_first, JP, HALF)
+        turned2 = turn("t2", picked2, P, F32)
+        picked0 = gather_words(pairs0[:].rearrange("p t e -> p (t e)").bitcast(U32), "wp0", JP, 18 * KIB)
+        turned0 = turn("t0", picked0, 2 * P, BF16, 26 * KIB)
+        picked3 = gather_words(wd_tiles[1][:].bitcast(U32), "wp3", JP)
+        turned3 = turn("t3", picked3, P, F32, 30 * KIB)
+        wq2 = quantize_rows("w2", turned2, 1)
+        wq = quantize_rows("w0", turned0, 2) + wq2
+        h_third = make_h(HALF, P, 26 * KIB)
+        wq.extend(quantize_rows("w3", turned3, 1))
+        h_third = quantize("h2", h_third, JP, P)
+        h_fourth = quantize("h3", make_h(HALF + P, P, 30 * KIB), JP, P)
         finish([0, 1], h_first, 0, HALF)
-        h_third = make_h(x_third, HALF, P)
-        wq.append(quantize("w1", turned1[:].rearrange("p a n i -> p (a n i)"), JP, 2 * P))
-        h_fourth = make_h(x_fourth, HALF + P, P)
         finish([2, 3], h_first, 0, HALF)
         finish([0, 1, 2, 3], h_third, HALF, P)
         finish([0, 1, 2, 3], h_fourth, HALF + P, P)

@@ -20,7 +20,6 @@ ALU = mybir.AluOpType
 P = 128
 KP = K // 512
 JP = S // 512
-HALF = M // 2
 PIECES = 4
 KIB = 1024
 
@@ -34,14 +33,10 @@ def tile_list_cross_modal_shortlist_kernel(
         stream = ctx.enter_context(tc.tile_pool(name="stream", bufs=1))
         psum = ctx.enter_context(tc.psum_pool(name="psum", bufs=1))
 
-        def sb(name, shape, dtype):
-            return keep.tile(shape, dtype, name=name, align_bytes=64)
-
-        def placed(name, shape, dtype, at):
+        def sb(name, shape, dtype, at=None):
+            if at is None:
+                return keep.tile(shape, dtype, name=name, align_bytes=64)
             return stream.tile(shape, dtype, name=name, align_bytes=64, offset=at)
-
-        def tile(name, shape, dtype, at):
-            return sb(name, shape, dtype) if at is None else placed(name, shape, dtype, at)
 
         banks = []
 
@@ -51,8 +46,6 @@ def tile_list_cross_modal_shortlist_kernel(
 
         offsets = keep.tile([P, S // 16], U16, name="offsets")
         nc.sync.dma_start(offsets[:], offs)
-        g_rows = sb("g_rows", [JP, 512], F32)
-        nc.scalar.dma_start(g_rows[:], g.rearrange("(a c) -> a c", a=JP))
 
         sw1 = sb("sw1", [P, T // 4], I32)
         sw2 = sb("sw2", [P, T // 4], I32)
@@ -60,22 +53,22 @@ def tile_list_cross_modal_shortlist_kernel(
         shifted1 = sb("shifted1", [P, S // 4], I32)
         g_slots = sb("g_slots", [P, 4, P], F32)
         warm = sb("warm", [P, 2], F32)
-        nc.vector.memset(sw1[:], 0)
-        nc.vector.memset(warm[:], 0.0)
-        nc.vector.memset(sw2[:], 0)
-        nc.vector.memset(xts[:], 0)
-        nc.vector.memset(shifted1[:], 0)
-        nc.vector.memset(g_slots[:], 0.0)
         ident = sb("ident", [P, P], F32)
         make_identity(nc, ident[:])
+        nc.vector.memset(sw1[:], 0)
+        nc.vector.memset(sw2[:], 0)
+        nc.vector.memset(xts[:], 0)
+        nc.vector.memset(warm[:], 0.0)
+        nc.vector.memset(shifted1[:], 0)
+        nc.vector.memset(g_slots[:], 0.0)
         nc.scalar.activation(warm[:, 1:2], warm[:, 0:1], ACT.Sigmoid)
 
-        def load_scales(win, src):
+        def load_scales(queue, win, src):
             for q in range(4):
-                nc.sync.dma_start(win[32 * q : 32 * q + 8, :], src.bitcast(I32)[:, 4 * q : 4 * q + 4, :])
+                queue.dma_start(win[32 * q : 32 * q + 8, :], src.bitcast(I32)[:, 4 * q : 4 * q + 4, :])
 
         def load_words(src, kp, name, at=None):
-            win = tile(name, [P, T], I32, at)
+            win = sb(name, [P, T], I32, at)
             nc.sync.dma_start(win[:], src[kp].rearrange("p t i -> p (t i)").bitcast(I32))
             return win
 
@@ -84,26 +77,29 @@ def tile_list_cross_modal_shortlist_kernel(
             nc.sync.dma_start(raw[:], x[512 * kp : 512 * (kp + 1), :].rearrange("(p i) m -> p i m", i=4))
             return raw
 
-        def load_wd(pair, piece, at=None):
+        def load_pair_piece(piece, at=None):
             width = T // PIECES
-            raw = tile("wd%d%d" % (pair, piece), [P, 2, width], F32, at)
-            rows = wdT[2 * P * pair : 2 * P * (pair + 1), width * piece : width * (piece + 1)]
+            raw = sb("pair%d" % piece, [P, 2, width], F32, at)
+            rows = wdT[0 : 2 * P, width * piece : width * (piece + 1)]
             nc.sync.dma_start(raw[:], rows.rearrange("(p e) t -> p e t", e=2))
             return raw
 
-        def load_tile(nt, at=None):
-            win = tile("wd%d" % nt, [P, T], F32, at)
+        def load_wd(nt):
+            win = sb("wd%d" % nt, [P, T], F32)
             nc.sync.dma_start(win[:], wdT[P * nt : P * (nt + 1), :])
             return win
 
-        load_scales(sw1, tab_scales)
-        x_raw = [load_x(0)]
-        load_scales(sw2, tab2_scales)
-        x_raw.append(load_x(1))
+        load_scales(nc.sync, sw1, tab_scales)
+        load_scales(nc.gpsimd, sw2, tab2_scales)
         w1 = [load_words(tab_words, 0, "w1_0")]
         xs = xt_scales.bitcast(I32)
         for q in range(4):
             nc.sync.dma_start(xts[32 * q : 32 * q + 4, :, :], xs[:, 4 * q : 4 * q + 4, :].rearrange("a r c -> r a c"))
+        g_rows = sb("g_rows", [JP, 512], F32)
+        nc.sync.dma_start(g_rows[:], g.rearrange("(a c) -> a c", a=JP))
+        w1.append(load_words(tab_words, 1, "w1_1", 0))
+        xtw = sb("xtw", [P, KP, M // 2], I32)
+        nc.sync.dma_start(xtw[:], xt_words.bitcast(I32).rearrange("a p c -> p a c"))
 
         nc.scalar.copy(
             g_slots[0:JP].rearrange("p i (q s) -> p i q s", s=8), g_rows[:].rearrange("p (q i s) -> p i q s", i=4, s=8)
@@ -121,102 +117,53 @@ def tile_list_cross_modal_shortlist_kernel(
                 picked[:].bitcast(I32).rearrange("p (b i h) -> p i b h", i=4, h=2),
             )
 
-        def gather_words(words, name, parts, at=None):
-            picked = tile(name, [P, S], U32, at)
+        def gather_words(words, name, parts):
+            picked = sb(name, [P, S], U32)
             blocks = picked[:].rearrange("p (i b s) -> p b i s", i=4, s=8)
             for part in range(parts):
                 first, last = 32 * part // parts, 32 * (part + 1) // parts
                 nc.vector.tensor_copy(blocks[:, first:last], words.indirect(offsets[:, 2 * first : 2 * last]))
             return picked
 
-        def cast_x(kp):
-            woven = sb("xb%d" % kp, [P, M, 4], BF16)
-            nc.scalar.copy(
-                woven[:].rearrange("p (c r) i -> p c i r", r=4), x_raw[kp][:].rearrange("p i (c r) -> p c i r", r=4)
-            )
-            return woven[:].rearrange("p m i -> p (m i)")
+        def weave(name, planes, copies, at=None):
+            woven = sb(name, [P, M, 4], BF16, at)
+            width = M // len(copies)
+            for part, copy in enumerate(copies):
+                span = slice(width * part, width * (part + 1))
+                copy(
+                    woven[:, span, :].rearrange("p (c r) i -> p c i r", r=4),
+                    planes[:, :, span].rearrange("p i (c r) -> p c i r", r=4),
+                )
+            return woven
 
-        def quantize(name, woven, passes, width, at=None):
-            shape = [P, passes * width]
-            codes = sb(name + "c", shape, U32) if at is None else placed(name + "c", shape, U32, at)
-            scales = sb(name + "s", [P, passes * width], U8)
-            nc.vector.quantize_mx(out=codes[:].bitcast(FP8X4), scales=scales[:], in_=woven)
+        def quantize(name, woven, width, at=None):
+            codes = sb(name + "c", [P, width], U32, at)
+            scales = sb(name + "s", [P, width], U8)
+            nc.vector.quantize_mx(out=codes[:].bitcast(FP8X4), scales=scales[:], in_=woven.rearrange("p n i -> p (n i)"))
             return codes, scales
 
         def cols(a, i):
             return slice(256 * i + P * a, 256 * i + P * (a + 1))
 
-        def cast_pair(pair):
-            pairs = sb("pairs%d" % pair, [P, T, 2], BF16)
-            width = T // PIECES
-            for c in range(PIECES):
-                nc.scalar.copy(pairs[:, width * c : width * (c + 1), :], wd_raw[pair][c][:].rearrange("p e t -> p t e"))
-            return pairs
+        ordered1 = sb("ordered1", [P, S // 4], I32)
+        gather_scales(sw1, sb("picked1", [P, S], U8), ordered1)
+        nc.sync.dma_start(shifted1[0:100, :], ordered1[4:104, :])
+        planes1 = [ordered1, shifted1]
+        x_raw = [load_x(0)]
+        w2 = [load_words(tab2_words, 0, "w2_0", 8 * KIB)]
+        x_raw.append(load_x(1))
+        w2.append(load_words(tab2_words, 1, "w2_1"))
+        pair_raw = [load_pair_piece(c) for c in range(PIECES - 1)]
+        pair_raw.append(load_pair_piece(PIECES - 1, 18 * KIB))
+        wd = {nt: load_wd(nt) for nt in (2, 3)}
 
-        def make_h(first, width, at=None):
-            woven = tile("h%d" % first, [P, JP, width, 4], BF16, at)
-            for a in range(JP):
-                for c in range(width // P):
-                    span = slice(first + P * c, first + P * (c + 1))
-                    bank = next_bank([P, 4, P])
-                    for i in range(4):
-                        for kp in range(KP):
-                            nc.tensor.matmul_mx(
-                                out=bank[:, i, :],
-                                lhsT=v2[kp][:, cols(a, i)].bitcast(FP8X4),
-                                lhsT_scale=plane2[4 * kp : P, :].bitcast(U8)[:, cols(a, i)],
-                                rhs=xq[kp][0][:, span].bitcast(FP8X4),
-                                rhs_scale=xq[kp][1][:, span],
-                                start=(kp == 0),
-                                stop=(kp == KP - 1),
-                            )
-                    nc.vector.tensor_tensor(
-                        woven[:, a, P * c : P * (c + 1), :].rearrange("p (u r) i -> p u i r", r=2),
-                        bank[:].rearrange("p i (u r) -> p u i r", r=2),
-                        gated[a][:, :, span].rearrange("p i (u r) -> p u i r", r=2),
-                        ALU.mult,
-                    )
-            return woven[:].rearrange("p a m i -> p (a m i)")
+        v1 = [gather_words(w1[0][:].bitcast(U32), "v1_0", 1)]
+        v1.append(gather_words(w1[1][:].bitcast(U32), "v1_1", JP))
+        plane2 = sb("plane2", [P, S // 4], I32)
+        gather_scales(sw2, sb("picked2", [P, S], U8, 0), plane2)
 
-        def turn(name, picked, rows, dtype, at=None):
-            turned = tile(name, [P, JP, rows, 4], BF16, at)
-            for a in range(JP):
-                bank = next_bank([P, 4, P])
-                for i in range(4):
-                    nc.tensor.transpose(bank[:, i, :], picked[:, cols(a, i)].bitcast(F32), ident[:])
-                nc.scalar.copy(turned[:, a], bank[:].bitcast(dtype).rearrange("p i n -> p n i"))
-            return turned
-
-        out_rows = out.rearrange("(t p) m -> p t m", p=P)
-
-        def finish(tiles, hq, first, width):
-            bank = next_bank([P, len(tiles), width])
-            for at, nt in enumerate(tiles):
-                for a in range(JP):
-                    span = slice(width * a, width * (a + 1))
-                    nc.tensor.matmul_mx(
-                        out=bank[:, at, :],
-                        lhsT=wq[nt][a][0].bitcast(FP8X4),
-                        lhsT_scale=wq[nt][a][1],
-                        rhs=hq[0][:, span].bitcast(FP8X4),
-                        rhs_scale=hq[1][:, span],
-                        start=(a == 0),
-                        stop=(a == JP - 1),
-                    )
-            name = "%d_%d" % (tiles[0], first)
-            mag = sb("mag" + name, [P, len(tiles), width], F32)
-            res = sb("res" + name, [P, len(tiles), width], F32)
-            nc.scalar.activation(mag[:], bank[:], ACT.Abs)
-            nc.scalar.activation(res[:], mag[:], ACT.Sqrt)
-            nc.sync.dma_start(out_rows[:, tiles[0] : tiles[-1] + 1, first : first + width], res[:])
-
-        def quantize_rows(name, turned, tiles):
-            codes, scales = quantize(name, turned[:].rearrange("p a n i -> p (a n i)"), JP, P * tiles)
-            spans = [[slice(P * (tiles * a + t), P * (tiles * a + t + 1)) for a in range(JP)] for t in range(tiles)]
-            return [[(codes[:, span], scales[:, span]) for span in row] for row in spans]
-
-        def open_gates(a):
-            sigs = []
+        sig = {}
+        for a in range(JP):
             for i in range(4):
                 acc = next_bank([P, M])
                 for kp in range(KP):
@@ -229,61 +176,120 @@ def tile_list_cross_modal_shortlist_kernel(
                         start=(kp == 0),
                         stop=(kp == KP - 1),
                     )
-                sigs.append(sb("sig%d%d" % (a, i), [P, M], F32))
-                nc.scalar.activation(sigs[i][:], acc[:], ACT.Sigmoid)
-            return sigs
+                sig[a, i] = sb("sig%d%d" % (a, i), [P, M], F32)
+                nc.scalar.activation(sig[a, i][:], acc[:], ACT.Sigmoid)
 
-        def gains_on_scalar(a, span):
-            for i in range(4):
-                nc.scalar.activation(gated[a][:, i, span], sigs[a][i][:, span], ACT.Copy, scale=gains[:, i, a : a + 1])
-
-        def gains_on_vector(a, span):
-            for i in range(4):
-                nc.vector.tensor_scalar(gated[a][:, i, span], sigs[a][i][:, span], gains[:, i, a : a + 1], None, ALU.mult)
-
-        ordered1 = sb("ordered1", [P, S // 4], I32)
-        gather_scales(sw1, sb("picked1", [P, S], U8), ordered1)
-        w1.append(load_words(tab_words, 1, "w1_1", 2 * KIB))
-        xtw = sb("xtw", [P, KP, M // 2], I32)
-        nc.sync.dma_start(xtw[:], xt_words.bitcast(I32).rearrange("a p c -> p a c"))
-        nc.sync.dma_start(shifted1[0:100, :], ordered1[4:104, :])
-        planes1 = [ordered1, shifted1]
-        w2 = [load_words(tab2_words, 0, "w2_0"), load_words(tab2_words, 1, "w2_1", 10 * KIB)]
-        wd_raw = [[load_wd(0, c) for c in range(PIECES)]]
-        wd_tiles = [load_tile(2, 18 * KIB), load_tile(3)]
-
-        plane2 = sb("plane2", [P, S // 4], I32)
-        gather_scales(sw2, placed("picked2", [P, S], U8, 0), plane2)
-        x_woven = [cast_x(kp) for kp in range(KP)]
-        xq = [quantize("x0", x_woven[0], 1, M, 0)]
-        v1 = [gather_words(w1[0][:].bitcast(U32), "v1_0", 1)]
-        v1.append(gather_words(w1[1][:].bitcast(U32), "v1_1", JP))
-        xq.append(quantize("x1", x_woven[1], 1, M, 2 * KIB))
-        gated = [sb("gated0", [P, 4, M], F32)]
-        sigs = [open_gates(a) for a in range(JP)]
-        gains_on_scalar(0, slice(0, M))
+        x_woven = [weave("xb0", x_raw[0], [nc.scalar.copy])]
         v2 = [gather_words(w2[0][:].bitcast(U32), "v2_0", 1)]
-        v2.append(gather_words(w2[1][:].bitcast(U32), "v2_1", 1))
-        gated.append(placed("gated1", [P, 4, M], F32, 10 * KIB))
-        gains_on_vector(1, slice(0, M))
-        pairs0 = cast_pair(0)
+        xq = [quantize("x0", x_woven[0][:], M, 8 * KIB)]
+        x_woven.append(weave("xb1", x_raw[1], [nc.scalar.copy, nc.vector.tensor_copy]))
         root_warm = sb("root_warm", [P, 1], F32)
-        nc.scalar.activation(root_warm[:], pairs0[:, T - 1, 0:1], ACT.Sqrt, scale=0.0)
-        h_first = make_h(0, HALF)
-        picked2 = gather_words(wd_tiles[0][:].bitcast(U32), "wp2", 1)
-        h_first = quantize("h0", h_first, JP, HALF)
-        turned2 = turn("t2", picked2, P, F32)
-        picked0 = gather_words(pairs0[:].rearrange("p t e -> p (t e)").bitcast(U32), "wp0", JP, 18 * KIB)
-        turned0 = turn("t0", picked0, 2 * P, BF16, 26 * KIB)
-        picked3 = gather_words(wd_tiles[1][:].bitcast(U32), "wp3", JP)
-        turned3 = turn("t3", picked3, P, F32, 30 * KIB)
-        wq2 = quantize_rows("w2", turned2, 1)
-        wq = quantize_rows("w0", turned0, 2) + wq2
-        h_third = make_h(HALF, P, 26 * KIB)
-        wq.extend(quantize_rows("w3", turned3, 1))
-        h_third = quantize("h2", h_third, JP, P)
-        h_fourth = quantize("h3", make_h(HALF + P, P, 30 * KIB), JP, P)
-        finish([0, 1], h_first, 0, HALF)
-        finish([2, 3], h_first, 0, HALF)
-        finish([0, 1, 2, 3], h_third, HALF, P)
-        finish([0, 1, 2, 3], h_fourth, HALF + P, P)
+        nc.scalar.activation(root_warm[:], x_woven[1][:, 0, 0:1], ACT.Sqrt, bias=sig[1, 3][:, 0:1], scale=0.0)
+        xq.append(quantize("x1", x_woven[1][:], M))
+        v2.append(gather_words(w2[1][:].bitcast(U32), "v2_1", JP))
+
+        def make_h(a):
+            flat = sb("hp%d" % a, [P, 4, M], BF16)
+            for i in range(4):
+                acc = next_bank([P, M])
+                for kp in range(KP):
+                    nc.tensor.matmul_mx(
+                        out=acc[:],
+                        lhsT=v2[kp][:, cols(a, i)].bitcast(FP8X4),
+                        lhsT_scale=plane2[4 * kp : P, :].bitcast(U8)[:, cols(a, i)],
+                        rhs=xq[kp][0][:].bitcast(FP8X4),
+                        rhs_scale=xq[kp][1][:],
+                        start=(kp == 0),
+                        stop=(kp == KP - 1),
+                    )
+                nc.vector.scalar_tensor_tensor(
+                    flat[:, i, :], acc[:], gains[:, i, a : a + 1], sig[a, i][:], ALU.mult, ALU.mult
+                )
+            return flat
+
+        def cast_pair():
+            pairs = sb("pairs", [P, T, 2], BF16)
+            width = T // PIECES
+            for c in range(PIECES):
+                nc.scalar.copy(pairs[:, width * c : width * (c + 1), :], pair_raw[c][:].rearrange("p e t -> p t e"))
+            return pairs
+
+        def turn_pair(picked, at):
+            turned = sb("turned01", [P, JP, 2 * P, 4], BF16, at)
+            for a in range(JP):
+                bank = next_bank([P, 4, P])
+                for i in range(4):
+                    nc.tensor.transpose(bank[:, i, :], picked[:, cols(a, i)].bitcast(F32), ident[:])
+                nc.scalar.copy(turned[:, a], bank[:].bitcast(BF16).rearrange("p i n -> p n i"))
+            return turned
+
+        def gather_wd(nt, groups, at=None):
+            picked = sb("wg%d" % nt, [P, 2, JP * 256], BF16, at)
+            for group in groups:
+                first, last = group[0], group[-1] + 1
+                nc.vector.tensor_copy(
+                    picked[:, :, 256 * first : 256 * last].rearrange("p u (b s e) -> p b u e s", s=8, e=2),
+                    wd[nt][:].indirect(offsets[:, 32 * first : 32 * last]),
+                )
+            return picked
+
+        def turn_wd(nt, picked, groups, copy):
+            turned = sb("wt%d" % nt, [P, JP, P, 4], BF16)
+            for group in groups:
+                bank = next_bank([P, len(group), 2, P])
+                for at, a in enumerate(group):
+                    for u in range(2):
+                        words = picked[:, u, 256 * a : 256 * (a + 1)].bitcast(F32)
+                        nc.tensor.transpose(bank[:, at, u, :], words, ident[:])
+                words = turned[:, group[0] : group[-1] + 1].rearrange("p a n i -> p a (n i)").bitcast(F32)
+                copy(words.rearrange("p a (n u) -> p a n u", u=2), bank[:].rearrange("p a u n -> p a n u"))
+            return turned
+
+        def quantize_rows(name, turned, tiles, groups):
+            parts = {}
+            for group in groups:
+                woven = turned[:, group[0] : group[-1] + 1].rearrange("p a n i -> p (a n) i")
+                codes, scales = quantize("%s_%d" % (name, group[0]), woven, P * tiles * len(group))
+                for at, a in enumerate(group):
+                    for t in range(tiles):
+                        span = slice(P * (tiles * at + t), P * (tiles * at + t + 1))
+                        parts[t, a] = (codes[:, span], scales[:, span])
+            return [[parts[t, a] for a in range(JP)] for t in range(tiles)]
+
+        def finish(nt, wq, parts):
+            width = M // parts
+            for part in range(parts):
+                span = slice(width * part, width * (part + 1))
+                bank = next_bank([P, width])
+                for a in range(JP):
+                    nc.tensor.matmul_mx(
+                        out=bank[:],
+                        lhsT=wq[a][0].bitcast(FP8X4),
+                        lhsT_scale=wq[a][1],
+                        rhs=hq[a][0][:, span].bitcast(FP8X4),
+                        rhs_scale=hq[a][1][:, span],
+                        start=(a == 0),
+                        stop=(a == JP - 1),
+                    )
+                mag = sb("mag%d_%d" % (nt, part), [P, width], F32)
+                res = sb("res%d_%d" % (nt, part), [P, width], F32)
+                nc.scalar.activation(mag[:], bank[:], ACT.Abs)
+                nc.scalar.activation(res[:], mag[:], ACT.Sqrt)
+                nc.sync.dma_start(out[P * nt : P * (nt + 1), span], res[:])
+
+        both, apart = [[0, 1]], [[0], [1]]
+        flat = [make_h(a) for a in range(JP)]
+        pairs = cast_pair()
+        h_woven = [weave("hw%d" % a, flat[a], [nc.scalar.copy], (16 + 4 * a) * KIB) for a in range(JP)]
+        picked01 = gather_words(pairs[:].rearrange("p t e -> p (t e)").bitcast(U32), "wg01", JP)
+        picked2 = gather_wd(2, both)
+        hq = [quantize("h%d" % a, h_woven[a][:], M) for a in range(JP)]
+        turned01 = turn_pair(picked01, 28 * KIB)
+        turned2 = turn_wd(2, picked2, both, nc.scalar.copy)
+        wq01 = quantize_rows("w01", turned01, 2, both)
+        finish(0, wq01[0], 1)
+        finish(1, wq01[1], 1)
+        picked3 = gather_wd(3, apart, 28 * KIB)
+        finish(2, quantize_rows("w2", turned2, 1, both)[0], 1)
+        turned3 = turn_wd(3, picked3, apart, nc.vector.tensor_copy)
+        finish(3, quantize_rows("w3", turned3, 1, apart)[0], 2)

@@ -63,8 +63,8 @@ def tile_list_cross_modal_shortlist_kernel(
         nc.vector.memset(g_slots[:], 0.0)
         nc.scalar.activation(warm[:, 1:2], warm[:, 0:1], ACT.Sigmoid)
 
-        def load_scales(queue, win, src):
-            for q in range(4):
+        def load_scales(queue, win, src, quadrants):
+            for q in quadrants:
                 queue.dma_start(win[32 * q : 32 * q + 8, :], src.bitcast(I32)[:, 4 * q : 4 * q + 4, :])
 
         def load_words(src, kp, name, at=None):
@@ -89,40 +89,42 @@ def tile_list_cross_modal_shortlist_kernel(
             nc.sync.dma_start(win[:], wdT[P * nt : P * (nt + 1), :])
             return win
 
-        load_scales(nc.sync, sw1, tab_scales)
-        load_scales(nc.gpsimd, sw2, tab2_scales)
+        load_scales(nc.gpsimd, sw1, tab_scales, range(3))
+        load_scales(nc.gpsimd, sw2, tab2_scales, range(4))
         w1 = [load_words(tab_words, 0, "w1_0")]
-        xs = xt_scales.bitcast(I32)
-        for q in range(4):
-            nc.sync.dma_start(xts[32 * q : 32 * q + 4, :, :], xs[:, 4 * q : 4 * q + 4, :].rearrange("a r c -> r a c"))
+        load_scales(nc.sync, sw1, tab_scales, [3])
         g_rows = sb("g_rows", [JP, 512], F32)
         nc.sync.dma_start(g_rows[:], g.rearrange("(a c) -> a c", a=JP))
         w1.append(load_words(tab_words, 1, "w1_1", 0))
+        xs = xt_scales.bitcast(I32)
+        for q in range(4):
+            nc.sync.dma_start(xts[32 * q : 32 * q + 4, :, :], xs[:, 4 * q : 4 * q + 4, :].rearrange("a r c -> r a c"))
         xtw = sb("xtw", [P, KP, M // 2], I32)
         nc.sync.dma_start(xtw[:], xt_words.bitcast(I32).rearrange("a p c -> p a c"))
+        x_raw = [load_x(kp) for kp in range(KP)]
 
-        nc.scalar.copy(
-            g_slots[0:JP].rearrange("p i (q s) -> p i q s", s=8), g_rows[:].rearrange("p (q i s) -> p i q s", i=4, s=8)
-        )
-        g_bank = next_bank([P, 4, P])
-        for i in range(4):
-            nc.tensor.transpose(g_bank[:, i, :], g_slots[:, i, :], ident[:])
-        gains = sb("gains", [P, 4, JP], F32)
-        nc.scalar.copy(gains[:], g_bank[:, :, 0:JP])
-
-        def gather_scales(win, picked, plane):
+        def gather_scales(win, name, at=None):
+            picked = sb(name, [P, S], U8, at)
             nc.vector.tensor_copy(picked[:], win[:].bitcast(U8).indirect(offsets[:]))
+            return picked
+
+        def order_scales(picked, plane):
             nc.vector.tensor_copy(
                 plane[:].rearrange("p (i b h) -> p i b h", i=4, h=2),
                 picked[:].bitcast(I32).rearrange("p (b i h) -> p i b h", i=4, h=2),
             )
 
-        def gather_words(words, name, parts):
-            picked = sb(name, [P, S], U32)
+        def gather_words(words, name, parts, at=None):
+            picked = sb(name, [P, S], U32, at)
             blocks = picked[:].rearrange("p (i b s) -> p b i s", i=4, s=8)
             for part in range(parts):
                 first, last = 32 * part // parts, 32 * (part + 1) // parts
                 nc.vector.tensor_copy(blocks[:, first:last], words.indirect(offsets[:, 2 * first : 2 * last]))
+            return picked
+
+        def gather_pass(picked, words, a):
+            blocks = picked.rearrange("p i (b s) -> p b i s", s=8)
+            nc.vector.tensor_copy(blocks, words.indirect(offsets[:, 32 * a : 32 * (a + 1)]))
             return picked
 
         def weave(name, planes, copies, at=None):
@@ -145,22 +147,28 @@ def tile_list_cross_modal_shortlist_kernel(
         def cols(a, i):
             return slice(256 * i + P * a, 256 * i + P * (a + 1))
 
+        v1 = [gather_words(w1[0][:].bitcast(U32), "v1_0", 1)]
+        nc.scalar.copy(
+            g_slots[0:JP].rearrange("p i (q s) -> p i q s", s=8), g_rows[:].rearrange("p (q i s) -> p i q s", i=4, s=8)
+        )
+        g_bank = next_bank([P, 4, P])
+        for i in range(4):
+            nc.tensor.transpose(g_bank[:, i, :], g_slots[:, i, :], ident[:])
+        gains = sb("gains", [P, 4, JP], F32)
+        nc.scalar.copy(gains[:], g_bank[:, :, 0:JP])
+
         ordered1 = sb("ordered1", [P, S // 4], I32)
-        gather_scales(sw1, sb("picked1", [P, S], U8), ordered1)
+        order_scales(gather_scales(sw1, "picked1"), ordered1)
         nc.sync.dma_start(shifted1[0:100, :], ordered1[4:104, :])
         planes1 = [ordered1, shifted1]
-        x_raw = [load_x(0)]
-        w2 = [load_words(tab2_words, 0, "w2_0", 8 * KIB)]
-        x_raw.append(load_x(1))
-        w2.append(load_words(tab2_words, 1, "w2_1"))
-        pair_raw = [load_pair_piece(c) for c in range(PIECES - 1)]
-        pair_raw.append(load_pair_piece(PIECES - 1, 18 * KIB))
+        w2 = [load_words(tab2_words, kp, "w2_%d" % kp) for kp in range(KP)]
+        pair_raw = [load_pair_piece(c) for c in range(PIECES)]
         wd = {nt: load_wd(nt) for nt in (2, 3)}
 
-        v1 = [gather_words(w1[0][:].bitcast(U32), "v1_0", 1)]
         v1.append(gather_words(w1[1][:].bitcast(U32), "v1_1", JP))
         plane2 = sb("plane2", [P, S // 4], I32)
-        gather_scales(sw2, sb("picked2", [P, S], U8, 0), plane2)
+        picked_scales2 = gather_scales(sw2, "picked2", 0)
+        x_woven = [weave("xb%d" % kp, x_raw[kp], [nc.scalar.copy]) for kp in range(KP)]
 
         sig = {}
         for a in range(JP):
@@ -179,14 +187,36 @@ def tile_list_cross_modal_shortlist_kernel(
                 sig[a, i] = sb("sig%d%d" % (a, i), [P, M], F32)
                 nc.scalar.activation(sig[a, i][:], acc[:], ACT.Sigmoid)
 
-        x_woven = [weave("xb0", x_raw[0], [nc.scalar.copy])]
-        v2 = [gather_words(w2[0][:].bitcast(U32), "v2_0", 1)]
-        xq = [quantize("x0", x_woven[0][:], M, 8 * KIB)]
-        x_woven.append(weave("xb1", x_raw[1], [nc.scalar.copy, nc.vector.tensor_copy]))
-        root_warm = sb("root_warm", [P, 1], F32)
-        nc.scalar.activation(root_warm[:], x_woven[1][:, 0, 0:1], ACT.Sqrt, bias=sig[1, 3][:, 0:1], scale=0.0)
+        xq = [quantize("x0", x_woven[0][:], M)]
+        order_scales(picked_scales2, plane2)
         xq.append(quantize("x1", x_woven[1][:], M))
+        v2 = [gather_words(w2[0][:].bitcast(U32), "v2_0", JP)]
         v2.append(gather_words(w2[1][:].bitcast(U32), "v2_1", JP))
+        pairs = sb("pairs", [P, T, 2], BF16)
+        width = T // PIECES
+        for c in range(PIECES):
+            nc.scalar.copy(pairs[:, width * c : width * (c + 1), :], pair_raw[c][:].rearrange("p e t -> p t e"))
+        root_warm = sb("root_warm", [P, 1], F32)
+        nc.scalar.activation(root_warm[:], pairs[:, T - width - 1, 0:1], ACT.Sqrt, bias=sig[1, 3][:, 0:1], scale=0.0)
+
+        def weave_h(name, planes, on_pool):
+            woven = sb(name, [P, M, 4], BF16)
+            nc.gpsimd.tensor_scalar(
+                woven[:, 0:on_pool], planes[:, :, 0:on_pool].rearrange("p i m -> p m i"), 1.0, 0.0, ALU.mult, ALU.add
+            )
+            if on_pool < M:
+                nc.scalar.copy(
+                    woven[:, on_pool:M].rearrange("p (c r) i -> p c i r", r=4),
+                    planes[:, :, on_pool:M].rearrange("p i (c r) -> p c i r", r=4),
+                )
+            return woven
+
+        def turn(picked, turned, view, copy):
+            bank = next_bank([P, 4, P])
+            for i in range(4):
+                nc.tensor.transpose(bank[:, i, :], picked[:, i, :].bitcast(F32), ident[:])
+            copy(turned, bank[:].bitcast(view).rearrange("p i n -> p n i"))
+
 
         def make_h(a):
             flat = sb("hp%d" % a, [P, 4, M], BF16)
@@ -207,89 +237,60 @@ def tile_list_cross_modal_shortlist_kernel(
                 )
             return flat
 
-        def cast_pair():
-            pairs = sb("pairs", [P, T, 2], BF16)
-            width = T // PIECES
-            for c in range(PIECES):
-                nc.scalar.copy(pairs[:, width * c : width * (c + 1), :], pair_raw[c][:].rearrange("p e t -> p t e"))
-            return pairs
-
-        def turn_pair(picked, at):
-            turned = sb("turned01", [P, JP, 2 * P, 4], BF16, at)
+        def pool_rows(wq, span):
+            bank = next_bank([P, span.stop - span.start])
             for a in range(JP):
-                bank = next_bank([P, 4, P])
-                for i in range(4):
-                    nc.tensor.transpose(bank[:, i, :], picked[:, cols(a, i)].bitcast(F32), ident[:])
-                nc.scalar.copy(turned[:, a], bank[:].bitcast(BF16).rearrange("p i n -> p n i"))
-            return turned
-
-        def gather_wd(nt, groups, at=None):
-            picked = sb("wg%d" % nt, [P, 2, JP * 256], BF16, at)
-            for group in groups:
-                first, last = group[0], group[-1] + 1
-                nc.vector.tensor_copy(
-                    picked[:, :, 256 * first : 256 * last].rearrange("p u (b s e) -> p b u e s", s=8, e=2),
-                    wd[nt][:].indirect(offsets[:, 32 * first : 32 * last]),
+                nc.tensor.matmul_mx(
+                    out=bank[:],
+                    lhsT=wq[a][0].bitcast(FP8X4),
+                    lhsT_scale=wq[a][1],
+                    rhs=hq[a][0][:, span].bitcast(FP8X4),
+                    rhs_scale=hq[a][1][:, span],
+                    start=(a == 0),
+                    stop=(a == JP - 1),
                 )
-            return picked
+            return bank
 
-        def turn_wd(nt, picked, groups, copy):
-            turned = sb("wt%d" % nt, [P, JP, P, 4], BF16)
-            for group in groups:
-                bank = next_bank([P, len(group), 2, P])
-                for at, a in enumerate(group):
-                    for u in range(2):
-                        words = picked[:, u, 256 * a : 256 * (a + 1)].bitcast(F32)
-                        nc.tensor.transpose(bank[:, at, u, :], words, ident[:])
-                words = turned[:, group[0] : group[-1] + 1].rearrange("p a n i -> p a (n i)").bitcast(F32)
-                copy(words.rearrange("p a (n u) -> p a n u", u=2), bank[:].rearrange("p a u n -> p a n u"))
-            return turned
+        def finish(nt, bank, span):
+            width = span.stop - span.start
+            mag = sb("mag%d_%d" % (nt, span.start), [P, width], F32)
+            res = sb("res%d_%d" % (nt, span.start), [P, width], F32)
+            nc.scalar.activation(mag[:], bank[:], ACT.Abs)
+            nc.scalar.activation(res[:], mag[:], ACT.Sqrt)
+            nc.sync.dma_start(out[P * nt : P * (nt + 1), span], res[:])
 
-        def quantize_rows(name, turned, tiles, groups):
-            parts = {}
-            for group in groups:
-                woven = turned[:, group[0] : group[-1] + 1].rearrange("p a n i -> p (a n) i")
-                codes, scales = quantize("%s_%d" % (name, group[0]), woven, P * tiles * len(group))
-                for at, a in enumerate(group):
-                    for t in range(tiles):
-                        span = slice(P * (tiles * at + t), P * (tiles * at + t + 1))
-                        parts[t, a] = (codes[:, span], scales[:, span])
-            return [[parts[t, a] for a in range(JP)] for t in range(tiles)]
+        def parts(quantized, starts):
+            return [(quantized[0][:, c : c + P], quantized[1][:, c : c + P]) for c in starts]
 
-        def finish(nt, wq, parts):
-            width = M // parts
-            for part in range(parts):
-                span = slice(width * part, width * (part + 1))
-                bank = next_bank([P, width])
-                for a in range(JP):
-                    nc.tensor.matmul_mx(
-                        out=bank[:],
-                        lhsT=wq[a][0].bitcast(FP8X4),
-                        lhsT_scale=wq[a][1],
-                        rhs=hq[a][0][:, span].bitcast(FP8X4),
-                        rhs_scale=hq[a][1][:, span],
-                        start=(a == 0),
-                        stop=(a == JP - 1),
-                    )
-                mag = sb("mag%d_%d" % (nt, part), [P, width], F32)
-                res = sb("res%d_%d" % (nt, part), [P, width], F32)
-                nc.scalar.activation(mag[:], bank[:], ACT.Abs)
-                nc.scalar.activation(res[:], mag[:], ACT.Sqrt)
-                nc.sync.dma_start(out[P * nt : P * (nt + 1), span], res[:])
-
-        both, apart = [[0, 1]], [[0], [1]]
         flat = [make_h(a) for a in range(JP)]
-        pairs = cast_pair()
-        h_woven = [weave("hw%d" % a, flat[a], [nc.scalar.copy], (16 + 4 * a) * KIB) for a in range(JP)]
-        picked01 = gather_words(pairs[:].rearrange("p t e -> p (t e)").bitcast(U32), "wg01", JP)
-        picked2 = gather_wd(2, both)
-        hq = [quantize("h%d" % a, h_woven[a][:], M) for a in range(JP)]
-        turned01 = turn_pair(picked01, 28 * KIB)
-        turned2 = turn_wd(2, picked2, both, nc.scalar.copy)
-        wq01 = quantize_rows("w01", turned01, 2, both)
-        finish(0, wq01[0], 1)
-        finish(1, wq01[1], 1)
-        picked3 = gather_wd(3, apart, 28 * KIB)
-        finish(2, quantize_rows("w2", turned2, 1, both)[0], 1)
-        turned3 = turn_wd(3, picked3, apart, nc.vector.tensor_copy)
-        finish(3, quantize_rows("w3", turned3, 1, apart)[0], 2)
+        h_woven = [weave_h("hw0", flat[0], M), weave_h("hw1", flat[1], M // 2)]
+        pair_words = pairs[:].rearrange("p t e -> p (t e)").bitcast(U32)
+        picked01 = [gather_pass(sb("wg01_%d" % a, [P, 4, P], U32)[:], pair_words, a) for a in range(JP)]
+        hq = [quantize("h0", h_woven[0][:], M)]
+        picked2 = [gather_pass(sb("wg2_0", [P, 4, P], U32)[:], wd[2][:].bitcast(U32), 0)]
+        hq.append(quantize("h1", h_woven[1][:], M))
+        turned01 = [sb("wt01_0", [P, 2 * P, 4], BF16), sb("wt01_1", [P, 2 * P, 4], BF16, 9 * KIB)]
+        wq01 = []
+        for a in range(JP):
+            turn(picked01[a], turned01[a][:], BF16, nc.scalar.copy)
+            wq01.append(quantize("w01_%d" % a, turned01[a][:], 2 * P))
+        whole = slice(0, M)
+        halves = [slice(0, M // 2), slice(M // 2, M)]
+        turned2 = sb("wt2", [P, JP, P, 4], BF16)
+        turn(picked2[0], turned2[:, 0], F32, nc.scalar.copy)
+        sums = [pool_rows([(c[:, P * t : P * (t + 1)], s[:, P * t : P * (t + 1)]) for c, s in wq01], whole) for t in range(2)]
+        picked2.append(gather_pass(sb("wg2_1", [P, 4, P], U32, 8 * KIB)[:], wd[2][:].bitcast(U32), 1))
+        both3 = sb("wg3", [P, JP, 4, P], U32, 10 * KIB)
+        picked3 = [gather_pass(both3[:, a], wd[3][:].bitcast(U32), a) for a in range(JP)]
+        turn(picked2[1], turned2[:, 1], F32, nc.scalar.copy)
+        wq2 = quantize("w2", turned2[:].rearrange("p a n i -> p (a n) i"), P * JP)
+        sums.append(pool_rows(parts(wq2, [0, P]), whole))
+        turned3 = [sb("wt3_%d" % a, [P, P, 4], BF16) for a in range(JP)]
+        for a in range(JP):
+            turn(picked3[a], turned3[a][:], F32, nc.vector.tensor_copy)
+        wq3 = [quantize("w3_%d" % a, turned3[a][:], P) for a in range(JP)]
+        last = [pool_rows([(c[:], s[:]) for c, s in wq3], span) for span in halves]
+        for nt in range(3):
+            finish(nt, sums[nt], whole)
+        for bank, span in zip(last, halves):
+            finish(3, bank, span)

@@ -55,12 +55,18 @@ def tile_list_cross_modal_shortlist_kernel(
         warm = sb("warm", [P, 2], F32)
         ident = sb("ident", [P, P], F32)
         make_identity(nc, ident[:])
-        nc.vector.memset(sw1[:], 0)
-        nc.vector.memset(sw2[:], 0)
-        nc.vector.memset(xts[:], 0)
-        nc.vector.memset(warm[:], 0.0)
-        nc.vector.memset(shifted1[:], 0)
-        nc.vector.memset(g_slots[:], 0.0)
+
+        def clear(rows):
+            width = rows.shape[1]
+            nc.vector.memset(rows[:, 0 : width - 1], 0)
+            nc.vector.memset(rows[:, width - 1 : width], 0)
+
+        clear(sw2[:])
+        clear(sw1[:])
+        clear(warm[:])
+        clear(g_slots[:].rearrange("p i c -> p (i c)"))
+        clear(xts[:].rearrange("p a c -> p (a c)"))
+        clear(shifted1[:])
         nc.scalar.activation(warm[:, 1:2], warm[:, 0:1], ACT.Sigmoid)
 
         def load_scales(queue, win, src, quadrants):
@@ -84,18 +90,20 @@ def tile_list_cross_modal_shortlist_kernel(
             nc.sync.dma_start(raw[:], rows.rearrange("(p e) t -> p e t", e=2))
             return raw
 
-        def load_wd(nt):
-            win = sb("wd%d" % nt, [P, T], F32)
+        def load_wd(nt, at=None):
+            win = sb("wd%d" % nt, [P, T], F32, at)
             nc.sync.dma_start(win[:], wdT[P * nt : P * (nt + 1), :])
             return win
 
-        load_scales(nc.gpsimd, sw1, tab_scales, range(3))
-        load_scales(nc.gpsimd, sw2, tab2_scales, range(4))
+        load_scales(nc.gpsimd, sw2, tab2_scales, range(3))
         w1 = [load_words(tab_words, 0, "w1_0")]
-        load_scales(nc.sync, sw1, tab_scales, [3])
+        rows1 = tab_scales.bitcast(I32).rearrange("a (q r) c -> r q a c", r=4)
+        for r in range(4):
+            nc.sync.dma_start(sw1[r:P:16, :], rows1[r])
         g_rows = sb("g_rows", [JP, 512], F32)
         nc.sync.dma_start(g_rows[:], g.rearrange("(a c) -> a c", a=JP))
-        w1.append(load_words(tab_words, 1, "w1_1", 0))
+        w1.append(load_words(tab_words, 1, "w1_1"))
+        load_scales(nc.sync, sw2, tab2_scales, [3])
         xs = xt_scales.bitcast(I32)
         for q in range(4):
             nc.sync.dma_start(xts[32 * q : 32 * q + 4, :, :], xs[:, 4 * q : 4 * q + 4, :].rearrange("a r c -> r a c"))
@@ -159,16 +167,19 @@ def tile_list_cross_modal_shortlist_kernel(
 
         ordered1 = sb("ordered1", [P, S // 4], I32)
         order_scales(gather_scales(sw1, "picked1"), ordered1)
-        nc.sync.dma_start(shifted1[0:100, :], ordered1[4:104, :])
+        nc.sync.dma_start(shifted1[0 : P - 16, :], ordered1[16:P, :])
         planes1 = [ordered1, shifted1]
         w2 = [load_words(tab2_words, kp, "w2_%d" % kp) for kp in range(KP)]
-        pair_raw = [load_pair_piece(c) for c in range(PIECES)]
-        wd = {nt: load_wd(nt) for nt in (2, 3)}
+        pair_raw = [load_pair_piece(c) for c in range(PIECES - 1)]
+        pair_raw.append(load_pair_piece(PIECES - 1, 10 * KIB))
+        wd = {2: load_wd(2)}
 
         v1.append(gather_words(w1[1][:].bitcast(U32), "v1_1", JP))
         plane2 = sb("plane2", [P, S // 4], I32)
-        picked_scales2 = gather_scales(sw2, "picked2", 0)
-        x_woven = [weave("xb%d" % kp, x_raw[kp], [nc.scalar.copy]) for kp in range(KP)]
+        order_scales(gather_scales(sw2, "picked2"), plane2)
+        x_woven = [weave("xb0", x_raw[0], [nc.scalar.copy], None)]
+        x_woven.append(weave("xb1", x_raw[1], [nc.scalar.copy, nc.vector.tensor_copy]))
+        xq = [quantize("x%d" % kp, x_woven[kp][:], M) for kp in range(KP)]
 
         sig = {}
         for a in range(JP):
@@ -187,29 +198,12 @@ def tile_list_cross_modal_shortlist_kernel(
                 sig[a, i] = sb("sig%d%d" % (a, i), [P, M], F32)
                 nc.scalar.activation(sig[a, i][:], acc[:], ACT.Sigmoid)
 
-        xq = [quantize("x0", x_woven[0][:], M)]
-        order_scales(picked_scales2, plane2)
-        xq.append(quantize("x1", x_woven[1][:], M))
         v2 = [gather_words(w2[0][:].bitcast(U32), "v2_0", JP)]
         v2.append(gather_words(w2[1][:].bitcast(U32), "v2_1", JP))
         pairs = sb("pairs", [P, T, 2], BF16)
         width = T // PIECES
         for c in range(PIECES):
             nc.scalar.copy(pairs[:, width * c : width * (c + 1), :], pair_raw[c][:].rearrange("p e t -> p t e"))
-        root_warm = sb("root_warm", [P, 1], F32)
-        nc.scalar.activation(root_warm[:], pairs[:, T - width - 1, 0:1], ACT.Sqrt, bias=sig[1, 3][:, 0:1], scale=0.0)
-
-        def weave_h(name, planes, on_pool):
-            woven = sb(name, [P, M, 4], BF16)
-            nc.gpsimd.tensor_scalar(
-                woven[:, 0:on_pool], planes[:, :, 0:on_pool].rearrange("p i m -> p m i"), 1.0, 0.0, ALU.mult, ALU.add
-            )
-            if on_pool < M:
-                nc.scalar.copy(
-                    woven[:, on_pool:M].rearrange("p (c r) i -> p c i r", r=4),
-                    planes[:, :, on_pool:M].rearrange("p i (c r) -> p c i r", r=4),
-                )
-            return woven
 
         def turn(picked, turned, view, copy):
             bank = next_bank([P, 4, P])
@@ -219,7 +213,7 @@ def tile_list_cross_modal_shortlist_kernel(
 
 
         def make_h(a):
-            flat = sb("hp%d" % a, [P, 4, M], BF16)
+            flat = sb("hp%d" % a, [P, 4, M], BF16, 0 if a == 0 else None)
             for i in range(4):
                 acc = next_bank([P, M])
                 for kp in range(KP):
@@ -263,32 +257,33 @@ def tile_list_cross_modal_shortlist_kernel(
             return [(quantized[0][:, c : c + P], quantized[1][:, c : c + P]) for c in starts]
 
         flat = [make_h(a) for a in range(JP)]
-        h_woven = [weave_h("hw0", flat[0], M), weave_h("hw1", flat[1], M // 2)]
         pair_words = pairs[:].rearrange("p t e -> p (t e)").bitcast(U32)
         picked01 = [gather_pass(sb("wg01_%d" % a, [P, 4, P], U32)[:], pair_words, a) for a in range(JP)]
-        hq = [quantize("h0", h_woven[0][:], M)]
-        picked2 = [gather_pass(sb("wg2_0", [P, 4, P], U32)[:], wd[2][:].bitcast(U32), 0)]
-        hq.append(quantize("h1", h_woven[1][:], M))
-        turned01 = [sb("wt01_0", [P, 2 * P, 4], BF16), sb("wt01_1", [P, 2 * P, 4], BF16, 9 * KIB)]
+        h_woven = [weave("hw0", flat[0], [nc.scalar.copy], 8 * KIB), weave("hw1", flat[1], [nc.scalar.copy], 12 * KIB)]
+        wd[3] = load_wd(3, 0)
+        picked2 = [gather_pass(sb("wg2_%d" % a, [P, 4, P], U32)[:], wd[2][:].bitcast(U32), a) for a in range(JP)]
+        hq = [quantize("h%d" % a, h_woven[a][:], M) for a in range(JP)]
         wq01 = []
         for a in range(JP):
-            turn(picked01[a], turned01[a][:], BF16, nc.scalar.copy)
-            wq01.append(quantize("w01_%d" % a, turned01[a][:], 2 * P))
+            turned = sb("wt01_%d" % a, [P, 2 * P, 4], BF16)
+            turn(picked01[a], turned[:], BF16, nc.scalar.copy)
+            wq01.append(quantize("w01_%d" % a, turned[:], 2 * P))
         whole = slice(0, M)
         halves = [slice(0, M // 2), slice(M // 2, M)]
-        turned2 = sb("wt2", [P, JP, P, 4], BF16)
-        turn(picked2[0], turned2[:, 0], F32, nc.scalar.copy)
         sums = [pool_rows([(c[:, P * t : P * (t + 1)], s[:, P * t : P * (t + 1)]) for c, s in wq01], whole) for t in range(2)]
-        picked2.append(gather_pass(sb("wg2_1", [P, 4, P], U32, 8 * KIB)[:], wd[2][:].bitcast(U32), 1))
-        both3 = sb("wg3", [P, JP, 4, P], U32, 10 * KIB)
-        picked3 = [gather_pass(both3[:, a], wd[3][:].bitcast(U32), a) for a in range(JP)]
-        turn(picked2[1], turned2[:, 1], F32, nc.scalar.copy)
-        wq2 = quantize("w2", turned2[:].rearrange("p a n i -> p (a n) i"), P * JP)
-        sums.append(pool_rows(parts(wq2, [0, P]), whole))
-        turned3 = [sb("wt3_%d" % a, [P, P, 4], BF16) for a in range(JP)]
+        turned2 = sb("wt2", [P, JP, P, 4], BF16)
         for a in range(JP):
-            turn(picked3[a], turned3[a][:], F32, nc.vector.tensor_copy)
-        wq3 = [quantize("w3_%d" % a, turned3[a][:], P) for a in range(JP)]
+            turn(picked2[a], turned2[:, a], F32, nc.scalar.copy)
+        root_warm = sb("root_warm", [P, 1], F32)
+        nc.scalar.activation(root_warm[:], turned2[:, 0, 0, 0:1], ACT.Sqrt, bias=sig[1, 3][:, 0:1], scale=0.0)
+        picked3 = [gather_pass(sb("wg3_%d" % a, [P, 4, P], U32)[:], wd[3][:].bitcast(U32), a) for a in range(JP)]
+        wq2 = quantize("w2", turned2[:].rearrange("p a n i -> p (a n) i"), P * JP)
+        turned3 = [sb("wt3_%d" % a, [P, P, 4], BF16) for a in range(JP)]
+        wq3 = []
+        for a in range(JP):
+            turn(picked3[a], turned3[a][:], F32, [nc.vector.tensor_copy, nc.vector.tensor_copy][a])
+            wq3.append(quantize("w3_%d" % a, turned3[a][:], P))
+        sums.append(pool_rows(parts(wq2, [0, P]), whole))
         last = [pool_rows([(c[:], s[:]) for c, s in wq3], span) for span in halves]
         for nt in range(3):
             finish(nt, sums[nt], whole)

@@ -178,7 +178,7 @@ def tile_list_cross_modal_shortlist_kernel(
         plane2 = sb("plane2", [P, S // 4], I32)
         order_scales(gather_scales(sw2, "picked2"), plane2)
         x_woven = [weave("xb0", x_raw[0], [nc.scalar.copy], None)]
-        x_woven.append(weave("xb1", x_raw[1], [nc.scalar.copy, nc.vector.tensor_copy]))
+        x_woven.append(weave("xb1", x_raw[1], [nc.scalar.copy]))
         xq = [quantize("x%d" % kp, x_woven[kp][:], M) for kp in range(KP)]
 
         sig = {}
@@ -278,13 +278,12 @@ def tile_list_cross_modal_shortlist_kernel(
         nc.scalar.activation(root_warm[:], turned2[:, 0, 0, 0:1], ACT.Sqrt, bias=sig[1, 3][:, 0:1], scale=0.0)
         picked3 = [gather_pass(sb("wg3_%d" % a, [P, 4, P], U32)[:], wd[3][:].bitcast(U32), a) for a in range(JP)]
         wq2 = quantize("w2", turned2[:].rearrange("p a n i -> p (a n) i"), P * JP)
-        turned3 = [sb("wt3_%d" % a, [P, P, 4], BF16) for a in range(JP)]
-        wq3 = []
+        turned3 = sb("wt3", [P, JP, P, 4], BF16)
         for a in range(JP):
-            turn(picked3[a], turned3[a][:], F32, [nc.vector.tensor_copy, nc.vector.tensor_copy][a])
-            wq3.append(quantize("w3_%d" % a, turned3[a][:], P))
+            turn(picked3[a], turned3[:, a], F32, [nc.vector.tensor_copy, nc.vector.tensor_copy][a])
+        wq3 = parts(quantize("w3", turned3[:].rearrange("p a n i -> p (a n) i"), P * JP), [0, P])
         sums.append(pool_rows(parts(wq2, [0, P]), whole))
-        last = [pool_rows([(c[:], s[:]) for c, s in wq3], span) for span in halves]
+        last = [pool_rows(wq3, span) for span in halves]
         for nt in range(3):
             finish(nt, sums[nt], whole)
         for bank, span in zip(last, halves):

@@ -135,6 +135,13 @@ def tile_list_cross_modal_shortlist_kernel(
             nc.vector.tensor_copy(blocks, words.indirect(offsets[:, 32 * a : 32 * (a + 1)]))
             return picked
 
+        def gather_rounded(name, rows, a):
+            picked = sb(name, [P, 2, 2 * P], BF16)
+            nc.vector.tensor_copy(
+                picked[:].rearrange("p u (b s e) -> p b u e s", s=8, e=2), rows.indirect(offsets[:, 32 * a : 32 * (a + 1)])
+            )
+            return picked
+
         def weave(name, planes, copies, at=None):
             woven = sb(name, [P, M, 4], BF16, at)
             width = M // len(copies)
@@ -212,6 +219,13 @@ def tile_list_cross_modal_shortlist_kernel(
             copy(turned, bank[:].bitcast(view).rearrange("p i n -> p n i"))
 
 
+        def turn_words(picked, turned, copy):
+            bank = next_bank([P, 2, P])
+            for u in range(2):
+                nc.tensor.transpose(bank[:, u, :], picked[:, u, :].bitcast(F32), ident[:])
+            words = turned.rearrange("p n i -> p (n i)").bitcast(F32)
+            copy(words.rearrange("p (n u) -> p n u", u=2), bank[:].rearrange("p u n -> p n u"))
+
         def make_h(a):
             flat = sb("hp%d" % a, [P, 4, M], BF16, 0 if a == 0 else None)
             for i in range(4):
@@ -261,7 +275,7 @@ def tile_list_cross_modal_shortlist_kernel(
         picked01 = [gather_pass(sb("wg01_%d" % a, [P, 4, P], U32)[:], pair_words, a) for a in range(JP)]
         h_woven = [weave("hw0", flat[0], [nc.scalar.copy], 8 * KIB), weave("hw1", flat[1], [nc.scalar.copy], 12 * KIB)]
         wd[3] = load_wd(3, 0)
-        picked2 = [gather_pass(sb("wg2_%d" % a, [P, 4, P], U32)[:], wd[2][:].bitcast(U32), a) for a in range(JP)]
+        picked2 = [gather_rounded("wg2_%d" % a, wd[2][:], a) for a in range(JP)]
         hq = [quantize("h%d" % a, h_woven[a][:], M) for a in range(JP)]
         wq01 = []
         for a in range(JP):
@@ -273,14 +287,14 @@ def tile_list_cross_modal_shortlist_kernel(
         sums = [pool_rows([(c[:, P * t : P * (t + 1)], s[:, P * t : P * (t + 1)]) for c, s in wq01], whole) for t in range(2)]
         turned2 = sb("wt2", [P, JP, P, 4], BF16)
         for a in range(JP):
-            turn(picked2[a], turned2[:, a], F32, nc.scalar.copy)
+            turn_words(picked2[a], turned2[:, a], nc.scalar.copy)
         root_warm = sb("root_warm", [P, 1], F32)
         nc.scalar.activation(root_warm[:], turned2[:, 0, 0, 0:1], ACT.Sqrt, bias=sig[1, 3][:, 0:1], scale=0.0)
-        picked3 = [gather_pass(sb("wg3_%d" % a, [P, 4, P], U32)[:], wd[3][:].bitcast(U32), a) for a in range(JP)]
+        picked3 = [gather_rounded("wg3_%d" % a, wd[3][:], a) for a in range(JP)]
         wq2 = quantize("w2", turned2[:].rearrange("p a n i -> p (a n) i"), P * JP)
         turned3 = sb("wt3", [P, JP, P, 4], BF16)
         for a in range(JP):
-            turn(picked3[a], turned3[:, a], F32, [nc.vector.tensor_copy, nc.vector.tensor_copy][a])
+            turn_words(picked3[a], turned3[:, a], [nc.vector.tensor_copy, nc.vector.tensor_copy][a])
         wq3 = parts(quantize("w3", turned3[:].rearrange("p a n i -> p (a n) i"), P * JP), [0, P])
         sums.append(pool_rows(parts(wq2, [0, P]), whole))
         last = [pool_rows(wq3, span) for span in halves]

@@ -51,7 +51,7 @@ def tile_list_cross_modal_shortlist_kernel(
         sw2 = sb("sw2", [P, T // 4], I32)
         xts = sb("xts", [P, KP, M // 4], I32)
         shifted1 = sb("shifted1", [P, S // 4], I32)
-        g_slots = sb("g_slots", [P, 4, P], F32)
+        g_slots = sb("g_slots", [P, 4, P], F32, 16 * KIB)
         warm = sb("warm", [P, 2], F32)
         ident = sb("ident", [P, P], F32)
         make_identity(nc, ident[:])
@@ -71,7 +71,7 @@ def tile_list_cross_modal_shortlist_kernel(
 
         def load_scales(queue, win, src, quadrants):
             for q in quadrants:
-                queue.dma_start(win[32 * q : 32 * q + 8, :], src.bitcast(I32)[:, 4 * q : 4 * q + 4, :])
+                queue.dma_start(win[32 * q + 8 : 32 * q + 16, :], src.bitcast(I32)[:, 4 * q : 4 * q + 4, :])
 
         def load_words(src, kp, name, at=None):
             win = sb(name, [P, T], I32, at)
@@ -104,12 +104,13 @@ def tile_list_cross_modal_shortlist_kernel(
         nc.sync.dma_start(g_rows[:], g.rearrange("(a c) -> a c", a=JP))
         w1.append(load_words(tab_words, 1, "w1_1"))
         load_scales(nc.sync, sw2, tab2_scales, [3])
+        x_raw = [load_x(0)]
         xs = xt_scales.bitcast(I32)
         for q in range(4):
             nc.sync.dma_start(xts[32 * q : 32 * q + 4, :, :], xs[:, 4 * q : 4 * q + 4, :].rearrange("a r c -> r a c"))
         xtw = sb("xtw", [P, KP, M // 2], I32)
         nc.sync.dma_start(xtw[:], xt_words.bitcast(I32).rearrange("a p c -> p a c"))
-        x_raw = [load_x(kp) for kp in range(KP)]
+        x_raw.append(load_x(1))
 
         def gather_scales(win, name, at=None):
             picked = sb(name, [P, S], U8, at)
@@ -166,19 +167,13 @@ def tile_list_cross_modal_shortlist_kernel(
         nc.scalar.copy(
             g_slots[0:JP].rearrange("p i (q s) -> p i q s", s=8), g_rows[:].rearrange("p (q i s) -> p i q s", i=4, s=8)
         )
-        g_bank = next_bank([P, 4, P])
-        for i in range(4):
-            nc.tensor.transpose(g_bank[:, i, :], g_slots[:, i, :], ident[:])
-        gains = sb("gains", [P, 4, JP], F32)
-        nc.scalar.copy(gains[:], g_bank[:, :, 0:JP])
 
         ordered1 = sb("ordered1", [P, S // 4], I32)
         order_scales(gather_scales(sw1, "picked1"), ordered1)
         nc.sync.dma_start(shifted1[0 : P - 16, :], ordered1[16:P, :])
         planes1 = [ordered1, shifted1]
-        w2 = [load_words(tab2_words, kp, "w2_%d" % kp) for kp in range(KP)]
-        pair_raw = [load_pair_piece(c) for c in range(PIECES - 1)]
-        pair_raw.append(load_pair_piece(PIECES - 1, 10 * KIB))
+        w2 = [load_words(tab2_words, 0, "w2_0"), load_words(tab2_words, 1, "w2_1")]
+        pair_raw = [load_pair_piece(c, 10 * KIB if c == PIECES - 2 else None) for c in range(PIECES)]
         wd = {2: load_wd(2)}
 
         v1.append(gather_words(w1[1][:].bitcast(U32), "v1_1", JP))
@@ -186,7 +181,7 @@ def tile_list_cross_modal_shortlist_kernel(
         order_scales(gather_scales(sw2, "picked2"), plane2)
         x_woven = [weave("xb0", x_raw[0], [nc.scalar.copy], None)]
         x_woven.append(weave("xb1", x_raw[1], [nc.scalar.copy]))
-        xq = [quantize("x%d" % kp, x_woven[kp][:], M) for kp in range(KP)]
+        xq = [quantize("x0", x_woven[0][:], M)]
 
         sig = {}
         for a in range(JP):
@@ -205,7 +200,13 @@ def tile_list_cross_modal_shortlist_kernel(
                 sig[a, i] = sb("sig%d%d" % (a, i), [P, M], F32)
                 nc.scalar.activation(sig[a, i][:], acc[:], ACT.Sigmoid)
 
+        g_bank = next_bank([P, 4, P])
+        for i in range(4):
+            nc.tensor.transpose(g_bank[:, i, :], g_slots[:, i, :], ident[:])
+        gains = sb("gains", [P, 4, JP], F32)
+        nc.scalar.copy(gains[:], g_bank[:, :, 0:JP])
         v2 = [gather_words(w2[0][:].bitcast(U32), "v2_0", JP)]
+        xq.append(quantize("x1", x_woven[1][:], M, 16 * KIB))
         v2.append(gather_words(w2[1][:].bitcast(U32), "v2_1", JP))
         pairs = sb("pairs", [P, T, 2], BF16)
         width = T // PIECES
@@ -234,7 +235,7 @@ def tile_list_cross_modal_shortlist_kernel(
                     nc.tensor.matmul_mx(
                         out=acc[:],
                         lhsT=v2[kp][:, cols(a, i)].bitcast(FP8X4),
-                        lhsT_scale=plane2[4 * kp : P, :].bitcast(U8)[:, cols(a, i)],
+                        lhsT_scale=plane2[8 + 4 * kp : P, :].bitcast(U8)[:, cols(a, i)],
                         rhs=xq[kp][0][:].bitcast(FP8X4),
                         rhs_scale=xq[kp][1][:],
                         start=(kp == 0),
@@ -259,11 +260,13 @@ def tile_list_cross_modal_shortlist_kernel(
                 )
             return bank
 
-        def finish(nt, bank, span):
-            width = span.stop - span.start
-            mag = sb("mag%d_%d" % (nt, span.start), [P, width], F32)
-            res = sb("res%d_%d" % (nt, span.start), [P, width], F32)
+        def magnitude(nt, bank, span):
+            mag = sb("mag%d_%d" % (nt, span.start), [P, span.stop - span.start], F32)
             nc.scalar.activation(mag[:], bank[:], ACT.Abs)
+            return nt, mag, span
+
+        def store_root(nt, mag, span):
+            res = sb("res%d_%d" % (nt, span.start), [P, span.stop - span.start], F32)
             nc.scalar.activation(res[:], mag[:], ACT.Sqrt)
             nc.sync.dma_start(out[P * nt : P * (nt + 1), span], res[:])
 
@@ -290,15 +293,22 @@ def tile_list_cross_modal_shortlist_kernel(
             turn_words(picked2[a], turned2[:, a], nc.scalar.copy)
         root_warm = sb("root_warm", [P, 1], F32)
         nc.scalar.activation(root_warm[:], turned2[:, 0, 0, 0:1], ACT.Sqrt, bias=sig[1, 3][:, 0:1], scale=0.0)
-        picked3 = [gather_rounded("wg3_%d" % a, wd[3][:], a) for a in range(JP)]
+        picked3 = [gather_rounded("wg3_0", wd[3][:], 0)]
         wq2 = quantize("w2", turned2[:].rearrange("p a n i -> p (a n) i"), P * JP)
-        turned3 = sb("wt3", [P, JP, P, 4], BF16)
+        picked3.append(gather_rounded("wg3_1", wd[3][:], 1))
+        wq3 = []
         for a in range(JP):
-            turn_words(picked3[a], turned3[:, a], [nc.vector.tensor_copy, nc.vector.tensor_copy][a])
-        wq3 = parts(quantize("w3", turned3[:].rearrange("p a n i -> p (a n) i"), P * JP), [0, P])
-        sums.append(pool_rows(parts(wq2, [0, P]), whole))
+            turned = sb("wt3_%d" % a, [P, P, 4], BF16)
+            turn_words(picked3[a], turned[:], nc.vector.tensor_copy)
+            codes, scales = quantize("w3_%d" % a, turned[:], P)
+            wq3.append((codes[:], scales[:]))
+            if a == 0:
+                sums.append(pool_rows(parts(wq2, [0, P]), whole))
         last = [pool_rows(wq3, span) for span in halves]
-        for nt in range(3):
-            finish(nt, sums[nt], whole)
-        for bank, span in zip(last, halves):
-            finish(3, bank, span)
+        mags = [magnitude(nt, sums[nt], whole) for nt in range(2)]
+        store_root(*mags[0])
+        mags.append(magnitude(2, sums[2], whole))
+        store_root(*mags[1])
+        store_root(*mags[2])
+        for mag in [magnitude(3, bank, span) for bank, span in zip(last, halves)]:
+            store_root(*mag)

@@ -95,19 +95,18 @@ def tile_list_cross_modal_shortlist_kernel(
             nc.sync.dma_start(win[:], wdT[P * nt : P * (nt + 1), :])
             return win
 
-        load_scales(nc.gpsimd, sw2, tab2_scales, range(3))
+        load_scales(nc.gpsimd, sw2, tab2_scales, range(4))
+        xs = xt_scales.bitcast(I32)
+        for q in range(4):
+            nc.gpsimd.dma_start(xts[32 * q : 32 * q + 4, :, :], xs[:, 4 * q : 4 * q + 4, :].rearrange("a r c -> r a c"))
+        g_rows = sb("g_rows", [JP, 512], F32)
+        nc.gpsimd.dma_start(g_rows[:], g.rearrange("(a c) -> a c", a=JP))
         w1 = [load_words(tab_words, 0, "w1_0")]
         rows1 = tab_scales.bitcast(I32).rearrange("a (q r) c -> r q a c", r=4)
         for r in range(4):
             nc.sync.dma_start(sw1[r:P:16, :], rows1[r])
-        g_rows = sb("g_rows", [JP, 512], F32)
-        nc.sync.dma_start(g_rows[:], g.rearrange("(a c) -> a c", a=JP))
-        w1.append(load_words(tab_words, 1, "w1_1"))
-        load_scales(nc.sync, sw2, tab2_scales, [3])
+        w1.append(load_words(tab_words, 1, "w1_1", 18 * KIB))
         x_raw = [load_x(0)]
-        xs = xt_scales.bitcast(I32)
-        for q in range(4):
-            nc.sync.dma_start(xts[32 * q : 32 * q + 4, :, :], xs[:, 4 * q : 4 * q + 4, :].rearrange("a r c -> r a c"))
         xtw = sb("xtw", [P, KP, M // 2], I32)
         nc.sync.dma_start(xtw[:], xt_words.bitcast(I32).rearrange("a p c -> p a c"))
         x_raw.append(load_x(1))
@@ -178,7 +177,7 @@ def tile_list_cross_modal_shortlist_kernel(
 
         v1.append(gather_words(w1[1][:].bitcast(U32), "v1_1", JP))
         plane2 = sb("plane2", [P, S // 4], I32)
-        order_scales(gather_scales(sw2, "picked2"), plane2)
+        order_scales(gather_scales(sw2, "picked2", 18 * KIB), plane2)
         x_woven = [weave("xb0", x_raw[0], [nc.scalar.copy], None)]
         x_woven.append(weave("xb1", x_raw[1], [nc.scalar.copy]))
         xq = [quantize("x0", x_woven[0][:], M)]

@@ -209,8 +209,6 @@ def tile_list_cross_modal_shortlist_kernel(
         v2.append(gather_words(w2[1][:].bitcast(U32), "v2_1", JP))
         pairs = sb("pairs", [P, T, 2], BF16)
         width = T // PIECES
-        for c in range(PIECES):
-            nc.scalar.copy(pairs[:, width * c : width * (c + 1), :], pair_raw[c][:].rearrange("p e t -> p t e"))
 
         def turn(picked, turned, view, copy):
             bank = next_bank([P, 4, P])
@@ -240,9 +238,13 @@ def tile_list_cross_modal_shortlist_kernel(
                         start=(kp == 0),
                         stop=(kp == KP - 1),
                     )
-                nc.vector.scalar_tensor_tensor(
-                    flat[:, i, :], acc[:], gains[:, i, a : a + 1], sig[a, i][:], ALU.mult, ALU.mult
-                )
+                gain = gains[:, i, a : a + 1]
+                if (a, i) == (0, 0):
+                    scaled = sb("scaled", [P, M], F32)
+                    nc.scalar.activation(scaled[:], acc[:], ACT.Copy, scale=gain)
+                    nc.gpsimd.tensor_tensor(flat[:, i, :], scaled[:], sig[a, i][:], ALU.mult)
+                else:
+                    nc.vector.scalar_tensor_tensor(flat[:, i, :], acc[:], gain, sig[a, i][:], ALU.mult, ALU.mult)
             return flat
 
         def pool_rows(wq, span):
@@ -273,6 +275,8 @@ def tile_list_cross_modal_shortlist_kernel(
             return [(quantized[0][:, c : c + P], quantized[1][:, c : c + P]) for c in starts]
 
         flat = [make_h(a) for a in range(JP)]
+        for c in range(PIECES):
+            nc.scalar.copy(pairs[:, width * c : width * (c + 1), :], pair_raw[c][:].rearrange("p e t -> p t e"))
         pair_words = pairs[:].rearrange("p t e -> p (t e)").bitcast(U32)
         picked01 = [gather_pass(sb("wg01_%d" % a, [P, 4, P], U32)[:], pair_words, a) for a in range(JP)]
         h_woven = [weave("hw0", flat[0], [nc.scalar.copy], 8 * KIB), weave("hw1", flat[1], [nc.scalar.copy], 12 * KIB)]

@@ -48,6 +48,7 @@ def tile_list_cross_modal_shortlist_kernel(
         nc.sync.dma_start(offsets[:], offs)
 
         sw1 = sb("sw1", [P, T // 4], I32)
+        nc.gpsimd.memset(sw1[:], 0)
         sw2 = sb("sw2", [P, T // 4], I32)
         xts = sb("xts", [P, KP, M // 4], I32)
         shifted1 = sb("shifted1", [P, S // 4], I32)
@@ -62,10 +63,9 @@ def tile_list_cross_modal_shortlist_kernel(
             nc.vector.memset(rows[:, width - 1 : width], 0)
 
         clear(sw2[:])
-        clear(sw1[:])
         clear(warm[:])
-        clear(g_slots[:].rearrange("p i c -> p (i c)"))
         clear(xts[:].rearrange("p a c -> p (a c)"))
+        clear(g_slots[:].rearrange("p i c -> p (i c)"))
         clear(shifted1[:])
         nc.scalar.activation(warm[:, 1:2], warm[:, 0:1], ACT.Sigmoid)
 
@@ -100,16 +100,14 @@ def tile_list_cross_modal_shortlist_kernel(
         for q in range(4):
             nc.gpsimd.dma_start(xts[32 * q : 32 * q + 4, :, :], xs[:, 4 * q : 4 * q + 4, :].rearrange("a r c -> r a c"))
         g_rows = sb("g_rows", [JP, 512], F32)
-        nc.gpsimd.dma_start(g_rows[:], g.rearrange("(a c) -> a c", a=JP))
-        w1 = [load_words(tab_words, 0, "w1_0")]
+        nc.sync.dma_start(g_rows[:], g.rearrange("(a c) -> a c", a=JP))
         rows1 = tab_scales.bitcast(I32).rearrange("a (q r) c -> r q a c", r=4)
         for r in range(4):
             nc.sync.dma_start(sw1[r:P:16, :], rows1[r])
-        w1.append(load_words(tab_words, 1, "w1_1", 18 * KIB))
-        x_raw = [load_x(0)]
+        w1 = [load_words(tab_words, 0, "w1_0"), load_words(tab_words, 1, "w1_1", 18 * KIB)]
         xtw = sb("xtw", [P, KP, M // 2], I32)
         nc.sync.dma_start(xtw[:], xt_words.bitcast(I32).rearrange("a p c -> p a c"))
-        x_raw.append(load_x(1))
+        x_raw = [load_x(kp) for kp in range(KP)]
 
         def gather_scales(win, name, at=None):
             picked = sb(name, [P, S], U8, at)
@@ -162,50 +160,57 @@ def tile_list_cross_modal_shortlist_kernel(
         def cols(a, i):
             return slice(256 * i + P * a, 256 * i + P * (a + 1))
 
-        v1 = [gather_words(w1[0][:].bitcast(U32), "v1_0", 1)]
-        nc.scalar.copy(
-            g_slots[0:JP].rearrange("p i (q s) -> p i q s", s=8), g_rows[:].rearrange("p (q i s) -> p i q s", i=4, s=8)
-        )
 
         ordered1 = sb("ordered1", [P, S // 4], I32)
         order_scales(gather_scales(sw1, "picked1"), ordered1)
         nc.sync.dma_start(shifted1[0 : P - 16, :], ordered1[16:P, :])
         planes1 = [ordered1, shifted1]
         w2 = [load_words(tab2_words, 0, "w2_0"), load_words(tab2_words, 1, "w2_1")]
-        pair_raw = [load_pair_piece(c, 10 * KIB if c == PIECES - 2 else None) for c in range(PIECES)]
+        pair_raw = [load_pair_piece(c, {0: 28 * KIB, PIECES - 2: 10 * KIB}.get(c)) for c in range(PIECES)]
         wd = {2: load_wd(2)}
 
+        v1 = [gather_words(w1[0][:].bitcast(U32), "v1_0", 1)]
         v1.append(gather_words(w1[1][:].bitcast(U32), "v1_1", JP))
         plane2 = sb("plane2", [P, S // 4], I32)
         order_scales(gather_scales(sw2, "picked2", 18 * KIB), plane2)
         x_woven = [weave("xb0", x_raw[0], [nc.scalar.copy], None)]
-        x_woven.append(weave("xb1", x_raw[1], [nc.scalar.copy]))
+        x_woven.append(sb("xb1", [P, M, 4], BF16))
+        cut = M - 192
+        nc.scalar.copy(
+            x_woven[1][:, 0:cut, :].rearrange("p (c r) i -> p c i r", r=4),
+            x_raw[1][:, :, 0:cut].rearrange("p i (c r) -> p c i r", r=4),
+        )
+        nc.vector.tensor_copy(x_woven[1][:, cut:M, :], x_raw[1][:, :, cut:M].rearrange("p i m -> p m i"))
         xq = [quantize("x0", x_woven[0][:], M)]
 
         sig = {}
         for a in range(JP):
             for i in range(4):
                 acc = next_bank([P, M])
-                for kp in range(KP):
+                passes = [1, 0] if a else [0, 1]
+                for kp in passes:
                     nc.tensor.matmul_mx(
                         out=acc[:],
                         lhsT=v1[kp][:, cols(a, i)].bitcast(FP8X4),
                         lhsT_scale=planes1[kp][:].bitcast(U8)[:, cols(a, i)],
                         rhs=xtw[:, kp, :].bitcast(U8).bitcast(FP4X4),
                         rhs_scale=xts[:, kp, :].bitcast(U8),
-                        start=(kp == 0),
-                        stop=(kp == KP - 1),
+                        start=(kp == passes[0]),
+                        stop=(kp == passes[-1]),
                     )
                 sig[a, i] = sb("sig%d%d" % (a, i), [P, M], F32)
                 nc.scalar.activation(sig[a, i][:], acc[:], ACT.Sigmoid)
 
+        nc.scalar.copy(
+            g_slots[0:JP].rearrange("p i (q s) -> p i q s", s=8), g_rows[:].rearrange("p (q i s) -> p i q s", i=4, s=8)
+        )
         g_bank = next_bank([P, 4, P])
         for i in range(4):
             nc.tensor.transpose(g_bank[:, i, :], g_slots[:, i, :], ident[:])
         gains = sb("gains", [P, 4, JP], F32)
         nc.scalar.copy(gains[:], g_bank[:, :, 0:JP])
+        xq.append(quantize("x1", x_woven[1][:], M))
         v2 = [gather_words(w2[0][:].bitcast(U32), "v2_0", JP)]
-        xq.append(quantize("x1", x_woven[1][:], M, 16 * KIB))
         v2.append(gather_words(w2[1][:].bitcast(U32), "v2_1", JP))
         pairs = sb("pairs", [P, T, 2], BF16)
         width = T // PIECES
@@ -228,19 +233,20 @@ def tile_list_cross_modal_shortlist_kernel(
             flat = sb("hp%d" % a, [P, 4, M], BF16, 0 if a == 0 else None)
             for i in range(4):
                 acc = next_bank([P, M])
-                for kp in range(KP):
+                passes = [1, 0] if a else [0, 1]
+                for kp in passes:
                     nc.tensor.matmul_mx(
                         out=acc[:],
                         lhsT=v2[kp][:, cols(a, i)].bitcast(FP8X4),
                         lhsT_scale=plane2[8 + 4 * kp : P, :].bitcast(U8)[:, cols(a, i)],
                         rhs=xq[kp][0][:].bitcast(FP8X4),
                         rhs_scale=xq[kp][1][:],
-                        start=(kp == 0),
-                        stop=(kp == KP - 1),
+                        start=(kp == passes[0]),
+                        stop=(kp == passes[-1]),
                     )
                 gain = gains[:, i, a : a + 1]
                 if (a, i) == (0, 0):
-                    scaled = sb("scaled", [P, M], F32)
+                    scaled = sb("scaled", [P, M], F32, 28 * KIB)
                     nc.scalar.activation(scaled[:], acc[:], ACT.Copy, scale=gain)
                     nc.gpsimd.tensor_tensor(flat[:, i, :], scaled[:], sig[a, i][:], ALU.mult)
                 else:

@@ -79,7 +79,7 @@ def tile_list_cross_modal_shortlist_kernel(
             return win
 
         def load_x(kp):
-            raw = sb("x%d" % kp, [P, 4, M], F32)
+            raw = sb("x%d" % kp, [P, 4, M], F32, None if kp else 32 * KIB)
             nc.sync.dma_start(raw[:], x[512 * kp : 512 * (kp + 1), :].rearrange("(p i) m -> p i m", i=4))
             return raw
 
@@ -171,17 +171,19 @@ def tile_list_cross_modal_shortlist_kernel(
 
         v1 = [gather_words(w1[0][:].bitcast(U32), "v1_0", 1)]
         v1.append(gather_words(w1[1][:].bitcast(U32), "v1_1", JP))
-        plane2 = sb("plane2", [P, S // 4], I32)
-        order_scales(gather_scales(sw2, "picked2", 18 * KIB), plane2)
+        picked_scales2 = gather_scales(sw2, "picked2", 18 * KIB)
         x_woven = [weave("xb0", x_raw[0], [nc.scalar.copy], None)]
         x_woven.append(sb("xb1", [P, M, 4], BF16))
-        cut = M - 192
+        cut = M - 128
         nc.scalar.copy(
             x_woven[1][:, 0:cut, :].rearrange("p (c r) i -> p c i r", r=4),
             x_raw[1][:, :, 0:cut].rearrange("p i (c r) -> p c i r", r=4),
         )
         nc.vector.tensor_copy(x_woven[1][:, cut:M, :], x_raw[1][:, :, cut:M].rearrange("p i m -> p m i"))
         xq = [quantize("x0", x_woven[0][:], M)]
+
+        plane2 = sb("plane2", [P, S // 4], I32, 32 * KIB)
+        order_scales(picked_scales2, plane2)
 
         sig = {}
         for a in range(JP):
@@ -245,8 +247,8 @@ def tile_list_cross_modal_shortlist_kernel(
                         stop=(kp == passes[-1]),
                     )
                 gain = gains[:, i, a : a + 1]
-                if (a, i) == (0, 0):
-                    scaled = sb("scaled", [P, M], F32, 28 * KIB)
+                if i == 3 * a:
+                    scaled = sb("scaled%d" % a, [P, M], F32, (12 if a else 28) * KIB)
                     nc.scalar.activation(scaled[:], acc[:], ACT.Copy, scale=gain)
                     nc.gpsimd.tensor_tensor(flat[:, i, :], scaled[:], sig[a, i][:], ALU.mult)
                 else:
@@ -280,12 +282,20 @@ def tile_list_cross_modal_shortlist_kernel(
         def parts(quantized, starts):
             return [(quantized[0][:, c : c + P], quantized[1][:, c : c + P]) for c in starts]
 
-        flat = [make_h(a) for a in range(JP)]
         for c in range(PIECES):
             nc.scalar.copy(pairs[:, width * c : width * (c + 1), :], pair_raw[c][:].rearrange("p e t -> p t e"))
+        flat = [make_h(a) for a in range(JP)]
         pair_words = pairs[:].rearrange("p t e -> p (t e)").bitcast(U32)
         picked01 = [gather_pass(sb("wg01_%d" % a, [P, 4, P], U32)[:], pair_words, a) for a in range(JP)]
-        h_woven = [weave("hw0", flat[0], [nc.scalar.copy], 8 * KIB), weave("hw1", flat[1], [nc.scalar.copy], 12 * KIB)]
+        h_woven = [weave("hw0", flat[0], [nc.scalar.copy], 8 * KIB), sb("hw1", [P, M, 4], BF16, 12 * KIB)]
+        cut = M - 256
+        nc.scalar.copy(
+            h_woven[1][:, 0:cut, :].rearrange("p (c r) i -> p c i r", r=4),
+            flat[1][:, :, 0:cut].rearrange("p i (c r) -> p c i r", r=4),
+        )
+        nc.gpsimd.tensor_scalar(
+            h_woven[1][:, cut:M, :], flat[1][:, :, cut:M].rearrange("p i m -> p m i"), 1.0, 0.0, ALU.mult, ALU.add
+        )
         wd[3] = load_wd(3, 0)
         picked2 = [gather_rounded("wg2_%d" % a, wd[2][:], a) for a in range(JP)]
         hq = [quantize("h%d" % a, h_woven[a][:], M) for a in range(JP)]

@@ -288,6 +288,8 @@ def tile_list_cross_modal_shortlist_kernel(
         pair_words = pairs[:].rearrange("p t e -> p (t e)").bitcast(U32)
         picked01 = [gather_pass(sb("wg01_%d" % a, [P, 4, P], U32)[:], pair_words, a) for a in range(JP)]
         h_woven = [weave("hw0", flat[0], [nc.scalar.copy], 8 * KIB), sb("hw1", [P, M, 4], BF16, 12 * KIB)]
+        turned01 = [sb("wt01_%d" % a, [P, 2 * P, 4], BF16) for a in range(JP)]
+        turn(picked01[0], turned01[0][:], BF16, nc.scalar.copy)
         cut = M - 256
         nc.scalar.copy(
             h_woven[1][:, 0:cut, :].rearrange("p (c r) i -> p c i r", r=4),
@@ -298,12 +300,11 @@ def tile_list_cross_modal_shortlist_kernel(
         )
         wd[3] = load_wd(3, 0)
         picked2 = [gather_rounded("wg2_%d" % a, wd[2][:], a) for a in range(JP)]
-        hq = [quantize("h%d" % a, h_woven[a][:], M) for a in range(JP)]
-        wq01 = []
+        turn(picked01[1], turned01[1][:], BF16, nc.scalar.copy)
+        hq, wq01 = [], []
         for a in range(JP):
-            turned = sb("wt01_%d" % a, [P, 2 * P, 4], BF16)
-            turn(picked01[a], turned[:], BF16, nc.scalar.copy)
-            wq01.append(quantize("w01_%d" % a, turned[:], 2 * P))
+            hq.append(quantize("h%d" % a, h_woven[a][:], M))
+            wq01.append(quantize("w01_%d" % a, turned01[a][:], 2 * P))
         whole = slice(0, M)
         halves = [slice(0, M // 2), slice(M // 2, M)]
         sums = [pool_rows([(c[:, P * t : P * (t + 1)], s[:, P * t : P * (t + 1)]) for c, s in wq01], whole) for t in range(2)]

@@ -99,26 +99,26 @@ def tile_list_cross_modal_shortlist_kernel(
         xs = xt_scales.bitcast(I32)
         for q in range(4):
             nc.gpsimd.dma_start(xts[32 * q : 32 * q + 4, :, :], xs[:, 4 * q : 4 * q + 4, :].rearrange("a r c -> r a c"))
-        g_rows = sb("g_rows", [JP, 512], F32)
-        nc.sync.dma_start(g_rows[:], g.rearrange("(a c) -> a c", a=JP))
+        first_words = sb("w1_0", [P, T], I32)
+        words0 = tab_words[0].rearrange("p t i -> p (t i)").bitcast(I32)
+        nc.sync.dma_start(first_words[:, 0 : T // 4], words0[:, 0 : T // 4])
         rows1 = tab_scales.bitcast(I32).rearrange("a (q r) c -> r q a c", r=4)
         for r in range(4):
             nc.sync.dma_start(sw1[r:P:16, :], rows1[r])
-        w1 = [load_words(tab_words, 0, "w1_0"), load_words(tab_words, 1, "w1_1", 18 * KIB)]
+        g_rows = sb("g_rows", [JP, 512], F32)
+        nc.sync.dma_start(g_rows[:], g.rearrange("(a c) -> a c", a=JP))
+        nc.sync.dma_start(first_words[:, T // 4 : T], words0[:, T // 4 : T])
+        w1 = [first_words, load_words(tab_words, 1, "w1_1", 18 * KIB)]
         xtw = sb("xtw", [P, KP, M // 2], I32)
         nc.sync.dma_start(xtw[:], xt_words.bitcast(I32).rearrange("a p c -> p a c"))
         x_raw = [load_x(kp) for kp in range(KP)]
 
         def gather_scales(win, name, at=None):
-            picked = sb(name, [P, S], U8, at)
-            nc.vector.tensor_copy(picked[:], win[:].bitcast(U8).indirect(offsets[:]))
-            return picked
-
-        def order_scales(picked, plane):
+            plane = sb(name, [P, S], U8, at)
             nc.vector.tensor_copy(
-                plane[:].rearrange("p (i b h) -> p i b h", i=4, h=2),
-                picked[:].bitcast(I32).rearrange("p (b i h) -> p i b h", i=4, h=2),
+                plane[:].rearrange("p (i b s) -> p b i s", i=4, s=8), win[:].bitcast(U8).indirect(offsets[:])
             )
+            return plane
 
         def gather_words(words, name, parts, at=None):
             picked = sb(name, [P, S], U32, at)
@@ -133,8 +133,8 @@ def tile_list_cross_modal_shortlist_kernel(
             nc.vector.tensor_copy(blocks, words.indirect(offsets[:, 32 * a : 32 * (a + 1)]))
             return picked
 
-        def gather_rounded(name, rows, a):
-            picked = sb(name, [P, 2, 2 * P], BF16)
+        def gather_rounded(name, rows, a, at=None):
+            picked = sb(name, [P, 2, 2 * P], BF16, at)
             nc.vector.tensor_copy(
                 picked[:].rearrange("p u (b s e) -> p b u e s", s=8, e=2), rows.indirect(offsets[:, 32 * a : 32 * (a + 1)])
             )
@@ -161,29 +161,25 @@ def tile_list_cross_modal_shortlist_kernel(
             return slice(256 * i + P * a, 256 * i + P * (a + 1))
 
 
-        ordered1 = sb("ordered1", [P, S // 4], I32)
-        order_scales(gather_scales(sw1, "picked1"), ordered1)
-        nc.sync.dma_start(shifted1[0 : P - 16, :], ordered1[16:P, :])
-        planes1 = [ordered1, shifted1]
+        plane1 = gather_scales(sw1, "plane1")
+        nc.sync.dma_start(shifted1[0 : P - 16, :], plane1[16:P, :].bitcast(I32))
+        planes1 = [plane1[:], shifted1[:].bitcast(U8)]
         w2 = [load_words(tab2_words, 0, "w2_0"), load_words(tab2_words, 1, "w2_1")]
         pair_raw = [load_pair_piece(c, {0: 28 * KIB, PIECES - 2: 10 * KIB}.get(c)) for c in range(PIECES)]
         wd = {2: load_wd(2)}
 
         v1 = [gather_words(w1[0][:].bitcast(U32), "v1_0", 1)]
         v1.append(gather_words(w1[1][:].bitcast(U32), "v1_1", JP))
-        picked_scales2 = gather_scales(sw2, "picked2", 18 * KIB)
+        plane2 = gather_scales(sw2, "plane2", 18 * KIB)
         x_woven = [weave("xb0", x_raw[0], [nc.scalar.copy], None)]
         x_woven.append(sb("xb1", [P, M, 4], BF16))
-        cut = M - 128
+        cut = M - 256
         nc.scalar.copy(
             x_woven[1][:, 0:cut, :].rearrange("p (c r) i -> p c i r", r=4),
             x_raw[1][:, :, 0:cut].rearrange("p i (c r) -> p c i r", r=4),
         )
         nc.vector.tensor_copy(x_woven[1][:, cut:M, :], x_raw[1][:, :, cut:M].rearrange("p i m -> p m i"))
         xq = [quantize("x0", x_woven[0][:], M)]
-
-        plane2 = sb("plane2", [P, S // 4], I32, 32 * KIB)
-        order_scales(picked_scales2, plane2)
 
         sig = {}
         for a in range(JP):
@@ -194,7 +190,7 @@ def tile_list_cross_modal_shortlist_kernel(
                     nc.tensor.matmul_mx(
                         out=acc[:],
                         lhsT=v1[kp][:, cols(a, i)].bitcast(FP8X4),
-                        lhsT_scale=planes1[kp][:].bitcast(U8)[:, cols(a, i)],
+                        lhsT_scale=planes1[kp][:, cols(a, i)],
                         rhs=xtw[:, kp, :].bitcast(U8).bitcast(FP4X4),
                         rhs_scale=xts[:, kp, :].bitcast(U8),
                         start=(kp == passes[0]),
@@ -232,7 +228,7 @@ def tile_list_cross_modal_shortlist_kernel(
             copy(words.rearrange("p (n u) -> p n u", u=2), bank[:].rearrange("p u n -> p n u"))
 
         def make_h(a):
-            flat = sb("hp%d" % a, [P, 4, M], BF16, 0 if a == 0 else None)
+            flat = sb("hp%d" % a, [P, 4, M], BF16)
             for i in range(4):
                 acc = next_bank([P, M])
                 passes = [1, 0] if a else [0, 1]
@@ -240,7 +236,7 @@ def tile_list_cross_modal_shortlist_kernel(
                     nc.tensor.matmul_mx(
                         out=acc[:],
                         lhsT=v2[kp][:, cols(a, i)].bitcast(FP8X4),
-                        lhsT_scale=plane2[8 + 4 * kp : P, :].bitcast(U8)[:, cols(a, i)],
+                        lhsT_scale=plane2[8 + 4 * kp : P, cols(a, i)],
                         rhs=xq[kp][0][:].bitcast(FP8X4),
                         rhs_scale=xq[kp][1][:],
                         start=(kp == passes[0]),
@@ -288,7 +284,7 @@ def tile_list_cross_modal_shortlist_kernel(
         pair_words = pairs[:].rearrange("p t e -> p (t e)").bitcast(U32)
         picked01 = [gather_pass(sb("wg01_%d" % a, [P, 4, P], U32)[:], pair_words, a) for a in range(JP)]
         h_woven = [weave("hw0", flat[0], [nc.scalar.copy], 8 * KIB), sb("hw1", [P, M, 4], BF16, 12 * KIB)]
-        turned01 = [sb("wt01_%d" % a, [P, 2 * P, 4], BF16) for a in range(JP)]
+        turned01 = [sb("wt01_%d" % a, [P, 2 * P, 4], BF16, 0 if a else None) for a in range(JP)]
         turn(picked01[0], turned01[0][:], BF16, nc.scalar.copy)
         cut = M - 256
         nc.scalar.copy(
@@ -298,7 +294,7 @@ def tile_list_cross_modal_shortlist_kernel(
         nc.gpsimd.tensor_scalar(
             h_woven[1][:, cut:M, :], flat[1][:, :, cut:M].rearrange("p i m -> p m i"), 1.0, 0.0, ALU.mult, ALU.add
         )
-        wd[3] = load_wd(3, 0)
+        wd[3] = load_wd(3)
         picked2 = [gather_rounded("wg2_%d" % a, wd[2][:], a) for a in range(JP)]
         turn(picked01[1], turned01[1][:], BF16, nc.scalar.copy)
         hq, wq01 = [], []
@@ -313,9 +309,9 @@ def tile_list_cross_modal_shortlist_kernel(
             turn_words(picked2[a], turned2[:, a], nc.scalar.copy)
         root_warm = sb("root_warm", [P, 1], F32)
         nc.scalar.activation(root_warm[:], turned2[:, 0, 0, 0:1], ACT.Sqrt, bias=sig[1, 3][:, 0:1], scale=0.0)
-        picked3 = [gather_rounded("wg3_0", wd[3][:], 0)]
+        picked3 = [gather_rounded("wg3_0", wd[3][:], 0, 0)]
         wq2 = quantize("w2", turned2[:].rearrange("p a n i -> p (a n) i"), P * JP)
-        picked3.append(gather_rounded("wg3_1", wd[3][:], 1))
+        picked3.append(gather_rounded("wg3_1", wd[3][:], 1, KIB))
         wq3 = []
         for a in range(JP):
             turned = sb("wt3_%d" % a, [P, P, 4], BF16)

@@ -20,8 +20,20 @@ ALU = mybir.AluOpType
 P = 128
 KP = K // 512
 JP = S // 512
+BANKS = 8
 PIECES = 4
+HEAD_COLUMNS = T // 4
+VECTOR_X_COLUMNS = 256
+GPSIMD_H_COLUMNS = 256
+GPSIMD_SLOT = (0, 3)
+
 KIB = 1024
+AT_LAST_TURN = 0
+AT_H0 = 8 * KIB
+AT_THIRD_PIECE = 10 * KIB
+AT_H1 = 12 * KIB
+AT_TAB_LAST = 18 * KIB
+AT_FIRST_PIECE = 28 * KIB
 
 
 def tile_list_cross_modal_shortlist_kernel(
@@ -41,18 +53,18 @@ def tile_list_cross_modal_shortlist_kernel(
         banks = []
 
         def next_bank(shape):
-            banks.append(psum.tile(shape, F32, name="bank%d" % (len(banks) % 8)))
+            banks.append(psum.tile(shape, F32, name="bank%d" % (len(banks) % BANKS)))
             return banks[-1]
 
         offsets = keep.tile([P, S // 16], U16, name="offsets")
         nc.sync.dma_start(offsets[:], offs)
 
-        sw1 = sb("sw1", [P, T // 4], I32)
-        nc.gpsimd.memset(sw1[:], 0)
-        sw2 = sb("sw2", [P, T // 4], I32)
-        xts = sb("xts", [P, KP, M // 4], I32)
-        shifted1 = sb("shifted1", [P, S // 4], I32)
-        g_slots = sb("g_slots", [P, 4, P], F32, 16 * KIB)
+        tab_rows = sb("sw1", [P, T // 4], I32)
+        nc.gpsimd.memset(tab_rows[:], 0)
+        tab2_rows = sb("sw2", [P, T // 4], I32)
+        xt_planes = sb("xts", [P, KP, M // 4], I32)
+        tab_plane_moved = sb("shifted1", [P, S // 4], I32)
+        g_slots = sb("g_slots", [P, 4, P], F32)
         warm = sb("warm", [P, 2], F32)
         ident = sb("ident", [P, P], F32)
         make_identity(nc, ident[:])
@@ -62,97 +74,92 @@ def tile_list_cross_modal_shortlist_kernel(
             nc.vector.memset(rows[:, 0 : width - 1], 0)
             nc.vector.memset(rows[:, width - 1 : width], 0)
 
-        clear(sw2[:])
-        clear(warm[:])
-        clear(xts[:].rearrange("p a c -> p (a c)"))
+        clear(tab2_rows[:])
+        nc.vector.memset(warm[:, 0:1], 0)
+        clear(xt_planes[:].rearrange("p a c -> p (a c)"))
         clear(g_slots[:].rearrange("p i c -> p (i c)"))
-        clear(shifted1[:])
+        clear(tab_plane_moved[:])
         nc.scalar.activation(warm[:, 1:2], warm[:, 0:1], ACT.Sigmoid)
 
-        def load_scales(queue, win, src, quadrants):
-            for q in quadrants:
-                queue.dma_start(win[32 * q + 8 : 32 * q + 16, :], src.bitcast(I32)[:, 4 * q : 4 * q + 4, :])
-
         def load_words(src, kp, name, at=None):
-            win = sb(name, [P, T], I32, at)
-            nc.sync.dma_start(win[:], src[kp].rearrange("p t i -> p (t i)").bitcast(I32))
-            return win
+            words = sb(name, [P, T], I32, at)
+            nc.sync.dma_start(words[:], src[kp].rearrange("p t i -> p (t i)").bitcast(I32))
+            return words
 
         def load_x(kp):
-            raw = sb("x%d" % kp, [P, 4, M], F32, None if kp else 32 * KIB)
+            raw = sb("x%d" % kp, [P, 4, M], F32)
             nc.sync.dma_start(raw[:], x[512 * kp : 512 * (kp + 1), :].rearrange("(p i) m -> p i m", i=4))
             return raw
 
-        def load_pair_piece(piece, at=None):
-            width = T // PIECES
-            raw = sb("pair%d" % piece, [P, 2, width], F32, at)
-            rows = wdT[0 : 2 * P, width * piece : width * (piece + 1)]
-            nc.sync.dma_start(raw[:], rows.rearrange("(p e) t -> p e t", e=2))
+        piece = T // PIECES
+
+        def load_pair_piece(c, at):
+            raw = sb("pair%d" % c, [P, 2, piece], F32, at)
+            nc.sync.dma_start(raw[:], wdT[0 : 2 * P, piece * c : piece * (c + 1)].rearrange("(p e) t -> p e t", e=2))
             return raw
 
-        def load_wd(nt, at=None):
-            win = sb("wd%d" % nt, [P, T], F32, at)
-            nc.sync.dma_start(win[:], wdT[P * nt : P * (nt + 1), :])
-            return win
+        def load_wd(nt):
+            rows = sb("wd%d" % nt, [P, T], F32)
+            nc.sync.dma_start(rows[:], wdT[P * nt : P * (nt + 1), :])
+            return rows
 
-        load_scales(nc.gpsimd, sw2, tab2_scales, range(4))
-        xs = xt_scales.bitcast(I32)
         for q in range(4):
-            nc.gpsimd.dma_start(xts[32 * q : 32 * q + 4, :, :], xs[:, 4 * q : 4 * q + 4, :].rearrange("a r c -> r a c"))
+            nc.gpsimd.dma_start(tab2_rows[32 * q + 8 : 32 * q + 16, :], tab2_scales.bitcast(I32)[:, 4 * q : 4 * q + 4, :])
+        xt_rows = xt_scales.bitcast(I32)
+        for q in range(4):
+            nc.gpsimd.dma_start(
+                xt_planes[32 * q : 32 * q + 4, :, :], xt_rows[:, 4 * q : 4 * q + 4, :].rearrange("a r c -> r a c")
+            )
         first_words = sb("w1_0", [P, T], I32)
-        words0 = tab_words[0].rearrange("p t i -> p (t i)").bitcast(I32)
-        nc.sync.dma_start(first_words[:, 0 : T // 4], words0[:, 0 : T // 4])
-        rows1 = tab_scales.bitcast(I32).rearrange("a (q r) c -> r q a c", r=4)
+        first_src = tab_words[0].rearrange("p t i -> p (t i)").bitcast(I32)
+        nc.sync.dma_start(first_words[:, 0:HEAD_COLUMNS], first_src[:, 0:HEAD_COLUMNS])
+        tab_src = tab_scales.bitcast(I32).rearrange("a (q r) c -> r q a c", r=4)
         for r in range(4):
-            nc.sync.dma_start(sw1[r:P:16, :], rows1[r])
+            nc.sync.dma_start(tab_rows[r:P:16, :], tab_src[r])
         g_rows = sb("g_rows", [JP, 512], F32)
         nc.sync.dma_start(g_rows[:], g.rearrange("(a c) -> a c", a=JP))
-        nc.sync.dma_start(first_words[:, T // 4 : T], words0[:, T // 4 : T])
-        w1 = [first_words, load_words(tab_words, 1, "w1_1", 18 * KIB)]
-        xtw = sb("xtw", [P, KP, M // 2], I32)
-        nc.sync.dma_start(xtw[:], xt_words.bitcast(I32).rearrange("a p c -> p a c"))
+        nc.sync.dma_start(first_words[:, HEAD_COLUMNS:T], first_src[:, HEAD_COLUMNS:T])
+        tab = [first_words, load_words(tab_words, 1, "w1_1", AT_TAB_LAST)]
+        xt = sb("xtw", [P, KP, M // 2], I32)
+        nc.sync.dma_start(xt[:], xt_words.bitcast(I32).rearrange("a p c -> p a c"))
         x_raw = [load_x(kp) for kp in range(KP)]
 
-        def gather_scales(win, name, at=None):
+        def gather_scales(rows, name, at=None):
             plane = sb(name, [P, S], U8, at)
             nc.vector.tensor_copy(
-                plane[:].rearrange("p (i b s) -> p b i s", i=4, s=8), win[:].bitcast(U8).indirect(offsets[:])
+                plane[:].rearrange("p (i b s) -> p b i s", i=4, s=8), rows[:].bitcast(U8).indirect(offsets[:])
             )
             return plane
 
-        def gather_words(words, name, parts, at=None):
-            picked = sb(name, [P, S], U32, at)
+        def gather_words(words, name, parts):
+            picked = sb(name, [P, S], U32)
             blocks = picked[:].rearrange("p (i b s) -> p b i s", i=4, s=8)
             for part in range(parts):
                 first, last = 32 * part // parts, 32 * (part + 1) // parts
-                nc.vector.tensor_copy(blocks[:, first:last], words.indirect(offsets[:, 2 * first : 2 * last]))
+                nc.vector.tensor_copy(
+                    blocks[:, first:last], words[:].bitcast(U32).indirect(offsets[:, 2 * first : 2 * last])
+                )
             return picked
 
-        def gather_pass(picked, words, a):
-            blocks = picked.rearrange("p i (b s) -> p b i s", s=8)
-            nc.vector.tensor_copy(blocks, words.indirect(offsets[:, 32 * a : 32 * (a + 1)]))
+        def gather_pair(words, a):
+            picked = sb("wg01_%d" % a, [P, 4, P], U32)
+            nc.vector.tensor_copy(
+                picked[:].rearrange("p i (q s) -> p q i s", s=8), words.indirect(offsets[:, 32 * a : 32 * (a + 1)])
+            )
             return picked
 
         def gather_rounded(name, rows, a, at=None):
             picked = sb(name, [P, 2, 2 * P], BF16, at)
             nc.vector.tensor_copy(
-                picked[:].rearrange("p u (b s e) -> p b u e s", s=8, e=2), rows.indirect(offsets[:, 32 * a : 32 * (a + 1)])
+                picked[:].rearrange("p u (q s e) -> p q u e s", s=8, e=2), rows.indirect(offsets[:, 32 * a : 32 * (a + 1)])
             )
             return picked
 
-        def weave(name, planes, copies, at=None):
-            woven = sb(name, [P, M, 4], BF16, at)
-            width = M // len(copies)
-            for part, copy in enumerate(copies):
-                span = slice(width * part, width * (part + 1))
-                copy(
-                    woven[:, span, :].rearrange("p (c r) i -> p c i r", r=4),
-                    planes[:, :, span].rearrange("p i (c r) -> p c i r", r=4),
-                )
-            return woven
+        def weave(woven, slots):
+            nc.scalar.copy(woven.rearrange("p (c r) i -> p c i r", r=4), slots.rearrange("p i (c r) -> p c i r", r=4))
 
-        def quantize(name, woven, width, at=None):
-            codes = sb(name + "c", [P, width], U32, at)
+        def quantize(name, woven, width):
+            codes = sb(name + "c", [P, width], U32)
             scales = sb(name + "s", [P, width], U8)
             nc.vector.quantize_mx(out=codes[:].bitcast(FP8X4), scales=scales[:], in_=woven.rearrange("p n i -> p (n i)"))
             return codes, scales
@@ -160,44 +167,41 @@ def tile_list_cross_modal_shortlist_kernel(
         def cols(a, i):
             return slice(256 * i + P * a, 256 * i + P * (a + 1))
 
+        def k_order(a):
+            return [1, 0] if a else [0, 1]
 
-        plane1 = gather_scales(sw1, "plane1")
-        nc.sync.dma_start(shifted1[0 : P - 16, :], plane1[16:P, :].bitcast(I32))
-        planes1 = [plane1[:], shifted1[:].bitcast(U8)]
-        w2 = [load_words(tab2_words, 0, "w2_0"), load_words(tab2_words, 1, "w2_1")]
-        pair_raw = [load_pair_piece(c, {0: 28 * KIB, PIECES - 2: 10 * KIB}.get(c)) for c in range(PIECES)]
-        wd = {2: load_wd(2)}
+        tab_plane = gather_scales(tab_rows, "plane1")
+        nc.sync.dma_start(tab_plane_moved[0 : P - 16, :], tab_plane[16:P, :].bitcast(I32))
+        tab_planes = [tab_plane[:], tab_plane_moved[:].bitcast(U8)]
+        tab2 = [load_words(tab2_words, kp, "w2_%d" % kp) for kp in range(KP)]
+        pair_raw = [load_pair_piece(c, {0: AT_FIRST_PIECE, 2: AT_THIRD_PIECE}.get(c)) for c in range(PIECES)]
+        wd2 = load_wd(2)
 
-        v1 = [gather_words(w1[0][:].bitcast(U32), "v1_0", 1)]
-        v1.append(gather_words(w1[1][:].bitcast(U32), "v1_1", JP))
-        plane2 = gather_scales(sw2, "plane2", 18 * KIB)
-        x_woven = [weave("xb0", x_raw[0], [nc.scalar.copy], None)]
-        x_woven.append(sb("xb1", [P, M, 4], BF16))
-        cut = M - 256
-        nc.scalar.copy(
-            x_woven[1][:, 0:cut, :].rearrange("p (c r) i -> p c i r", r=4),
-            x_raw[1][:, :, 0:cut].rearrange("p i (c r) -> p c i r", r=4),
-        )
-        nc.vector.tensor_copy(x_woven[1][:, cut:M, :], x_raw[1][:, :, cut:M].rearrange("p i m -> p m i"))
+        v = [gather_words(tab[0], "v1_0", 1), gather_words(tab[1], "v1_1", JP)]
+        tab2_plane = gather_scales(tab2_rows, "plane2", AT_TAB_LAST)
+        x_woven = [sb("xb%d" % kp, [P, M, 4], BF16) for kp in range(KP)]
+        weave(x_woven[0][:], x_raw[0][:])
+        x_cut = M - VECTOR_X_COLUMNS
+        weave(x_woven[1][:, 0:x_cut, :], x_raw[1][:, :, 0:x_cut])
+        nc.vector.tensor_copy(x_woven[1][:, x_cut:M, :], x_raw[1][:, :, x_cut:M].rearrange("p i m -> p m i"))
         xq = [quantize("x0", x_woven[0][:], M)]
 
-        sig = {}
+        gate = {}
         for a in range(JP):
             for i in range(4):
                 acc = next_bank([P, M])
-                passes = [1, 0] if a else [0, 1]
-                for kp in passes:
+                for kp in k_order(a):
                     nc.tensor.matmul_mx(
                         out=acc[:],
-                        lhsT=v1[kp][:, cols(a, i)].bitcast(FP8X4),
-                        lhsT_scale=planes1[kp][:, cols(a, i)],
-                        rhs=xtw[:, kp, :].bitcast(U8).bitcast(FP4X4),
-                        rhs_scale=xts[:, kp, :].bitcast(U8),
-                        start=(kp == passes[0]),
-                        stop=(kp == passes[-1]),
+                        lhsT=v[kp][:, cols(a, i)].bitcast(FP8X4),
+                        lhsT_scale=tab_planes[kp][:, cols(a, i)],
+                        rhs=xt[:, kp, :].bitcast(U8).bitcast(FP4X4),
+                        rhs_scale=xt_planes[:, kp, :].bitcast(U8),
+                        start=(kp == k_order(a)[0]),
+                        stop=(kp == k_order(a)[-1]),
                     )
-                sig[a, i] = sb("sig%d%d" % (a, i), [P, M], F32)
-                nc.scalar.activation(sig[a, i][:], acc[:], ACT.Sigmoid)
+                gate[a, i] = sb("sig%d%d" % (a, i), [P, M], F32)
+                nc.scalar.activation(gate[a, i][:], acc[:], ACT.Sigmoid)
 
         nc.scalar.copy(
             g_slots[0:JP].rearrange("p i (q s) -> p i q s", s=8), g_rows[:].rearrange("p (q i s) -> p i q s", i=4, s=8)
@@ -208,19 +212,16 @@ def tile_list_cross_modal_shortlist_kernel(
         gains = sb("gains", [P, 4, JP], F32)
         nc.scalar.copy(gains[:], g_bank[:, :, 0:JP])
         xq.append(quantize("x1", x_woven[1][:], M))
-        v2 = [gather_words(w2[0][:].bitcast(U32), "v2_0", JP)]
-        v2.append(gather_words(w2[1][:].bitcast(U32), "v2_1", JP))
-        pairs = sb("pairs", [P, T, 2], BF16)
-        width = T // PIECES
+        v2 = [gather_words(tab2[kp], "v2_%d" % kp, JP) for kp in range(KP)]
+        pair = sb("pairs", [P, T, 2], BF16)
 
-        def turn(picked, turned, view, copy):
+        def turn_pair(picked, turned):
             bank = next_bank([P, 4, P])
             for i in range(4):
                 nc.tensor.transpose(bank[:, i, :], picked[:, i, :].bitcast(F32), ident[:])
-            copy(turned, bank[:].bitcast(view).rearrange("p i n -> p n i"))
+            nc.scalar.copy(turned, bank[:].bitcast(BF16).rearrange("p i n -> p n i"))
 
-
-        def turn_words(picked, turned, copy):
+        def turn_rounded(picked, turned, copy):
             bank = next_bank([P, 2, P])
             for u in range(2):
                 nc.tensor.transpose(bank[:, u, :], picked[:, u, :].bitcast(F32), ident[:])
@@ -228,28 +229,27 @@ def tile_list_cross_modal_shortlist_kernel(
             copy(words.rearrange("p (n u) -> p n u", u=2), bank[:].rearrange("p u n -> p n u"))
 
         def make_h(a):
-            flat = sb("hp%d" % a, [P, 4, M], BF16)
+            slots = sb("hp%d" % a, [P, 4, M], BF16)
             for i in range(4):
                 acc = next_bank([P, M])
-                passes = [1, 0] if a else [0, 1]
-                for kp in passes:
+                for kp in k_order(a):
                     nc.tensor.matmul_mx(
                         out=acc[:],
                         lhsT=v2[kp][:, cols(a, i)].bitcast(FP8X4),
-                        lhsT_scale=plane2[8 + 4 * kp : P, cols(a, i)],
+                        lhsT_scale=tab2_plane[8 + 4 * kp : P, cols(a, i)],
                         rhs=xq[kp][0][:].bitcast(FP8X4),
                         rhs_scale=xq[kp][1][:],
-                        start=(kp == passes[0]),
-                        stop=(kp == passes[-1]),
+                        start=(kp == k_order(a)[0]),
+                        stop=(kp == k_order(a)[-1]),
                     )
                 gain = gains[:, i, a : a + 1]
-                if i == 3 * a:
-                    scaled = sb("scaled%d" % a, [P, M], F32, (12 if a else 28) * KIB)
+                if i == GPSIMD_SLOT[a]:
+                    scaled = sb("scaled%d" % a, [P, M], F32, AT_H1 if a else AT_FIRST_PIECE)
                     nc.scalar.activation(scaled[:], acc[:], ACT.Copy, scale=gain)
-                    nc.gpsimd.tensor_tensor(flat[:, i, :], scaled[:], sig[a, i][:], ALU.mult)
+                    nc.gpsimd.tensor_tensor(slots[:, i, :], scaled[:], gate[a, i][:], ALU.mult)
                 else:
-                    nc.vector.scalar_tensor_tensor(flat[:, i, :], acc[:], gain, sig[a, i][:], ALU.mult, ALU.mult)
-            return flat
+                    nc.vector.scalar_tensor_tensor(slots[:, i, :], acc[:], gain, gate[a, i][:], ALU.mult, ALU.mult)
+            return slots
 
         def pool_rows(wq, span):
             bank = next_bank([P, span.stop - span.start])
@@ -275,51 +275,49 @@ def tile_list_cross_modal_shortlist_kernel(
             nc.scalar.activation(res[:], mag[:], ACT.Sqrt)
             nc.sync.dma_start(out[P * nt : P * (nt + 1), span], res[:])
 
-        def parts(quantized, starts):
-            return [(quantized[0][:, c : c + P], quantized[1][:, c : c + P]) for c in starts]
-
         for c in range(PIECES):
-            nc.scalar.copy(pairs[:, width * c : width * (c + 1), :], pair_raw[c][:].rearrange("p e t -> p t e"))
-        flat = [make_h(a) for a in range(JP)]
-        pair_words = pairs[:].rearrange("p t e -> p (t e)").bitcast(U32)
-        picked01 = [gather_pass(sb("wg01_%d" % a, [P, 4, P], U32)[:], pair_words, a) for a in range(JP)]
-        h_woven = [weave("hw0", flat[0], [nc.scalar.copy], 8 * KIB), sb("hw1", [P, M, 4], BF16, 12 * KIB)]
-        turned01 = [sb("wt01_%d" % a, [P, 2 * P, 4], BF16, 0 if a else None) for a in range(JP)]
-        turn(picked01[0], turned01[0][:], BF16, nc.scalar.copy)
-        cut = M - 256
-        nc.scalar.copy(
-            h_woven[1][:, 0:cut, :].rearrange("p (c r) i -> p c i r", r=4),
-            flat[1][:, :, 0:cut].rearrange("p i (c r) -> p c i r", r=4),
-        )
+            nc.scalar.copy(pair[:, piece * c : piece * (c + 1), :], pair_raw[c][:].rearrange("p e t -> p t e"))
+        h_slots = [make_h(a) for a in range(JP)]
+        pair_words = pair[:].rearrange("p t e -> p (t e)").bitcast(U32)
+        pair_picked = [gather_pair(pair_words, a) for a in range(JP)]
+        h_woven = [sb("hw0", [P, M, 4], BF16, AT_H0), sb("hw1", [P, M, 4], BF16, AT_H1)]
+        weave(h_woven[0][:], h_slots[0][:])
+        pair_turned = [sb("wt01_%d" % a, [P, 2 * P, 4], BF16, AT_LAST_TURN if a else None) for a in range(JP)]
+        turn_pair(pair_picked[0], pair_turned[0][:])
+        h_cut = M - GPSIMD_H_COLUMNS
+        weave(h_woven[1][:, 0:h_cut, :], h_slots[1][:, :, 0:h_cut])
         nc.gpsimd.tensor_scalar(
-            h_woven[1][:, cut:M, :], flat[1][:, :, cut:M].rearrange("p i m -> p m i"), 1.0, 0.0, ALU.mult, ALU.add
+            h_woven[1][:, h_cut:M, :], h_slots[1][:, :, h_cut:M].rearrange("p i m -> p m i"), 1.0, 0.0, ALU.mult, ALU.add
         )
-        wd[3] = load_wd(3)
-        picked2 = [gather_rounded("wg2_%d" % a, wd[2][:], a) for a in range(JP)]
-        turn(picked01[1], turned01[1][:], BF16, nc.scalar.copy)
-        hq, wq01 = [], []
+        wd3 = load_wd(3)
+        picked2 = [gather_rounded("wg2_%d" % a, wd2[:], a) for a in range(JP)]
+        turn_pair(pair_picked[1], pair_turned[1][:])
+        hq, pair_q = [], []
         for a in range(JP):
             hq.append(quantize("h%d" % a, h_woven[a][:], M))
-            wq01.append(quantize("w01_%d" % a, turned01[a][:], 2 * P))
+            pair_q.append(quantize("w01_%d" % a, pair_turned[a][:], 2 * P))
         whole = slice(0, M)
         halves = [slice(0, M // 2), slice(M // 2, M)]
-        sums = [pool_rows([(c[:, P * t : P * (t + 1)], s[:, P * t : P * (t + 1)]) for c, s in wq01], whole) for t in range(2)]
+        sums = [
+            pool_rows([(c[:, P * nt : P * (nt + 1)], s[:, P * nt : P * (nt + 1)]) for c, s in pair_q], whole)
+            for nt in range(2)
+        ]
         turned2 = sb("wt2", [P, JP, P, 4], BF16)
         for a in range(JP):
-            turn_words(picked2[a], turned2[:, a], nc.scalar.copy)
+            turn_rounded(picked2[a], turned2[:, a], nc.scalar.copy)
         root_warm = sb("root_warm", [P, 1], F32)
-        nc.scalar.activation(root_warm[:], turned2[:, 0, 0, 0:1], ACT.Sqrt, bias=sig[1, 3][:, 0:1], scale=0.0)
-        picked3 = [gather_rounded("wg3_0", wd[3][:], 0, 0)]
-        wq2 = quantize("w2", turned2[:].rearrange("p a n i -> p (a n) i"), P * JP)
-        picked3.append(gather_rounded("wg3_1", wd[3][:], 1, KIB))
+        nc.scalar.activation(root_warm[:], turned2[:, 0, 0, 0:1], ACT.Sqrt, bias=gate[1, 3][:, 0:1], scale=0.0)
+        picked3 = [gather_rounded("wg3_0", wd3[:], 0, AT_LAST_TURN)]
+        codes2, scales2 = quantize("w2", turned2[:].rearrange("p a n i -> p (a n) i"), P * JP)
+        picked3.append(gather_rounded("wg3_1", wd3[:], 1, AT_LAST_TURN + KIB))
         wq3 = []
         for a in range(JP):
-            turned = sb("wt3_%d" % a, [P, P, 4], BF16)
-            turn_words(picked3[a], turned[:], nc.vector.tensor_copy)
-            codes, scales = quantize("w3_%d" % a, turned[:], P)
-            wq3.append((codes[:], scales[:]))
+            turned3 = sb("wt3_%d" % a, [P, P, 4], BF16)
+            turn_rounded(picked3[a], turned3[:], nc.vector.tensor_copy)
+            codes3, scales3 = quantize("w3_%d" % a, turned3[:], P)
+            wq3.append((codes3[:], scales3[:]))
             if a == 0:
-                sums.append(pool_rows(parts(wq2, [0, P]), whole))
+                sums.append(pool_rows([(codes2[:, c : c + P], scales2[:, c : c + P]) for c in (0, P)], whole))
         last = [pool_rows(wq3, span) for span in halves]
         mags = [magnitude(nt, sums[nt], whole) for nt in range(2)]
         store_root(*mags[0])

from contextlib import ExitStack

import concourse.mybir as mybir
from concourse.masks import make_identity

K, T, S, M, N = 1024, 2048, 1024, 512, 512
FLOPS = 2 * (2 * K * S * M + S * N * M)

F32 = mybir.dt.float32
BF16 = mybir.dt.bfloat16
I32 = mybir.dt.int32
U32 = mybir.dt.uint32
U16 = mybir.dt.uint16
U8 = mybir.dt.uint8
FP8X4 = mybir.dt.float8_e4m3fn_x4
FP4X4 = mybir.dt.float4_e2m1fn_x4
ACT = mybir.ActivationFunctionType
ALU = mybir.AluOpType

P = 128
KP = K // 512
JP = S // 512
BANKS = 8
PIECES = 4
HEAD_COLUMNS = T // 4
VECTOR_X_COLUMNS = 256
GPSIMD_H_COLUMNS = 256
GPSIMD_SLOT = (0, 3)

KIB = 1024
AT_LAST_TURN = 0
AT_H0 = 8 * KIB
AT_THIRD_PIECE = 10 * KIB
AT_H1 = 12 * KIB
AT_TAB_LAST = 18 * KIB
AT_FIRST_PIECE = 28 * KIB


def tile_list_cross_modal_shortlist_kernel(
    tc, tab_words, tab_scales, tab2_words, tab2_scales, xt_words, xt_scales, x, g, wdT, offs, out
):
    nc = tc.nc
    with ExitStack() as ctx:
        keep = ctx.enter_context(tc.tile_pool(name="keep", bufs=1))
        stream = ctx.enter_context(tc.tile_pool(name="stream", bufs=1))
        psum = ctx.enter_context(tc.psum_pool(name="psum", bufs=1))

        def sb(name, shape, dtype, at=None):
            if at is None:
                return keep.tile(shape, dtype, name=name, align_bytes=64)
            return stream.tile(shape, dtype, name=name, align_bytes=64, offset=at)

        banks = []

        def next_bank(shape):
            banks.append(psum.tile(shape, F32, name="bank%d" % (len(banks) % BANKS)))
            return banks[-1]

        offsets = keep.tile([P, S // 16], U16, name="offsets")
        nc.sync.dma_start(offsets[:], offs)

        tab_rows = sb("sw1", [P, T // 4], I32)
        nc.gpsimd.memset(tab_rows[:], 0)
        tab2_rows = sb("sw2", [P, T // 4], I32)
        xt_planes = sb("xts", [P, KP, M // 4], I32)
        tab_plane_moved = sb("shifted1", [P, S // 4], I32)
        g_slots = sb("g_slots", [P, 4, P], F32)
        warm = sb("warm", [P, 2], F32)
        ident = sb("ident", [P, P], F32)
        make_identity(nc, ident[:])

        def clear(rows):
            width = rows.shape[1]
            nc.vector.memset(rows[:, 0 : width - 1], 0)
            nc.vector.memset(rows[:, width - 1 : width], 0)

        clear(tab2_rows[:])
        nc.vector.memset(warm[:, 0:1], 0)
        clear(xt_planes[:].rearrange("p a c -> p (a c)"))
        clear(g_slots[:].rearrange("p i c -> p (i c)"))
        clear(tab_plane_moved[:])
        nc.scalar.activation(warm[:, 1:2], warm[:, 0:1], ACT.Sigmoid)

        def load_words(src, kp, name, at=None):
            words = sb(name, [P, T], I32, at)
            nc.sync.dma_start(words[:], src[kp].rearrange("p t i -> p (t i)").bitcast(I32))
            return words

        def load_x(kp):
            raw = sb("x%d" % kp, [P, 4, M], F32)
            nc.sync.dma_start(raw[:], x[512 * kp : 512 * (kp + 1), :].rearrange("(p i) m -> p i m", i=4))
            return raw

        piece = T // PIECES

        def load_pair_piece(c, at):
            raw = sb("pair%d" % c, [P, 2, piece], F32, at)
            nc.sync.dma_start(raw[:], wdT[0 : 2 * P, piece * c : piece * (c + 1)].rearrange("(p e) t -> p e t", e=2))
            return raw

        def load_wd(nt):
            rows = sb("wd%d" % nt, [P, T], F32)
            nc.sync.dma_start(rows[:], wdT[P * nt : P * (nt + 1), :])
            return rows

        for q in range(4):
            nc.gpsimd.dma_start(tab2_rows[32 * q + 8 : 32 * q + 16, :], tab2_scales.bitcast(I32)[:, 4 * q : 4 * q + 4, :])
        xt_rows = xt_scales.bitcast(I32)
        for q in range(4):
            nc.gpsimd.dma_start(
                xt_planes[32 * q : 32 * q + 4, :, :], xt_rows[:, 4 * q : 4 * q + 4, :].rearrange("a r c -> r a c")
            )
        first_words = sb("w1_0", [P, T], I32)
        first_src = tab_words[0].rearrange("p t i -> p (t i)").bitcast(I32)
        nc.sync.dma_start(first_words[:, 0:HEAD_COLUMNS], first_src[:, 0:HEAD_COLUMNS])
        tab_src = tab_scales.bitcast(I32).rearrange("a (q r) c -> r q a c", r=4)
        for r in range(4):
            nc.sync.dma_start(tab_rows[r:P:16, :], tab_src[r])
        g_rows = sb("g_rows", [JP, 512], F32)
        nc.sync.dma_start(g_rows[:], g.rearrange("(a c) -> a c", a=JP))
        nc.sync.dma_start(first_words[:, HEAD_COLUMNS:T], first_src[:, HEAD_COLUMNS:T])
        tab = [first_words, load_words(tab_words, 1, "w1_1", AT_TAB_LAST)]
        xt = sb("xtw", [P, KP, M // 2], I32)
        nc.sync.dma_start(xt[:], xt_words.bitcast(I32).rearrange("a p c -> p a c"))
        x_raw = [load_x(kp) for kp in range(KP)]

        def gather_scales(rows, name, at=None):
            plane = sb(name, [P, S], U8, at)
            nc.vector.tensor_copy(
                plane[:].rearrange("p (i b s) -> p b i s", i=4, s=8), rows[:].bitcast(U8).indirect(offsets[:])
            )
            return plane

        def gather_words(words, name, parts):
            picked = sb(name, [P, S], U32)
            blocks = picked[:].rearrange("p (i b s) -> p b i s", i=4, s=8)
            for part in range(parts):
                first, last = 32 * part // parts, 32 * (part + 1) // parts
                nc.vector.tensor_copy(
                    blocks[:, first:last], words[:].bitcast(U32).indirect(offsets[:, 2 * first : 2 * last])
                )
            return picked

        def gather_pair(words, a):
            picked = sb("wg01_%d" % a, [P, 4, P], U32)
            nc.vector.tensor_copy(
                picked[:].rearrange("p i (q s) -> p q i s", s=8), words.indirect(offsets[:, 32 * a : 32 * (a + 1)])
            )
            return picked

        def gather_rounded(name, rows, a, at=None):
            picked = sb(name, [P, 2, 2 * P], BF16, at)
            nc.vector.tensor_copy(
                picked[:].rearrange("p u (q s e) -> p q u e s", s=8, e=2), rows.indirect(offsets[:, 32 * a : 32 * (a + 1)])
            )
            return picked

        def weave(woven, slots):
            nc.scalar.copy(woven.rearrange("p (c r) i -> p c i r", r=4), slots.rearrange("p i (c r) -> p c i r", r=4))

        def quantize(name, woven, width):
            codes = sb(name + "c", [P, width], U32)
            scales = sb(name + "s", [P, width], U8)
            nc.vector.quantize_mx(out=codes[:].bitcast(FP8X4), scales=scales[:], in_=woven.rearrange("p n i -> p (n i)"))
            return codes, scales

        def cols(a, i):
            return slice(256 * i + P * a, 256 * i + P * (a + 1))

        def k_order(a):
            return [1, 0] if a else [0, 1]

        tab_plane = gather_scales(tab_rows, "plane1")
        nc.sync.dma_start(tab_plane_moved[0 : P - 16, :], tab_plane[16:P, :].bitcast(I32))
        tab_planes = [tab_plane[:], tab_plane_moved[:].bitcast(U8)]
        tab2 = [load_words(tab2_words, kp, "w2_%d" % kp) for kp in range(KP)]
        pair_raw = [load_pair_piece(c, {0: AT_FIRST_PIECE, 2: AT_THIRD_PIECE}.get(c)) for c in range(PIECES)]
        wd2 = load_wd(2)

        v = [gather_words(tab[0], "v1_0", 1), gather_words(tab[1], "v1_1", JP)]
        tab2_plane = gather_scales(tab2_rows, "plane2", AT_TAB_LAST)
        x_woven = [sb("xb%d" % kp, [P, M, 4], BF16) for kp in range(KP)]
        weave(x_woven[0][:], x_raw[0][:])
        x_cut = M - VECTOR_X_COLUMNS
        weave(x_woven[1][:, 0:x_cut, :], x_raw[1][:, :, 0:x_cut])
        nc.vector.tensor_copy(x_woven[1][:, x_cut:M, :], x_raw[1][:, :, x_cut:M].rearrange("p i m -> p m i"))
        xq = [quantize("x0", x_woven[0][:], M)]

        gate = {}
        for a in range(JP):
            for i in range(4):
                acc = next_bank([P, M])
                for kp in k_order(a):
                    nc.tensor.matmul_mx(
                        out=acc[:],
                        lhsT=v[kp][:, cols(a, i)].bitcast(FP8X4),
                        lhsT_scale=tab_planes[kp][:, cols(a, i)],
                        rhs=xt[:, kp, :].bitcast(U8).bitcast(FP4X4),
                        rhs_scale=xt_planes[:, kp, :].bitcast(U8),
                        start=(kp == k_order(a)[0]),
                        stop=(kp == k_order(a)[-1]),
                    )
                gate[a, i] = sb("sig%d%d" % (a, i), [P, M], F32)
                nc.scalar.activation(gate[a, i][:], acc[:], ACT.Sigmoid)

        nc.scalar.copy(
            g_slots[0:JP].rearrange("p i (q s) -> p i q s", s=8), g_rows[:].rearrange("p (q i s) -> p i q s", i=4, s=8)
        )
        g_bank = next_bank([P, 4, P])
        for i in range(4):
            nc.tensor.transpose(g_bank[:, i, :], g_slots[:, i, :], ident[:])
        gains = sb("gains", [P, 4, JP], F32)
        nc.scalar.copy(gains[:], g_bank[:, :, 0:JP])
        xq.append(quantize("x1", x_woven[1][:], M))
        v2 = [gather_words(tab2[kp], "v2_%d" % kp, JP) for kp in range(KP)]
        pair = sb("pairs", [P, T, 2], BF16)

        def turn_pair(picked, turned):
            bank = next_bank([P, 4, P])
            for i in range(4):
                nc.tensor.transpose(bank[:, i, :], picked[:, i, :].bitcast(F32), ident[:])
            nc.scalar.copy(turned, bank[:].bitcast(BF16).rearrange("p i n -> p n i"))

        def turn_rounded(picked, turned, copy):
            bank = next_bank([P, 2, P])
            for u in range(2):
                nc.tensor.transpose(bank[:, u, :], picked[:, u, :].bitcast(F32), ident[:])
            words = turned.rearrange("p n i -> p (n i)").bitcast(F32)
            copy(words.rearrange("p (n u) -> p n u", u=2), bank[:].rearrange("p u n -> p n u"))

        def make_h(a):
            slots = sb("hp%d" % a, [P, 4, M], BF16)
            for i in range(4):
                acc = next_bank([P, M])
                for kp in k_order(a):
                    nc.tensor.matmul_mx(
                        out=acc[:],
                        lhsT=v2[kp][:, cols(a, i)].bitcast(FP8X4),
                        lhsT_scale=tab2_plane[8 + 4 * kp : P, cols(a, i)],
                        rhs=xq[kp][0][:].bitcast(FP8X4),
                        rhs_scale=xq[kp][1][:],
                        start=(kp == k_order(a)[0]),
                        stop=(kp == k_order(a)[-1]),
                    )
                gain = gains[:, i, a : a + 1]
                if i == GPSIMD_SLOT[a]:
                    scaled = sb("scaled%d" % a, [P, M], F32, AT_H1 if a else AT_FIRST_PIECE)
                    nc.scalar.activation(scaled[:], acc[:], ACT.Copy, scale=gain)
                    nc.gpsimd.tensor_tensor(slots[:, i, :], scaled[:], gate[a, i][:], ALU.mult)
                else:
                    nc.vector.scalar_tensor_tensor(slots[:, i, :], acc[:], gain, gate[a, i][:], ALU.mult, ALU.mult)
            return slots

        def pool_rows(wq, span):
            bank = next_bank([P, span.stop - span.start])
            for a in range(JP):
                nc.tensor.matmul_mx(
                    out=bank[:],
                    lhsT=wq[a][0].bitcast(FP8X4),
                    lhsT_scale=wq[a][1],
                    rhs=hq[a][0][:, span].bitcast(FP8X4),
                    rhs_scale=hq[a][1][:, span],
                    start=(a == 0),
                    stop=(a == JP - 1),
                )
            return bank

        def magnitude(nt, bank, span):
            mag = sb("mag%d_%d" % (nt, span.start), [P, span.stop - span.start], F32)
            nc.scalar.activation(mag[:], bank[:], ACT.Abs)
            return nt, mag, span

        def store_root(nt, mag, span):
            res = sb("res%d_%d" % (nt, span.start), [P, span.stop - span.start], F32)
            nc.scalar.activation(res[:], mag[:], ACT.Sqrt)
            nc.sync.dma_start(out[P * nt : P * (nt + 1), span], res[:])

        for c in range(PIECES):
            nc.scalar.copy(pair[:, piece * c : piece * (c + 1), :], pair_raw[c][:].rearrange("p e t -> p t e"))
        h_slots = [make_h(a) for a in range(JP)]
        pair_words = pair[:].rearrange("p t e -> p (t e)").bitcast(U32)
        pair_picked = [gather_pair(pair_words, a) for a in range(JP)]
        h_woven = [sb("hw0", [P, M, 4], BF16, AT_H0), sb("hw1", [P, M, 4], BF16, AT_H1)]
        weave(h_woven[0][:], h_slots[0][:])
        pair_turned = [sb("wt01_%d" % a, [P, 2 * P, 4], BF16, AT_LAST_TURN if a else None) for a in range(JP)]
        turn_pair(pair_picked[0], pair_turned[0][:])
        h_cut = M - GPSIMD_H_COLUMNS
        weave(h_woven[1][:, 0:h_cut, :], h_slots[1][:, :, 0:h_cut])
        nc.gpsimd.tensor_scalar(
            h_woven[1][:, h_cut:M, :], h_slots[1][:, :, h_cut:M].rearrange("p i m -> p m i"), 1.0, 0.0, ALU.mult, ALU.add
        )
        wd3 = load_wd(3)
        picked2 = [gather_rounded("wg2_%d" % a, wd2[:], a) for a in range(JP)]
        turn_pair(pair_picked[1], pair_turned[1][:])
        hq, pair_q = [], []
        for a in range(JP):
            hq.append(quantize("h%d" % a, h_woven[a][:], M))
            pair_q.append(quantize("w01_%d" % a, pair_turned[a][:], 2 * P))
        whole = slice(0, M)
        halves = [slice(0, M // 2), slice(M // 2, M)]
        sums = [
            pool_rows([(c[:, P * nt : P * (nt + 1)], s[:, P * nt : P * (nt + 1)]) for c, s in pair_q], whole)
            for nt in range(2)
        ]
        turned2 = sb("wt2", [P, JP, P, 4], BF16)
        for a in range(JP):
            turn_rounded(picked2[a], turned2[:, a], nc.scalar.copy)
        root_warm = sb("root_warm", [P, 1], F32)
        nc.scalar.activation(root_warm[:], turned2[:, 0, 0, 0:1], ACT.Sqrt, bias=gate[1, 3][:, 0:1], scale=0.0)
        picked3 = [gather_rounded("wg3_0", wd3[:], 0, AT_LAST_TURN)]
        codes2, scales2 = quantize("w2", turned2[:].rearrange("p a n i -> p (a n) i"), P * JP)
        picked3.append(gather_rounded("wg3_1", wd3[:], 1, AT_LAST_TURN + KIB))
        wq3 = []
        for a in range(JP):
            turned3 = sb("wt3_%d" % a, [P, P, 4], BF16)
            turn_rounded(picked3[a], turned3[:], nc.vector.tensor_copy)
            codes3, scales3 = quantize("w3_%d" % a, turned3[:], P)
            wq3.append((codes3[:], scales3[:]))
            if a == 0:
                sums.append(pool_rows([(codes2[:, c : c + P], scales2[:, c : c + P]) for c in (0, P)], whole))
        last = [pool_rows(wq3, span) for span in halves]
        mags = [magnitude(nt, sums[nt], whole) for nt in range(2)]
        store_root(*mags[0])
        mags.append(magnitude(2, sums[2], whole))
        store_root(*mags[1])
        store_root(*mags[2])
        for mag in [magnitude(3, bank, span) for bank, span in zip(last, halves)]:
            store_root(*mag)
